import numpy as np, ml_dtypes
CORES = [40,41,42,43,44,45,46,47]
N = 8
BF = ml_dtypes.bfloat16
V, HP, Y, L, A, R, LM, C, RO, H = 4096, 16384, 1024, 64, 2, 4, 24, 768, 3, 9
Q, TOP = L * A * R, 2 ** 20
def chain(rng, brk, gone, uneven):
    s = (N, 8, 16, V); i = np.arange(V)
    last = np.maximum.accumulate(np.where(rng.random(s) < brk, i, 0), axis=-1)
    off = np.exp2(19.8 * rng.random(s)).astype(np.int64) if uneven else rng.integers(1, TOP - V, s)
    away = rng.random(s) < gone
    p = np.where(away, 0, np.take_along_axis(off, last, -1) + i)
    one = rng.random(s) < 0.3; one[..., 0] = False; one[..., 1:] &= away[..., :-1] & ~away[..., 1:]
    return np.where(one, 1, p)
def place(p, order):
    inv = np.argsort(order, axis=-1)
    return np.stack([p[:, g][:, :, inv[g]] for g in range(8)], axis=1)
def names_of(rng, order, jump, power):
    i = np.arange(HP); last = np.maximum.accumulate(np.where(rng.random((N, 8, HP)) < jump, i, 0), axis=-1)
    first = (V * rng.random((N, 8, HP)) ** power).astype(np.int64)
    c = (np.take_along_axis(first, last, -1) + i - last) % V
    return np.take_along_axis(np.broadcast_to(order, (N, 8, V)), c, -1)
def parts(rng, uneven=False):
    order = np.argsort(rng.random((8, V)), axis=-1)
    brk = rng.choice(np.array([0.02, 0.1, 0.3]), (N, 8, 16, 1)); gone = rng.choice(np.array([0.05, 0.2, 0.35]), (N, 8, 16, 1))
    top = rng.integers(LM // 2, LM + 1, (N, 8, 1)); top[0] = LM
    d = {"wpos": place(chain(rng, brk, gone, uneven), order), "heap": names_of(rng, order, 0.25, 3 if uneven else 1),
         "gst": rng.integers(0, HP - LM + 1, (N, 8, Y)), "gln": ((top + 1) * rng.random((N, 8, Y))).astype(np.int64),
         "sens": rng.integers(0, Y, (N, 8, A * Y)), "rel": rng.integers(0, N * Y, (N, 8, R * Y)), "nxt": rng.integers(0, Y, (N, 8, Y)), "cur": rng.integers(0, Y, (N, 8, L))}
    return d, order
def pack(d):
    r = {"wpos": np.ascontiguousarray(d["wpos"].reshape(N, 128, V)).astype(np.int32)}
    for k in ("heap", "gst", "gln", "sens", "rel", "nxt", "cur"): r[k] = np.ascontiguousarray(d[k]).astype(np.int32)
    return r
def some(rng, ln, n, k):
    return rng.choice(np.flatnonzero(ln == n), k)
def plant(rng, d, g, w):
    m, n = w.shape
    p = rng.integers(1, TOP - n + 1, (N, 16, m, 1)) + np.arange(n)
    d["wpos"][:, g][:, :, w.reshape(-1)] = p.reshape(N, 16, m * n)
    s = rng.integers(0, HP - LM - m * n + 1, (N, 1)) + n * np.arange(m)
    d["heap"][np.arange(N)[:, None], g, s[:, :1] + np.arange(m * n)] = w.reshape(-1)
    return s
def ask_few(rng, d, g, w, heads):
    m, n = len(w), len(heads); s = plant(rng, d, g, w)
    t = rng.permutation(Y)[:2 * m + 1]; u = rng.permutation(Y)[:n + 1]
    for k, ln in ((t[:m], 3), (t[m:2 * m], 2)):
        d["gst"][:, g][:, k] = s; d["gln"][:, g][:, k] = ln
    d["gln"][:, g, t[2 * m]] = 0
    for a in range(N):
        o = ((a + 1) % N) * Y; se = d["sens"][a, g].reshape(Y, A); re_ = d["rel"][a, g].reshape(Y, R)
        se[heads] = u[n]; se[heads, rng.integers(0, A, n)] = u[:n]; re_[u[n]] = o + t[2 * m]
        for i in range(n): re_[u[i]] = o + t[(np.arange(R) + i) % m + m * (a & 1)]
        d["nxt"][a, g, u[:n]] = np.roll(heads, -1); d["cur"][a, g] = heads[(np.arange(L) + a) % n]
    return u[:n], t
def setup_inputs(rng):
    return pack(parts(rng)[0])
def setup_inputs_spread(rng):
    d, order = parts(rng, True)
    e = rng.choice(np.array([0.3, 1.0, 4.0]), (N, 8, 1))
    d["gln"] = ((LM + 1) * rng.random((N, 8, Y)) ** e).astype(np.int64)
    d["gst"] = ((HP - LM + 1) * rng.random((N, 8, Y)) ** 2).astype(np.int64)
    q = ((N * rng.random((N, 8, R * Y)) ** 2).astype(np.int64) + np.arange(N)[:, None, None]) % N
    d["rel"] = q * Y + (Y * rng.random((N, 8, R * Y)) ** 1.5).astype(np.int64)
    d["sens"] = (Y * rng.random((N, 8, A * Y)) ** 2).astype(np.int64); d["cur"] = (Y * rng.random((N, 8, L)) ** 2).astype(np.int64)
    d["nxt"] = (Y * rng.random((N, 8, Y)) ** 0.5).astype(np.int64)
    for k in ("sens", "cur", "nxt"): d[k] = np.minimum(d[k], Y - 1)
    d["gln"] = np.minimum(d["gln"], LM); d["gst"] = np.minimum(d["gst"], HP - LM)
    return pack(d)
def setup_inputs_ends(rng):
    d, order = parts(rng)
    for k, hi in (("heap", V - 1), ("gst", HP - LM), ("sens", Y - 1), ("rel", N * Y - 1), ("nxt", Y - 1), ("cur", Y - 1), ("wpos", TOP - 1)):
        m = rng.random(d[k].shape); d[k] = np.where(m < 0.38, 0, np.where(m < 0.76, hi, d[k]))
    d["gln"] = LM * rng.integers(0, 2, (N, 8, Y))
    for g in range(8):
        o = rng.permutation(np.arange(1, V - 1)); c0 = np.concatenate([np.array([0]), o[:LM - 1]]); c1 = np.concatenate([o[LM:2 * LM - 1], np.array([V - 1])])
        if g == 3: c0 = np.roll(c0, -1)
        d["heap"][:, g, :LM] = c0; d["heap"][:, g, HP - LM:] = c1
        w = d["wpos"][:, g]; w[:, :, c0] = 1 + np.arange(LM); w[:, :, c1] = TOP - LM + np.arange(LM)
        if g < 3: w[:, g::3, c1[LM // 2]] = 0
        if g == 4 or g == 5:
            n = H if g == 4 else H - 1
            w[:, n:, c0] = TOP - 1; w[:, n:, c1] = TOP - 1
        if g == 6: w[:, 3, 0] = 0
    d["gst"][:, :, 0] = 0; d["gst"][:, :, Y - 1] = HP - LM; d["gln"][:, :, Y - 1] = LM; d["gln"][:, ::2, 0] = LM; d["gln"][:, 1::2, 0] = 0
    n = C // (A * R * LM)
    d["cur"][:, 7] = 0; d["cur"][:, 7, L - n:] = Y - 1; d["sens"][:, 7, :A] = 0; d["sens"][:, 7, (Y - 1) * A:] = Y - 1
    d["rel"][:, 7, :R] = 0; d["rel"][:, 7, (Y - 1) * R:] = N * Y - 1; d["nxt"][:, 7, 0] = Y - 1; d["nxt"][:, 7, Y - 1] = rng.choice(np.array([0, Y - 1]), N)
    d["cur"][:, 6, 0] = Y - 1; d["sens"][:, 6, (Y - 1) * A:] = Y - 1; d["sens"][:, 6, (Y - 1) * A] = Y - 2
    d["rel"][:, 6, (Y - 2) * R:] = N * Y - 1; d["rel"][:, 6, (Y - 2) * R] = 0; d["nxt"][:, 6, Y - 1] = 0; d["nxt"][:, 6, Y - 2] = Y - 1
    return pack(d)
def setup_inputs_corners(rng):
    d, order = parts(rng)
    d["gln"] = np.array([0, 1, LM - 1, LM, LM, LM, LM, 2])[np.argsort(rng.random((N, 8, Y)), axis=-1) & 7]
    d["gst"][:, 3] = rng.choice(np.array([0, 1, HP - LM - 1, HP - LM]), (N, Y))
    m = C // LM
    for a in range(N):
        for g in range(8):
            got = []
            for o in range(N):
                ln = d["gln"][o, g]; case = (o + 3 * a + g) % 6
                want = ([(LM, m)], [(LM, m - 1), (LM - 1, 1)], [(LM, m), (1, 1)], [(LM, m + m // 2)], [(0, 2)], [(1, m)])[case]
                for n, k in want: got.append(o * Y + some(rng, ln, n, k))
            have = np.concatenate(got)[:Q]
            have = rng.permutation(np.concatenate([have, a * Y + some(rng, d["gln"][a, g], 0, Q - len(have))]))
            w = rng.permutation(Y)[:L]; s = rng.permutation(Y)[:L * A]
            d["cur"][a, g] = w; d["sens"][a, g].reshape(Y, A)[w] = s.reshape(L, A); d["rel"][a, g].reshape(Y, R)[s] = have.reshape(L * A, R)
            if g % 4 == 1: d["nxt"][a, g, s] = np.repeat(w, A)
            if g % 4 == 2: d["nxt"][a, g] = rng.choice(np.array([0, Y - 1]), Y)
    return pack(d)
def setup_inputs_crowd(rng):
    d, order = parts(rng)
    n = np.array([16, 15, H, H - 1, 16, H + 1, H, H - 1])[(np.arange(8)[None, :] + np.arange(N)[:, None]) & 7]
    turn = (np.arange(16)[None, None, :] + rng.integers(0, 16, (N, 8, 1))) & 15
    off = rng.integers(1, TOP - V, (N, 8, 16, 1)); i = np.arange(V)
    d["wpos"] = place(np.where((turn < n[:, :, None])[..., None], off + i, (off + 257 * i) & (TOP - 1)), order)
    d["cur"][:, ::2] = rng.integers(0, Y, (N, 4, 1)); d["cur"][:, 1::4, :L - 1] = rng.integers(0, Y, (N, 2, 1))
    few = rng.integers(0, Y, (N, 2, 3)); d["cur"][:, 3::4] = np.take_along_axis(few, rng.integers(0, 3, (N, 2, L)), -1)
    d["gln"][:, 4:] = np.minimum(d["gln"][:, 4:], 4)
    d["rel"][:, 2] = np.arange(N)[:, None] * Y + rng.integers(0, Y, (N, R * Y)); d["rel"][:, 6] = (N - 1) * Y + rng.integers(0, Y, (N, R * Y))
    return pack(d)
def setup_inputs_calm(rng):
    d, order = parts(rng); gs = [int(x) for x in rng.permutation(8)[:4]]; c = rng.permutation(np.arange(4, V - 4))
    g = gs[0]; h = rng.permutation(Y)[:2]
    u, t = ask_few(rng, d, g, c[None, :3], h)
    d["nxt"][:, g][:, u] = h; d["rel"][:, g, u[1] * R + R - 1] = ((np.arange(N) + 1) % N) * Y + t[2]
    d["cur"][:, g] = h[0]; d["cur"][1::2, g, L - 1] = h[1]
    ask_few(rng, d, gs[1], np.stack([c[3:7], np.arange(4), c[7:11]], axis=1), rng.permutation(4))
    ask_few(rng, d, gs[2], np.stack([c[11:15], V - 1 - np.arange(4), c[15:19]], axis=1), Y - 1 - rng.permutation(4))
    g = gs[3]; m = L * R; t = rng.permutation(Y)
    s = plant(rng, d, g, rng.permutation(V)[:2 * m].reshape(m, 2))
    d["gst"][:, g][:, t[:m]] = s; d["gln"][:, g] = 1; d["gln"][:, g][:, t[:m]] = 2
    for a in range(N):
        o = ((a + N - 1) % N) * Y; w = rng.permutation(Y)[:L]; u = rng.permutation(Y)[:L * A].reshape(L, A); v = rng.integers(0, A, L); v[L - 1] = A - 1
        d["sens"][a, g].reshape(Y, A)[w] = u; d["cur"][a, g] = w; d["nxt"][a, g, u] = w[:, None]
        rows = d["rel"][a, g].reshape(Y, R); rows[u] = o + t[rng.integers(m, Y, (L, A, R))]
        rows[u[np.arange(L), v]] = o + rng.permutation(t[:m]).reshape(L, R)
    return pack(d)
def check_inputs(d):
    bad = []
    for k, hi in (("wpos", 2 ** 20 - 1), ("heap", V - 1), ("gst", HP - LM), ("gln", LM), ("sens", Y - 1), ("rel", N * Y - 1), ("nxt", Y - 1), ("cur", Y - 1)):
        if np.min(d[k]) < 0 or np.max(d[k]) > hi: bad.append("range of " + k)
    return bad
def reference(wpos, heap, gst, gln, sens, rel, nxt, cur):
    P = np.array(wpos, dtype=np.int32).reshape(N, 8, 16, V); w = cur.astype(np.int64)
    yt = np.zeros((N, 8, RO, L, A), np.int64); yb = np.zeros((N, 8, RO, L, R), np.int64); yw = np.zeros((N, 8, RO, L), np.int64)
    gi = np.arange(8)[:, None]; e = np.arange(LM)[:, None]
    for rnd in range(RO):
        for a in range(N):
            s = np.take_along_axis(sens[a], (w[a][:, :, None] * A + np.arange(A)).reshape(8, L * A), 1).astype(np.int64)
            rq = np.take_along_axis(rel[a], (s[:, :, None] * R + np.arange(R)).reshape(8, Q), 1).astype(np.int64)
            q = rq // Y; t = rq - q * Y; ln = gln[q, gi, t].astype(np.int64); st = gst[q, gi, t].astype(np.int64)
            kept = np.zeros((8, Q), np.int64)
            for o in range(N):
                m = np.where(q == o, ln, 0); before = np.add.accumulate(m, axis=1) - m
                kept = kept + np.minimum(np.maximum(C - before, 0), m)
            word = heap[q[:, None, :], gi[:, :, None], st[:, None, :] + e]
            x = np.take_along_axis(P[a], word.reshape(8, 1, LM * Q), 2).reshape(8, 16, LM, Q)
            x = np.where((e < kept[:, None, :])[:, None], x, 0)
            more = np.zeros(x.shape, bool); more[:, :, 1:] = (x[:, :, 1:] == x[:, :, :-1] + 1) & (x[:, :, :-1] > 0)
            run = np.zeros((8, 16, Q), np.int64); score = np.zeros((8, 16, Q), np.int64)
            for i in range(LM):
                run = np.where(x[:, :, i] > 0, np.where(more[:, :, i], run, 0) + 1, 0)
                score = score + np.where(run > 0, 2 * run - 1, 0)
            tot = np.add.reduce(np.add.reduce(score, axis=1).reshape(8, L, A, R), axis=3)
            win = np.argmax(tot, axis=2)
            hot = np.add.reduce(more, axis=1, dtype=np.int64) >= H
            at = np.maximum.reduce(np.where(hot, e, -1), axis=1)
            b = np.where(at >= 0, np.take_along_axis(word, np.maximum(at, 0)[:, None, :], 1)[:, 0], -1).reshape(8, L, A, R)
            b = np.take_along_axis(b, win[:, :, None, None], 2)[:, :, 0]
            if rnd < RO - 1:
                for g in range(8):
                    c = b[g].reshape(-1); P[a, g][:, c[c >= 0]] = 0
            sw = np.take_along_axis(s.reshape(8, L, A), win[:, :, None], 2)[:, :, 0]
            w[a] = np.take_along_axis(nxt[a], sw, 1)
            yt[a, :, rnd] = tot; yb[a, :, rnd] = b; yw[a, :, rnd] = w[a]
    return {"yt": yt.reshape(N, 8, RO * L * A).astype(np.float32), "yb": yb.reshape(N, 8, RO * L * R).astype(np.float32), "yw": yw.reshape(N, 8, RO * L).astype(np.float32)}

@@ -1,0 +1,802 @@
+from concourse.bass import DstId, RemoteDMATransfer
+from concourse.mybir import AluOpType as OP, AxisListType, ActivationFunctionType as AF
+
+F, B, H, I, U = "float32", "bfloat16", "float16", "int32", "uint16"
+BIG = float(2 ** 60)
+RO = 3
+
+
+def _scratch():
+    s = {}
+
+    def sb(dt, **kw):
+        for k, w in kw.items():
+            s[k] = ("sbuf", [128, w], dt)
+    sb(I, io_p=4, gst_r=68, gln_r=68, cur_r=4, rel_r=256, sens_r=128, nxt_r=64, heap_r=1024, pos_r=4096,
+       tli=704, lnf=704, tab=1024, n1=64, n2=64, n4=64, m1=32, m2=32, m3=32, ti=256)
+    sb(F, pc=40, ek=16, xf=256, sr0=144, bon=128, bop=128, bdp=128, bdm=128, b15=128,
+       relw=4096, sensw=2048, nxtw=1024, pt=4352, f1=128, f2=128, f3=128, f4=128, mend=384, m16=408,
+       ridx=32, base2=16, rfrac=256, negb=256, skw=64, sk=128, rqw=1024, cb=192, cd=32, pq=64, sel=96, winl=32,
+       wa=32, wb=32, va=32, vb=32, ua=32, ub=32,
+       a1=512, mq=512, g2=512, d0=512, ss=516, zc=32, zv=32, zd=32, ze=32, cc=388, p1s=384,
+       x0=776, x1=776, cs=416, ds=416, ge=512, uu=512, mc0=512, mc1=512, kv0=32, kv1=32, ep0=32, ep1=32,
+       rw=384, bw=512, bd=512, keyw=256, keyl=32, mn=32, ytb=384, ybb=768, ywb=192, nh=408)
+    sb(U, idu=256, l3=64)
+    sb(I, g2c=1024)
+    sb(F, idf=128)
+    sb(B, idn=128)
+    sb(B, iotab=384, idb=128, r143=144, rg=128, b1=128, b2=128, s2=144, s1=144, sd=144, sh=144, szb=144, sw4=144, tri=2048, hhi=1024, hlo=1024,
+       hw=16384, w0=6656, w1=6656, winw=192,
+       hh=512, val=512, g2b=512, ow=6144, dd0=768, dd1=768, ct0=768, ct1=768, rr0=768, rr1=768, ones=768, dg=512)
+    sb(H, sq0=144, sq4=144, skh=64, wc=128, sz=144, srh=144, bq=128, rs=2048, ht=256, hq=256, hs=128, hn=64, xm=512, lowh=32, b16=256)
+    sb(U, tl=704, lu=64, l2=64, offu=32, lsu0=32, lsu1=32, leu0=32, leu1=32, colu=32, bu=16, wiu=16)
+    for r in range(RO):
+        sb(U, **{"as%d" % r: 384, "al%d" % r: 384, "rs%d" % r: 384, "rl%d" % r: 384})
+    share = {"g2c": ("pos_r", 0), "tli": ("pos_r", 1024), "lnf": ("pos_r", 1728), "ti": ("pos_r", 2944),
+             "rel_r": ("pos_r", 3200), "sens_r": ("pos_r", 3456), "nxt_r": ("pos_r", 3584),
+             "dd0": ("ow", 0), "ct0": ("ow", 768), "rr0": ("ow", 1536), "dd1": ("ow", 2304), "ct1": ("ow", 3072), "rr1": ("ow", 3840),
+             "hhi": ("ow", 0), "hlo": ("ow", 1024), "a1": ("x0", 16), "mq": ("x1", 16)}
+    place, top, out = {}, {}, {}
+    for k, (_w, sh, dt) in s.items():
+        if k in share:
+            continue
+        if sh[1] >= 1024:
+            out[k] = s[k]
+            place[k] = (k, 0, sh[1])
+        else:
+            pool = "pool_" + dt
+            place[k] = (pool, top.get(pool, 0), sh[1])
+            top[pool] = top.get(pool, 0) + (sh[1] + 15) // 16 * 16
+            out[pool] = ("sbuf", [128, top[pool]], dt)
+    for k, (base, off) in share.items():
+        place[k] = (place[base][0], place[base][1] + off, s[k][1][1])
+    for k, w in (("py0", 1024), ("py1", 1024), ("pa", 512), ("pb", 512), ("pcc", 512), ("pd", 512)):
+        out[k] = ("psum", [128, w], F)
+        place[k] = (k, 0, w)
+    return out, place
+
+
+SCRATCH, PLACE = _scratch()
+SEMAPHORES = (["V", "S", "P", "G", "loc", "tarr", "dout"] + ["d%d" % k for k in range(10)]
+              + ["aa%d" % k for k in range(8)] + ["ra%d" % k for k in range(8)])
+
+
+def rank_program(g, core, T, topo):
+    rank = T.rank_of(core)
+    if rank is None:
+        return
+    N = len(T.cores)
+    Q = {"V": g.vector, "S": g.scalar, "P": g.tensor, "G": g, "Y": g.sync}
+    cnt = {"V": 0, "S": 0, "P": 0, "G": 0}
+    known = {e: {} for e in Q}
+    rec = {}
+    tot = {}
+
+    def a(name, lo=0, hi=None, st=1, rows=None):
+        name, off, w = PLACE[name]
+        lo, hi = off + lo, off + (w if hi is None else hi)
+        cs_ = slice(lo, hi, st) if st != 1 else slice(lo, hi)
+        ap = T[name][(slice(None) if rows is None else rows), cs_]
+        if SCRATCH[name][0] == "psum":
+            return (ap, name, lo // 512 * 512, (hi + 511) // 512 * 512, True)
+        return (ap, name, lo, hi, False)
+
+    def ind(win, off):
+        return (win[0].indirect(off[0]), win[1], win[2], win[3], False, off)
+
+    def need(e, tok):
+        if known[e].get(tok[0], 0) < tok[1]:
+            Q[e].wait_ge(T.sem[tok[0]], tok[1])
+            known[e][tok[0]] = tok[1]
+
+    def before(e, reads, writes):
+        toks = {}
+        for lst, wr in ((reads, False), (writes, True)):
+            for x in lst:
+                for (lo, hi, tok, w) in rec.get(x[1], []):
+                    if lo < x[3] and x[2] < hi and (w or wr or (x[4] and tok[0] != e)):
+                        if tok[0] == e and e == "P":
+                            continue
+                        toks[tok[0]] = max(toks.get(tok[0], 0), tok[1])
+        for k in sorted(toks):
+            need(e, (k, toks[k]))
+
+    def after(tok, reads, writes):
+        for x in reads:
+            l = [r for r in rec.get(x[1], []) if not (r[2][0] == tok[0] and not r[3] and x[2] <= r[0] and r[1] <= x[3])]
+            rec[x[1]] = l + [(x[2], x[3], tok, False)]
+        for x in writes:
+            l = [r for r in rec.get(x[1], []) if not (x[2] <= r[0] and r[1] <= x[3])]
+            rec[x[1]] = l + [(x[2], x[3], tok, True)]
+
+    def op(e, out, ins, call, inc=True):
+        reads = [x for x in ins if isinstance(x, tuple)]
+        reads = reads + [x[5] for x in reads + [out] if len(x) > 5]
+        before(e, reads, [out])
+        ins_ = call()
+        if inc:
+            ins_.then_inc(T.sem[e], 1)
+            cnt[e] += 1
+            after((e, cnt[e]), reads, [out])
+        else:
+            after((e, cnt[e] + 1), reads, [out])
+
+    def v_(x):
+        return x[0] if isinstance(x, tuple) else x
+
+    def ts(out, x, s1, o1, s2=None, o2=None):
+        if o2 is None:
+            op("V", out, [x, s1], lambda: g.vector.tensor_scalar(out[0], x[0], v_(s1), None, o1))
+        else:
+            op("V", out, [x, s1, s2], lambda: g.vector.tensor_scalar(out[0], x[0], v_(s1), v_(s2), o1, o2))
+
+    def tt(out, x, y, o):
+        op("V", out, [x, y], lambda: g.vector.tensor_tensor(out[0], x[0], y[0], o))
+
+    def cp(out, x):
+        op("V", out, [x], lambda: g.vector.tensor_copy(out[0], x[0]))
+
+    def ms(out, c):
+        op("V", out, [], lambda: g.vector.memset(out[0], c))
+
+    def scan(out, x, y, init, o0, o1):
+        op("V", out, [x, y, init], lambda: g.vector.tensor_tensor_scan(out[0], x[0], y[0], v_(init), o0, o1))
+
+    def act(out, x, f=AF.Identity, bias=None, scale=None):
+        kw = {}
+        if bias is not None:
+            kw["bias"] = v_(bias)
+        if scale is not None:
+            kw["scale"] = v_(scale)
+        op("S", out, [x, bias, scale], lambda: g.scalar.activation(out[0], x[0], f, **kw))
+
+    def iota(out, pat, base, cm, flt=True):
+        if flt:
+            op("G", out, [], lambda: g.iota(out[0], pat, base, cm, allow_small_or_imprecise_dtypes=True))
+        else:
+            op("G", out, [], lambda: g.iota(out[0], pat, base, cm))
+
+    def mm(out, l, r, start, stop, inc=None):
+        op("P", out, [l, r], lambda: g.tensor.matmul(out[0], l[0], r[0], start, stop), inc=stop if inc is None else inc)
+
+    def dmas(sem, lst):
+        for (e, o, i_) in lst:
+            before(e, [i_] if isinstance(i_, tuple) else [], [o] if isinstance(o, tuple) else [])
+            Q[e].dma_start(v_(o), v_(i_)).then_inc(T.sem[sem], 16)
+        tot[sem] = tot.get(sem, 0) + 16 * len(lst)
+        for (e, o, i_) in lst:
+            after((sem, tot[sem]), [i_] if isinstance(i_, tuple) else [], [o] if isinstance(o, tuple) else [])
+
+    def send(lst, per):
+        trs = []
+        for n, (d, src, dst, sem) in enumerate(lst):
+            before("G", [src], [])
+            dc = T.cores[d]
+            en = topo.engines(core, dc)
+            m = 0
+            for k in range(per):
+                m |= 1 << en[n * per + k]
+            rid, pid, _se = topo.addr(dc)
+            trs.append(RemoteDMATransfer(dst_ids=[DstId(rid=rid, pnc=pid)], dma_engine_mask=m, remote_sem=T.sem[sem],
+                                         src=src[0], dst=dst[0]))
+        g.remote_dma_fused(trs, local_sem=T.sem.loc)
+        tot["loc"] = tot.get("loc", 0) + per * len(lst)
+
+    def landed(sem, n, place):
+        tot[sem] = tot.get(sem, 0) + n
+        after((sem, tot[sem]), [], [place])
+
+    def sel(fam, k):
+        return a(fam, 15 - k, 143 - k)
+
+    def w2l(out, fam, src, lo, hi):
+        for k in range(16):
+            mm(out, sel(fam, k), a(src, lo + k, hi, 16), k == 0, k == 15)
+
+    col = {}
+
+    def pcol(name):
+        if name not in col:
+            col[name] = len(col)
+        return a("pc", col[name], col[name] + 1)
+
+    def ek(k):
+        return a("ek", k, k + 1)
+
+    others = [(rank + d) % N for d in range(1, N)]
+    order = [rank] + others
+
+    dmas("d0", [("Y", a("gst_r", 0, 64), T.gst[:]), ("S", a("gln_r", 0, 64), T.gln[:])])
+    dmas("d1", [("Y", a("rel_r"), T.rel[:])])
+    dmas("d2", [("S", a("sens_r"), T.sens[:])])
+    dmas("d3", [("S", a("cur_r"), T.cur[:])])
+    dmas("d4", [("Y", a("nxt_r"), T.nxt[:])])
+    dmas("d5", [("Y", a("heap_r"), T.heap[:])])
+    iota(a("io_p", 0, 1), [[0, 1]], 0, 1, False)
+    iota(a("xf"), [[1, 256]], 0, 0)
+
+    ms(a("hw", 0, 2048), 0.0)
+    act(a("hw", 2048, 4096), a("hw", 0, 2048))
+    act(a("hw", 4096, 6144), a("hw", 0, 2048))
+    ms(a("gst_r", 64, 68), 0)
+    ms(a("gln_r", 64, 68), 0)
+    ts(a("io_p", 1, 2), a("io_p", 0, 1), 15, OP.bitwise_and)
+    ts(a("io_p", 2, 3), a("io_p", 0, 1), 7, OP.bitwise_and)
+    ts(a("io_p", 3, 4), a("io_p", 0, 1), 3, OP.bitwise_and)
+    c_, c8, c4 = a("io_p", 1, 2), a("io_p", 2, 3), a("io_p", 3, 4)
+    cp(pcol("c"), c_)
+    tt(pcol("g16"), a("io_p", 0, 1), c_, OP.subtract)
+    cp(pcol("k"), c4)
+    ts(a("ek"), a("xf", 0, 16), pcol("c"), OP.is_equal)
+    ts(a("b1"), a("xf", 0, 128), pcol("g16"), OP.subtract)
+    ts(a("r143"), a("xf", 0, 144), pcol("g16"), OP.subtract, 15.0, OP.subtract)
+    ts(a("b2"), a("b1"), 15.0, OP.is_gt, 1000.0, OP.mult)
+    ts(pcol("lo8"), c_, 8, OP.is_lt)
+    tt(a("rg"), a("b1"), a("b2"), OP.subtract)
+
+    own = 88 * rank
+    tt(a("f1", 0, 66), a("gst_r", 0, 66), a("gln_r", 0, 66), OP.add)
+    ts(a("f2", 0, 66), a("gln_r", 0, 66), 0, OP.is_gt)
+    ts(a("f3", 0, 22), a("gln_r", 1, 66, 3), 32.0, OP.mult)
+    ts(a("f4", 0, 22), a("gln_r", 2, 66, 3), 1024.0, OP.mult)
+    tt(a("f1", 0, 66), a("f1", 0, 66), a("f2", 0, 66), OP.mult)
+    tt(a("f3", 0, 22), a("f3", 0, 22), a("gln_r", 0, 66, 3), OP.add)
+    ts(a("ti"), a("rel_r"), 1023, OP.bitwise_and)
+    tt(a("f3", 0, 22), a("f3", 0, 22), a("f4", 0, 22), OP.add)
+    for x in range(3):
+        cp(a("tl", own + x, own + 88, 4), a("f1", x, 66, 3))
+    cp(a("tl", own + 3, own + 88, 4), a("f3", 0, 22))
+    send([(d, a("tl", own, own + 88), a("tl", own, own + 88), "tarr") for d in others], 2)
+    tot["tarr"] = 2 * (N - 1)
+    for d in others:
+        after(("tarr", tot["tarr"]), [], [a("tl", 88 * d, 88 * d + 88)])
+    iota(a("w0"), [[0, 6656]], 0, 0)
+    iota(a("hw", 10240, 13312), [[0, 3072]], 0, 0)
+
+    cp(a("ht"), a("ti"))
+    tt(a("hq"), a("rel_r"), a("ti"), OP.subtract)
+    for k in range(16):
+        if k < 4:
+            ts(a("rs", 128 * k, 128 * k + 128), a("rg"), 0.0, OP.is_ge, ek(k), OP.mult)
+        py = "py%d" % (k // 4 % 2)
+        o = a(py, 256 * (k % 4), 256 * (k % 4) + 256)
+        mm(o, a("rs", 128 * k, 128 * k + 128), a("ht"), True, False)
+        mm(o, a("rs", 128 * k, 128 * k + 128), a("hq"), False, True)
+        if k % 4 == 3:
+            act(a("relw", 1024 * (k // 4), 1024 * (k // 4) + 1024), a(py))
+        if k == 3:
+            cp(a("hs"), a("sens_r"))
+            for j in range(4, 16):
+                ts(a("rs", 128 * j, 128 * j + 128), a("rg"), 0.0, OP.is_ge, ek(j), OP.mult)
+            for j in range(16):
+                mm(a(("pa", "pb", "pcc", "pd")[j // 4], 128 * (j % 4), 128 * (j % 4) + 128), a("rs", 128 * j, 128 * j + 128), a("hs"), True, True)
+    ts(pcol("hi8"), c_, 8, OP.is_ge)
+    ts(pcol("a0"), c8, 4, OP.is_lt, 4.0, OP.mult)
+    ts(pcol("a1"), c8, 4, OP.is_ge, 4.0, OP.mult)
+    ts(a("sr0"), a("r143"), 0.0, OP.is_equal, ek(0), OP.mult)
+    cp(a("hn"), a("nxt_r"))
+    cp(a("tli", 528, 704), a("tl", 3, 704, 4))
+    for x in range(3):
+        cp(a("tli", x, 528, 3), a("tl", x, 704, 4))
+    ts(a("lnf", 0, 528, 3), a("tli", 528, 704), 31, OP.bitwise_and)
+    ts(a("lnf", 1, 528, 3), a("tli", 528, 704), 5, OP.logical_shift_right, 31, OP.bitwise_and)
+    ts(a("lnf", 2, 528, 3), a("tli", 528, 704), 10, OP.logical_shift_right)
+    dmas("d7", [("Y", a("tab", rows=slice(8 + q, 128, 16)), a("tli", 66 * q, 66 * q + 64)) for q in range(N)]
+         + [("Y", a("tab", rows=slice(q, 128, 16)), a("lnf", 66 * q, 66 * q + 64)) for q in range(N)])
+    for j, p in enumerate(("pa", "pb", "pcc", "pd")):
+        cp(a("sensw", 512 * j, 512 * j + 512), a(p))
+
+    def senses(out_pieces, n, src):
+        m = n // 16
+        ts(a("l2", 0, m), src, 2.0, OP.mult)
+        ts(a("l2", 8, 8 + m), src, 2.0, OP.mult, 1.0, OP.add)
+        ts(a("f1", 0, n), ind(a("sensw"), a("l2", 0, m)), pcol("a0"), OP.mult, pcol("k"), OP.add)
+        ts(a("f2", 0, n), ind(a("sensw"), a("l2", 8, 8 + m)), pcol("a1"), OP.mult)
+        for (o, lo, hi) in out_pieces:
+            tt(o, a("f1", lo, hi), a("f2", lo, hi), OP.add)
+
+    def blend(out, ev, od, t="w"):
+        ts(a(t + "a"), ev, pcol("lo8"), OP.mult)
+        ts(a(t + "b"), od, pcol("hi8"), OP.mult)
+        tt(out, a(t + "a"), a(t + "b"), OP.add)
+
+    def lists_a(nc):
+        if nc == 1:
+            cp(a("l2", 0, 32), a("cb", 0, 32))
+        act(a("rqw", 0, 512 * nc), ind(a("relw"), a("l2", 0, 32 * nc)))
+        w2l(a("pd", 0, 32 * nc), "sr0", "rqw", 0, 512 * nc)
+
+    def lists_b(nc):
+        n = 32 * nc
+        cp(a("n1", 0, n), a("pd", 0, n))
+        ts(a("n4", 0, n), a("n1", 0, n), 1023, OP.bitwise_and)
+        ts(a("n2", 0, n), a("n1", 0, n), 10, OP.logical_shift_right)
+        cp(a("l3", 0, n), a("n4", 0, n))
+        ts(a("pq", 0, n), a("n2", 0, n), 768.0, OP.mult, 511.0, OP.add)
+        if nc == 2:
+            tt(a("cd", 0, 32), a("pq", 32, 64), a("pq", 0, 32), OP.subtract)
+
+    senses([(a("skw", i, 64, 4), 16 * i, 16 * i + 16) for i in range(4)], 64, a("cur_r"))
+    blend(a("cb", 0, 32), a("skw", 0, 64, 2), a("skw", 1, 64, 2))
+    lists_a(1)
+    dmas("d6", [("Y", a("pos_r"), T.wpos[:])])
+    ts(pcol("qb"), c8, -1024.0, OP.mult, -511.5, OP.add)
+    act(a("a1"), a("rqw", 0, 512), AF.Abs, bias=pcol("qb"))
+    act(a("hw", 6144, 8192), a("hw", 0, 2048))
+    cp(a("skh"), a("skw"))
+    cp(a("pt", 0, 1024), a("heap_r"))
+    ts(a("idf"), a("rg"), pcol("c"), OP.is_equal)
+    ts(a("idn"), a("rg"), pcol("c"), OP.is_equal, -1.0, OP.mult)
+    act(a("hhi"), a("pt", 0, 1024))
+    for j, p in enumerate(("pa", "pb")):
+        mm(a(p), a("idf"), a("pt", 512 * j, 512 * j + 512), True, False)
+        mm(a(p), a("idn"), a("hhi", 512 * j, 512 * j + 512), False, True)
+    b0 = 32768.5 / 2 ** 17
+    ts(pcol("u1"), c_, 2, OP.is_ge, 0.5, OP.mult)
+    ts(pcol("u2"), ek(1), b0, OP.mult)
+    tt(pcol("beta"), ek(0), ek(1), OP.subtract)
+    ts(pcol("h01"), c_, 2, OP.is_lt)
+    ts(pcol("nh8"), pcol("hi8"), -1.0, OP.mult)
+    ts(pcol("u3"), ek(2), -65536.0, OP.mult, ek(3), OP.subtract)
+    ts(pcol("wd"), pcol("hi8"), 2.0 ** -16, OP.mult, -(2.0 ** -17), OP.add)
+    tt(pcol("gam"), pcol("u1"), pcol("u2"), OP.add)
+    ts(pcol("bb0"), pcol("beta"), b0, OP.mult)
+    ts(pcol("nc"), c_, -1.0, OP.mult)
+    ts(pcol("wt"), pcol("h01"), float(2 ** 17), OP.mult, pcol("u3"), OP.add)
+    ts(a("bdp"), a("rg"), 0.0, OP.is_ge, pcol("wd"), OP.mult)
+    ts(a("sz"), a("r143"), 0.0, OP.is_equal, pcol("lo8"), OP.mult)
+    cp(a("ss", 0, 1), pcol("lo8"))
+    ts(a("bdm"), a("bdp"), -1.0, OP.mult)
+    ts(a("ridx"), a("xf", 0, 32), 16.0, OP.mult, pcol("c"), OP.add)
+    ts(a("idb"), a("rg"), pcol("c"), OP.is_equal)
+    ts(a("iotab"), a("hw", 0, 384), pcol("c"), OP.add, 1.0, OP.add)
+    ts(a("iotab", 0, 384, 48), a("hw", 0, 8), pcol("c"), OP.add)
+    ts(a("mq"), a("a1"), 512.0, OP.is_lt)
+    lists_b(1)
+    cp(a("sel", 64, 96), a("pq", 0, 32))
+
+    def startup_1():
+        for k in range(8):
+            ts(a("tri", 128 * k, 128 * k + 128), a("rg"), float(k), OP.is_ge, pcol("wt"), OP.mult)
+
+    def startup_2():
+        act(a("hlo", 0, 512), a("pa"))
+        act(a("hlo", 512, 1024), a("pb"))
+        for k in range(8, 16):
+            ts(a("tri", 128 * k, 128 * k + 128), a("rg"), float(k), OP.is_ge, pcol("wt"), OP.mult)
+
+    def startup_3():
+        ms(a("hw", 13312, 16384), 0.0)
+        dmas("d8", [("Y", a("hw", rows=slice(0, 128, 16)), a("hhi")), ("Y", a("hw", rows=slice(1, 128, 16)), a("hlo"))])
+        ts(a("b15"), a("rg"), 0.0, OP.is_ge, ek(15), OP.mult)
+        ms(a("mend"), 1.0)
+        ms(a("mend", 47, 384, 48), 0.0)
+        ms(a("cc", 0, 1), 0.0)
+        ts(a("szb"), a("r143"), 0.0, OP.is_equal, pcol("lo8"), OP.mult)
+        ts(a("b1"), a("rg"), pcol("c"), OP.is_equal, pcol("lo8"), OP.mult)
+        ts(a("b2"), a("rg"), -8.0, OP.add, pcol("c"), OP.is_equal)
+        ts(pcol("zm"), pcol("hi8"), -384.0, OP.mult, -192.5, OP.add)
+        tt(a("bq"), a("b1"), a("b2"), OP.add)
+
+    def startup_4():
+        iota(a("ones"), [[0, 768]], 1, 0)
+        iota(a("pt", 4096, 4352), [[0, 256]], 0, 0)
+        iota(a("m16"), [[0, 408]], -16, 0)
+        iota(a("cs"), [[0, 416]], 0, 0)
+        iota(a("ds"), [[0, 416]], 100, 0)
+        ts(a("sh"), a("r143"), 0.0, OP.is_equal, pcol("h01"), OP.mult)
+        ts(pcol("q0"), ek(0), 0.25, OP.mult)
+        ts(pcol("q4"), ek(4), 0.25, OP.mult)
+        ts(a("srh"), a("r143"), 0.0, OP.is_equal, ek(0), OP.mult)
+        ts(a("sq0"), a("r143"), 0.0, OP.is_equal, pcol("q0"), OP.mult)
+        ts(a("sq4"), a("r143"), 0.0, OP.is_equal, pcol("q4"), OP.mult)
+
+    def startup_5():
+        ts(pcol("w4"), ek(0), 4.0, OP.mult)
+        tt(pcol("u1"), c_, c4, OP.add)
+        ts(a("sw4"), a("r143"), 0.0, OP.is_equal, pcol("w4"), OP.mult)
+        ts(a("s2"), a("r143"), 0.0, OP.is_equal, 2.0, OP.mult)
+        ts(a("s1"), a("r143"), 0.0, OP.is_equal)
+        ts(a("sd"), a("r143"), 0.0, OP.is_equal, 1.0 / BIG, OP.mult)
+        ts(a("bon"), a("rg"), 0.0, OP.is_ge, -1.0, OP.mult)
+        ts(a("bop"), a("rg"), 0.0, OP.is_ge)
+        ts(pcol("u2"), c4, -2.0, OP.mult, pcol("u1"), OP.add)
+        ts(a("rfrac"), a("xf"), 1.0 / 512, OP.mult)
+        ts(pcol("u2"), pcol("u2"), pcol("c"), OP.add)
+        ts(a("base2"), a("xf", 0, 16), 32.0, OP.mult, pcol("u2"), OP.add)
+        ms(a("negb"), -BIG)
+        ts(pcol("lo512"), pcol("lo8"), 512.0, OP.mult)
+        ts(pcol("hi512"), pcol("hi8"), 512.0, OP.mult)
+        ms(a("x0", 7, 8), -BIG)
+        ms(a("x1", 7, 8), -BIG)
+
+
+    def positions(parts):
+        for k in parts:
+            py = a("py%d" % (k % 2))
+            for lo in (0, 512):
+                mm(a("py%d" % (k % 2), lo, lo + 512), a("idb"), a("ow", 2048 + 1024 * k + lo, 2560 + 1024 * k + lo), True, True)
+            tt(a("pt", 1024 * k, 1024 * k + 1024), a("pos_r", 1024 * k, 1024 * k + 1024), py, OP.subtract)
+
+    def absent():
+        act(a("hw", 8192, 10240), a("hw", 0, 2048))
+        ts(a("idu"), a("xf"), 16.0, OP.mult, pcol("c"), OP.add)
+        for k in range(4):
+            act(a("ow", 2048 + 1024 * k, 3072 + 1024 * k), ind(a("pos_r"), a("idu", 64 * k, 64 * k + 64)), AF.Relu, bias=BIG, scale=-BIG)
+
+    def nothing():
+        return None
+
+    def requests(r, gap1, gap1b, gap2, gap3, gap4, gap5, gap6):
+        w = "w%d" % (r % 2)
+        if r > 0:
+            cp(a("g2"), ind(a("g2c"), a("lu", 0, 32)))
+            act(a("d0"), ind(a("g2c"), a("lu", 0, 32)), AF.Relu, bias=1.0, scale=pcol("nh8"))
+        else:
+            tt(a("g2"), ind(a("tab"), a("l3", 0, 32)), a("mq"), OP.mult)
+            act(a("d0"), a("g2"), AF.Relu, bias=1.0, scale=pcol("nh8"))
+        act(a("pcc"), a("g2"), AF.Sign)
+        gap1()
+        scan(a("ss", 1, 513), a("d0"), a("g2"), pcol("lo8"), OP.mult, OP.add)
+        hv = (a("py0", 0, 256), a("py0", 512, 768))
+        lv = (a("py1", 0, 256), a("py1", 512, 768))
+        mm(hv[0], a("bdp"), a("ss", 1, 257), True, False)
+        mm(hv[0], a("bdm"), a("ss", 0, 256), False, True)
+        tt(a("xm"), a("pcc"), a("ss", 0, 512), OP.mult)
+        w2l(a("pcc", 0, 32), "sz", "xm", 0, 512)
+        mm(hv[1], a("bdp"), a("ss", 257, 513), True, False)
+        mm(hv[1], a("bdm"), a("ss", 256, 512), False, True)
+        act(a("g2b"), a("g2"))
+        gap1b()
+        gap2()
+        act(a("hh", 0, 256), hv[0], bias=pcol("bb0"), scale=pcol("beta"))
+        act(lv[0], hv[0], bias=pcol("gam"), scale=ek(1))
+        ts(a("zc"), a("pcc", 0, 32), 1.0, OP.max, 768.0, OP.min)
+        tt(a("zv"), a("pcc", 0, 32), a("zc"), OP.is_equal)
+        tt(a("zd"), a("zc"), a("sel", 64, 96), OP.add)
+        tt(a("val", 0, 256), lv[0], a("hh", 0, 256), OP.add)
+        tt(a("ze"), a("zd"), a("zv"), OP.mult)
+        gap3()
+        act(a("hh", 256, 512), hv[1], bias=pcol("bb0"), scale=pcol("beta"))
+        act(lv[1], hv[1], bias=pcol("gam"), scale=ek(1))
+        tt(a("ze"), a("ze"), a("ridx"), OP.max)
+        cp(a("offu"), a("ze"))
+        tt(a("val", 256, 512), lv[1], a("hh", 256, 512), OP.add)
+        gap4()
+        mm(a("pa", 0, 384), a("idb"), a("iotab"), True, False)
+        cp(ind(a(w), a("offu")), a("val"))
+        for k in range(16):
+            mm(a("pa", 0, 384), a("tri", 128 * k, 128 * k + 128), a(w, 512 + k, 6656, 16), False, k == 15)
+            if k == 3:
+                gap5()
+        scan(a("cc", 1, 385), a("pa", 0, 384), a("mend"), 0.0, OP.add, OP.mult)
+        mm(a("pcc", 0, 384), a("b15"), a("cc", 0, 384), True, True)
+        cp(a("p1s"), a("pa", 0, 384))
+        gap6()
+        tt(a("p1s"), a("pcc", 0, 384), a("p1s"), OP.add)
+        ts(a("as%d" % r), a("p1s"), 16383.0, OP.min)
+        send([(d, a("as%d" % r, 48 * d, 48 * d + 48), a("al%d" % r, 48 * rank, 48 * rank + 48), "aa%d" % rank) for d in others], 2)
+        for d in others:
+            landed("aa%d" % d, 2, a("al%d" % r, 48 * d, 48 * d + 48))
+
+    def segments_a(r):
+        w2l(a("pd", 0, 32), "szb", "g2b", 0, 512)
+        mm(a("pcc"), a("bq"), a("xm"), True, True)
+
+    def segments_s(r):
+        act(a("uu"), a("pcc"), AF.Abs, bias=pcol("zm"))
+        act(a("uu"), a("uu"), AF.Relu, bias=192.5, scale=-1.0)
+        act(a("mc%d" % (r % 2)), a("uu"), AF.Sign)
+
+    def segments_b(r):
+        s = str(r % 2)
+        ts(a("ua"), a("zc"), -1.0, OP.mult, 769.0, OP.add)
+        ts(a("ub"), a("zc"), 384.0, OP.is_gt, 384.0, OP.mult)
+        tt(a("ua"), a("pd", 0, 32), a("ua"), OP.min)
+        tt(a("ub"), a("zc"), a("ub"), OP.subtract)
+        tt(a("kv" + s), a("ua"), a("zv"), OP.mult)
+        tt(a("ep" + s), a("ua"), a("zd"), OP.add)
+        ts(a("lsu" + s), a("ub"), -1.0, OP.add)
+        tt(a("ua"), a("ub"), a("ua"), OP.add)
+        ts(a("leu" + s), a("ua"), -1.0, OP.add)
+
+    def own_gather(r, n, e):
+        d = order[n]
+        lst = a(("as%d" if d == rank else "al%d") % r, 48 * d, 48 * d + 48)
+        o = a("ow", 768 * n, 768 * n + 768)
+        if e == "S":
+            act(o, ind(a("hw"), lst))
+        else:
+            cp(o, ind(a("hw"), lst))
+
+    def own_extract(r, pr):
+        w2l(a("pa" if pr % 2 == 0 else "pcc", 0, 96), "sh", "ow", 1536 * pr, 1536 * pr + 1536)
+
+    def own_evac(r, pr):
+        p = "pa" if pr % 2 == 0 else "pcc"
+        if pr == 0:
+            cp(a("rl%d" % r, 48 * rank, 48 * rank + 48), a(p, 0, 48))
+            cp(a("rs%d" % r, 48, 96), a(p, 48, 96))
+        else:
+            cp(a("rs%d" % r, 96 * pr, 96 * pr + 96), a(p, 0, 96))
+
+    def own_send(r, ns):
+        send([(order[n], a("rs%d" % r, 48 * n, 48 * n + 48), a("rl%d" % r, 48 * rank, 48 * rank + 48), "ra%d" % rank) for n in ns], 4)
+
+    def candidates_a():
+        for k in range(16):
+            mm(a("py0", 0, 8), sel("sq4" if k % 2 else "sq0", k), a("skh", k // 2, 64, 8), k == 0, k == 15)
+
+    def candidates_b(last):
+        cp(a("l2", 0, 8), a("py0", 0, 8))
+        cp(a("wc"), ind(a("nxtw"), a("l2", 0, 8)))
+        if not last:
+            w2l(a("py0", 0, 8), "srh", "wc", 0, 128)
+
+    def candidates_d():
+        senses([(a("sk"), 0, 128)], 128, a("py0", 0, 8))
+        for x in range(2):
+            blend(a("cb", 96 * x, 96 * x + 32), a("sk", x, 128, 4), a("sk", 2 + x, 128, 4), "wu"[x])
+        for x in range(2):
+            cp(a("l2", 32 * x, 32 * x + 32), a("cb", 96 * x, 96 * x + 32))
+
+    def wide(r, lead):
+        w = "w%d" % (r % 2)
+        qs = [(rank - n) % N for n in range(N)]
+
+        def s_part(n):
+            q, s = qs[n], str(n % 2)
+            act(a("x" + s, 8, 776), ind(a("pt"), a("rl%d" % r, 48 * q, 48 * q + 48)))
+            act(a("py" + s, 0, 768), a("x" + s, 7, 775), AF.Relu, bias=1.0)
+
+        def p_part(n):
+            for h, p in enumerate(("pcc", "pd")):
+                lo = 512 + 768 * qs[n] + 384 * h
+                mm(a(p, 0, 384), a("idb"), a(w, lo, lo + 384), True, True)
+
+        s_part(0)
+        lead()
+        p_part(0)
+        for n in range(N):
+            q, s = qs[n], str(n % 2)
+            if n + 1 < N:
+                s_part(n + 1)
+            tt(a("dd" + s), a("x" + s, 8, 776), a("py" + s, 0, 768), OP.subtract)
+            for h, p in enumerate(("pcc", "pd")):
+                tt(a("ct" + s, 384 * h, 384 * h + 384), a("dd" + s, 384 * h, 384 * h + 384), a(p, 0, 384), OP.is_equal)
+            if n + 1 < N:
+                p_part(n + 1)
+            scan(a("rr" + s), a("ct" + s), a("ones"), 0.0, OP.mult, OP.add)
+            pieces = ((0, 0, 408), (1, 384, 768))
+            for fam, src, p in (("sd", "dd", "pa"), ("s1", "ct", "pb"), ("s2", "rr", "pa")):
+                for h, lo, hi in pieces:
+                    first = n == 0 and h == 0 and fam != "s2"
+                    last = n == N - 1 and h == 1 and fam != "sd"
+                    mm(a(p, 0, hi - lo), sel(fam, q + 8 * h), a(src + s, lo, hi), first, last, inc=(h == 1 and fam != "sd"))
+
+    def hot(r):
+        s = str(r % 2)
+        scan(a("ds", 1, 409), a("ones", 0, 408), a("nh"), 100.0, OP.add, OP.min)
+        tt(a("dg"), ind(a("ds"), a("leu" + s)), a("mc" + s), OP.mult)
+        w2l(a("pd", 0, 32), "s1", "dg", 0, 512)
+
+    def winners_list(r):
+        for k in range(16):
+            mm(a("py1", 0, 16), sel("sw4", k), a("winw", 64 * r + k // 4, 64 * r + 64, 4), k == 0, k == 15)
+
+    def winners_list_b():
+        tt(a("keyl", 0, 16), a("py1", 0, 16), a("base2"), OP.add)
+        cp(a("wiu"), a("keyl", 0, 16))
+
+    def totals(r):
+        s = str(r % 2)
+        last = r + 1 == RO
+        if not last:
+            both_senses_s()
+        act(a("nh"), a("pb", 0, 408), AF.Relu, bias=900.0, scale=-100.0)
+        if not last:
+            both_senses_v()
+        else:
+            ts(a("rw"), a("rl%d" % r), 1.0, OP.add)
+            hot(r)
+        scan(a("cs", 1, 409), a("pa", 0, 408), a("m16"), 0.0, OP.add, OP.add)
+        if last:
+            barrier_b(r)
+            barrier_c1(r)
+        tt(a("ge"), ind(a("cs"), a("leu" + s)), a("mc" + s), OP.mult)
+        for k in range(4):
+            mm(a("pcc", 0, 128), a("bop"), a("ge", k, 512, 4), k == 0, False)
+        tt(a("uu"), ind(a("cs"), a("lsu" + s)), a("mc" + s), OP.mult)
+        for k in range(4):
+            mm(a("pcc", 0, 128), a("bon"), a("uu", k, 512, 4), False, k == 3)
+        if not last:
+            hot(r)
+        else:
+            barrier_c2(r)
+            barrier_c3(r)
+            barrier_c4(r)
+        y0 = 128 * r
+        cp(a("ytb", y0, y0 + 128), a("pcc", 0, 128))
+        tt(a("winw", 64 * r, 64 * r + 64), a("ytb", y0 + 1, y0 + 128, 2), a("ytb", y0, y0 + 128, 2), OP.is_gt)
+
+    def choose(r):
+        ts(a("wa"), a("winw", 64 * r, 64 * r + 64, 2), pcol("lo512"), OP.mult)
+        ts(a("wb"), a("winw", 64 * r + 1, 64 * r + 64, 2), pcol("hi512"), OP.mult)
+        tt(a("wa"), a("wa"), a("ridx"), OP.add)
+        tt(a("winl"), a("wa"), a("wb"), OP.add)
+        cp(a("lu", 0, 32), a("winl"))
+        winners_list(r)
+
+    def window_base(r):
+        ts(a("wa"), a("winl"), 512.0, OP.is_ge)
+        tt(a("wa"), a("wa"), a("cd", 0, 32), OP.mult)
+        tt(a("sel", 64, 96), a("wa"), a("pq", 0, 32), OP.add)
+
+    def both_senses_s():
+        act(a("rqw"), a("rqw"), AF.Abs, bias=pcol("qb"))
+        act(a("rqw"), a("rqw"), AF.Relu, bias=float(2 ** 24), scale=-32768.0)
+
+    def both_senses_v():
+        tt(a("g2c"), ind(a("tab"), a("l3")), a("rqw"), OP.min)
+
+    def heads(r):
+        win = a("winw", 64 * r, 64 * r + 64)
+        jobs = [(a("ywb", 64 * r, 64 * r + 64), "wc", "f3")] + ([(a("skh"), "sk", "f4")] if r + 1 < RO else [])
+        for o, src, t in jobs:
+            tt(a(t, 0, 64), a(src, 1, 128, 2), a(src, 0, 128, 2), OP.subtract)
+        for o, src, t in jobs:
+            tt(a(t, 0, 64), a(t, 0, 64), win, OP.mult)
+        for o, src, t in jobs:
+            tt(o, a(t, 0, 64), a(src, 0, 128, 2), OP.add)
+
+    def barrier_b(r):
+        s = str(r % 2)
+        ts(a("va"), a("pd", 0, 32), 24.0, OP.min, 513.0, OP.add)
+        tt(a("vb"), a("pd", 0, 32), a("kv" + s), OP.is_ge)
+        tt(a("va"), a("ep" + s), a("va"), OP.subtract)
+        ts(a("vb"), a("vb"), 99.0, OP.mult)
+        ts(a("m1"), a("va"), 0.0, OP.max)
+        ts(a("m2"), a("m1"), 15, OP.bitwise_and)
+        ts(a("m3"), a("m1"), 4, OP.logical_shift_right)
+        tt(a("lowh"), a("m2"), a("vb"), OP.add)
+        cp(a("colu"), a("m3"))
+
+    def barrier_c1(r):
+        for k in range(16):
+            mm(a("pb", k, 512, 16), a("rs", 128 * k, 128 * k + 128), a("lowh"), True, True, inc=(k == 15))
+
+    def barrier_c2(r):
+        if r + 1 < RO:
+            act(a("bd"), a("pb"), AF.Abs, bias=pcol("nc"))
+            act(a("bd"), a("bd"), AF.Relu, bias=1.0, scale=-1.0)
+        else:
+            ts(a("bd"), a("pb"), pcol("c"), OP.is_equal)
+
+    def barrier_c3(r):
+        tt(a("bw"), ind(a("rw"), a("colu")), a("bd"), OP.mult)
+
+    def barrier_c4(r):
+        mm(a("pb"), a("bop"), a("bw"), True, True)
+
+    def barrier_d(r):
+        act(a("bd"), a("pb"), bias=-1.0)
+        if r + 1 < RO:
+            ts(a("b16"), ind(a("bd"), a("wiu")), -2047.0, OP.add)
+            w2l(a("pb", 0, 16), "srh", "b16", 0, 256)
+            tt(a("keyw"), a("b16"), a("rfrac"), OP.add)
+            act(a("ybb", 256 * r, 256 * r + 256), ind(a("bd"), a("wiu")))
+            ts(a("va", 0, 16), a("ridx", 0, 16), -1.0 / 512, OP.mult, -1.0 / 1024, OP.add)
+            ts(a("vb", 0, 16), a("ridx", 0, 16), 4096.0, OP.add)
+        else:
+            cp(a("ybb", 256 * r, 256 * r + 256), ind(a("bd"), a("wiu")))
+
+    def barrier_e(r, lo, hi):
+        if lo == 0:
+            tt(a("keyl", 0, 16), a("va", 0, 16), a("pb", 0, 16), OP.subtract)
+            ts(a("vb", 16, 32), a("pb", 0, 16), 2047.0, OP.add)
+            ts(a("keyl", 16, 32), a("pb", 0, 16), -1.0, OP.mult, -255.5 / 512, OP.add)
+            at = [768]
+            for i in range(16):
+                for x in range(2):
+                    o, k_, b_ = a("mn", 16 * x + i, 16 * x + i + 1), a("keyw", 16 * i, 256), a("keyl", 16 * x + i, 16 * x + i + 1)
+                    z = a("ow", at[0], at[0] + 256 - 16 * i)
+                    at[0] += 256 - 16 * i
+                    before("S", [], [z])
+                    op("S", o, [k_, b_], lambda: g.scalar.activation(z[0], k_[0], AF.Sign, bias=b_[0], accum_out=o[0]))
+                    after(("S", cnt["S"]), [], [z])
+        if hi == 16:
+            ts(a("va", 16, 32), a("vb", 16, 32), 0.0, OP.is_ge)
+            tt(a("vb", 16, 32), a("vb", 16, 32), a("vb", 0, 16), OP.subtract)
+            tt(a("va", 16, 32), a("va", 16, 32), a("vb", 16, 32), OP.mult)
+            tt(a("mn", 0, 16), a("mn", 0, 16), a("mn", 16, 32), OP.is_equal)
+            tt(a("va", 0, 16), a("va", 16, 32), a("mn", 0, 16), OP.mult)
+            tt(a("va", 0, 16), a("va", 0, 16), a("vb", 0, 16), OP.add)
+            cp(a("bu"), a("va", 0, 16))
+            cp(ind(a("pt"), a("bu")), a("negb"))
+
+    def next_table():
+        for k in range(16):
+            mm(a("py0", 64 * k, 64 * k + 64), a("rs", 128 * k, 128 * k + 128), a("hn"), True, True)
+        act(a("nxtw"), a("py0"))
+
+    OWN = ("SSSSVSVS", "SSVSVVVS", "SSVSVSVS")
+
+    def seq(*fs):
+        def run():
+            for f in fs:
+                f()
+        return run
+
+    for r in range(RO):
+        p = r - 1
+        last = r + 1 == RO
+        if r == 0:
+            requests(r, startup_1, nothing, startup_2, nothing, absent, seq(next_table, startup_3), nothing)
+        else:
+            requests(r, seq(lambda: barrier_b(p), lambda: barrier_c1(p)),
+                     seq(lambda: window_base(r), winners_list_b, lambda: barrier_c2(p)),
+                     lambda: ts(a("rw"), a("rl%d" % p), 1.0, OP.add),
+                     seq(lambda: barrier_c3(p), lambda: barrier_c4(p), lambda: segments_a(r)),
+                     nothing,
+                     seq(lambda: barrier_d(p), lambda: segments_s(r), lambda: barrier_e(p, 0, 0), lambda: heads(p), lambda: segments_b(r)),
+                     nothing)
+        eng = OWN[r]
+        own_gather(r, 0, eng[0])
+        if r == 0:
+            startup_4()
+            segments_a(r)
+            segments_s(r)
+            own_gather(r, 1, eng[1])
+            positions([0, 1, 2, 3])
+            own_gather(r, 2, eng[2])
+            own_gather(r, 3, eng[3])
+        candidates_a()
+        candidates_b(last)
+        if r > 0:
+            own_gather(r, 1, eng[1])
+        own_extract(r, 0)
+        if not last:
+            candidates_d()
+        if r > 0:
+            own_gather(r, 2, eng[2])
+            own_gather(r, 3, eng[3])
+        own_extract(r, 1)
+        own_evac(r, 0)
+        if r > 0:
+            barrier_e(p, 16, 16)
+        own_evac(r, 1)
+        own_send(r, [1, 2, 3])
+        if r == 0:
+            segments_b(r)
+            startup_5()
+        own_gather(r, 4, eng[4])
+        own_gather(r, 5, eng[5])
+        if not last:
+            lists_a(2)
+        own_extract(r, 2)
+        own_gather(r, 6, eng[6])
+        own_gather(r, 7, eng[7])
+        own_extract(r, 3)
+        own_evac(r, 2)
+        own_evac(r, 3)
+        own_send(r, [4, 5, 6, 7])
+        for d in others:
+            landed("ra%d" % d, 4, a("rl%d" % r, 48 * d, 48 * d + 48))
+        if not last:
+            iota(a("w%d" % ((r + 1) % 2), 0 if r == 0 else 512, 6656), [[0, 6656 if r == 0 else 6144]], 0, 0)
+        wide(r, nothing if last else (lambda: lists_b(2)))
+        totals(r)
+        if not last:
+            choose(r)
+    r = RO - 1
+    rows = slice(0, 128, 16)
+    winners_list(r)
+    heads(r)
+    dmas("dout", [("Y", T.yt[:], a("ytb", rows=rows)), ("Y", T.yw[:], a("ywb", rows=rows))])
+    winners_list_b()
+    barrier_d(r)
+    dmas("d9", [("Y", T.yb[:], a("ybb", rows=rows))])
+    for e in cnt:
+        need("G", (e, cnt[e]))
+    for s in sorted(tot):
+        need("G", (s, tot[s]))

@@ -2,8 +2,17 @@ from concourse.bass import DstId, RemoteDMATransfer
 from concourse.mybir import AluOpType as OP, AxisListType, ActivationFunctionType as AF
 
 F, B, H, I, U = "float32", "bfloat16", "float16", "int32", "uint16"
-BIG = float(2 ** 60)
 RO = 3
+CUT = 49152.0
+ADDR = ((0, 3), (3, 8))
+BACK = ((0, 1), (1, 3), (3, 5), (5, 8))
+OWN = "VVSVSSVS"
+PRESENT = "VSVSSVSS"
+DEEP = 2
+CYCLE = {"V": 0.00083, "S": 0.00083, "G": 0.00083, "P": 0.00042}
+FIXED = {"V": 0.05, "S": 0.065, "G": 0.13, "P": 0.0}
+GATHER, SCATTER = 1.56, 3.8
+WAKE, DMA_LATE, DMA_RATE, SEND, SEND_LATE, FIRST = 0.09, 1.5, 250e3, 0.6, 1.8, 3.0
 
 
 def _scratch():
@@ -13,34 +22,31 @@ def _scratch():
         for k, w in kw.items():
             s[k] = ("sbuf", [128, w], dt)
     sb(I, io_p=4, gst_r=68, gln_r=68, cur_r=4, rel_r=256, sens_r=128, nxt_r=64, heap_r=1024, pos_r=4096,
-       tli=704, lnf=704, tab=1024, n1=64, n2=64, n4=64, m1=32, m2=32, m3=32, ti=256)
-    sb(F, pc=40, ek=16, xf=256, sr0=144, bon=128, bop=128, bdp=128, bdm=128, b15=128,
-       relw=4096, sensw=2048, nxtw=1024, pt=4352, f1=128, f2=128, f3=128, f4=128, mend=384, m16=408,
-       ridx=32, base2=16, rfrac=256, negb=256, skw=64, sk=128, rqw=1024, cb=192, cd=32, pq=64, sel=96, winl=32,
-       wa=32, wb=32, va=32, vb=32, ua=32, ub=32,
-       a1=512, mq=512, g2=512, d0=512, ss=516, zc=32, zv=32, zd=32, ze=32, cc=388, p1s=384,
-       x0=776, x1=776, cs=416, ds=416, ge=512, uu=512, mc0=512, mc1=512, kv0=32, kv1=32, ep0=32, ep1=32,
-       rw=384, bw=512, bd=512, keyw=256, keyl=32, mn=32, ytb=384, ybb=768, ywb=192, nh=408)
-    sb(U, idu=256, l3=64)
-    sb(I, g2c=1024)
-    sb(F, idf=128)
-    sb(B, idn=128)
-    sb(B, iotab=384, idb=128, r143=144, rg=128, b1=128, b2=128, s2=144, s1=144, sd=144, sh=144, szb=144, sw4=144, tri=2048, hhi=1024, hlo=1024,
-       hw=16384, w0=6656, w1=6656, winw=192,
-       hh=512, val=512, g2b=512, ow=6144, dd0=768, dd1=768, ct0=768, ct1=768, rr0=768, rr1=768, ones=768, dg=512)
-    sb(H, sq0=144, sq4=144, skh=64, wc=128, sz=144, srh=144, bq=128, rs=2048, ht=256, hq=256, hs=128, hn=64, xm=512, lowh=32, b16=256)
-    sb(U, tl=704, lu=64, l2=64, offu=32, lsu0=32, lsu1=32, leu0=32, leu1=32, colu=32, bu=16, wiu=16)
+       tli=704, lnf=528, tab=1024, sw=1024, rp=768, ti=256, sp=256, sx=256, m1=16, m2=32)
+    sb(F, pc=40, ek=16, ek8=16, ek3=48, xf=256, bon=128, bop=128, bdp=128, bdm=128, b15=128, idf=128, lsf=144, wsf=144, rqf=144,
+       f1=144, f2=144, f3=144, f4=144, f5=144, f6=144, f7=128, mend=384, ridx=32, top=32, top2=16, cd2=16, nfr=16, gone=256, heapf=1024,
+       pt=4368, tsy=1024, gc=128, msk=1024, g2c=1024, pq=64, cd=32, sel=32,
+       wa=32, wb=32, wc=32, ab=32, wl=32, wm=32, winr=64, hd=64, hd2=64, ls0=64,
+       g2=512, d0=512, ss=516, zf=32, zt=32, zu=32, zo=32, cc=392, near=384,
+       sh_=32, se=32, sl=32, sr=32, sq=32, ba=32, bb=32, bd=32,
+       cs=416, ds=416, keep=408, nh=408, ge=512, mc=512, mk=256,
+       rw=392, keyw=256, keyl=32, mn=32, bu_=16, bv=16, ytb=384, ybb=768, ywb=192)
+    sb(B, iotab=384, idb=128, idn=128, r143=144, rg=128, b1=128, b2=128, b3=128, b4=128, bc=128, s2=144, s1=144, sh=144, szb=144, sf=144,
+       sk=144, sn=144, tri=2048, hhi=1024, hlo=1024, hw=16384, w=6656, relw=4096, rpb=768, rqw=1024,
+       hh=512, val=512, g2b=512, ow=6144, junk=4352, ones=408, fl=384, dg=512)
+    sb(H, sz=144, sm=144, boh=128, rfr=256, xm=512, bw=256)
+    sb(U, tl=704, idu=64, lu=32, l2=64, l3=128, lcur=4, lnx=64, lsy=8, offu=32, leu=32, rho=32, cl=32, bu=16, lx=384)
     for r in range(RO):
         sb(U, **{"as%d" % r: 384, "al%d" % r: 384, "rs%d" % r: 384, "rl%d" % r: 384})
-    share = {"g2c": ("pos_r", 0), "tli": ("pos_r", 1024), "lnf": ("pos_r", 1728), "ti": ("pos_r", 2944),
-             "rel_r": ("pos_r", 3200), "sens_r": ("pos_r", 3456), "nxt_r": ("pos_r", 3584),
-             "dd0": ("ow", 0), "ct0": ("ow", 768), "rr0": ("ow", 1536), "dd1": ("ow", 2304), "ct1": ("ow", 3072), "rr1": ("ow", 3840),
-             "hhi": ("ow", 0), "hlo": ("ow", 1024), "a1": ("x0", 16), "mq": ("x1", 16)}
+    for k in range(DEEP):
+        sb(F, **{"y%d" % k: 776})
+        sb(B, **{"ct%d" % k: 768, "rr%d" % k: 768, "pr%d" % k: 768})
+    share = {"hhi": ("junk", 0), "hlo": ("junk", 1024), "rpb": ("junk", 2048), "heapf": ("g2c", 0)}
     place, top, out = {}, {}, {}
     for k, (_w, sh, dt) in s.items():
         if k in share:
-            continue
-        if sh[1] >= 1024:
+            place[k] = (share[k][0], share[k][1], sh[1])
+        elif sh[1] >= 1024:
             out[k] = s[k]
             place[k] = (k, 0, sh[1])
         else:
@@ -48,17 +54,15 @@ def _scratch():
             place[k] = (pool, top.get(pool, 0), sh[1])
             top[pool] = top.get(pool, 0) + (sh[1] + 15) // 16 * 16
             out[pool] = ("sbuf", [128, top[pool]], dt)
-    for k, (base, off) in share.items():
-        place[k] = (place[base][0], place[base][1] + off, s[k][1][1])
-    for k, w in (("py0", 1024), ("py1", 1024), ("pa", 512), ("pb", 512), ("pcc", 512), ("pd", 512)):
-        out[k] = ("psum", [128, w], F)
-        place[k] = (k, 0, w)
+    for k in range(8):
+        out["p%d" % k] = ("psum", [128, 512], F)
+        place["p%d" % k] = ("p%d" % k, 0, 512)
     return out, place
 
 
 SCRATCH, PLACE = _scratch()
-SEMAPHORES = (["V", "S", "P", "G", "loc", "tarr", "dout"] + ["d%d" % k for k in range(10)]
-              + ["aa%d" % k for k in range(8)] + ["ra%d" % k for k in range(8)])
+SEMAPHORES = (["V", "S", "P", "G", "loc", "tarr", "clr"] + ["d%d" % k for k in range(12)] + ["q%d" % k for k in range(4)]
+              + ["aa%d" % k for k in range(1, 8)] + ["ra%d" % k for k in range(1, 8)])
 
 
 def rank_program(g, core, T, topo):
@@ -77,12 +81,13 @@ def rank_program(g, core, T, topo):
         lo, hi = off + lo, off + (w if hi is None else hi)
         cs_ = slice(lo, hi, st) if st != 1 else slice(lo, hi)
         ap = T[name][(slice(None) if rows is None else rows), cs_]
+        size = (128 if rows is None else 8, (hi - lo + st - 1) // st)
         if SCRATCH[name][0] == "psum":
-            return (ap, name, lo // 512 * 512, (hi + 511) // 512 * 512, True)
-        return (ap, name, lo, hi, False)
+            return (ap, name, 0, 512, True, size)
+        return (ap, name, lo, hi, False, size)
 
     def ind(win, off):
-        return (win[0].indirect(off[0]), win[1], win[2], win[3], False, off)
+        return (win[0].indirect(off[0]), win[1], win[2], win[3], False, (128, 16 * off[5][1]), off)
 
     def need(e, tok):
         if known[e].get(tok[0], 0) < tok[1]:
@@ -109,89 +114,162 @@ def rank_program(g, core, T, topo):
             l = [r for r in rec.get(x[1], []) if not (x[2] <= r[0] and r[1] <= x[3])]
             rec[x[1]] = l + [(x[2], x[3], tok, True)]
 
-    def op(e, out, ins, call, inc=True):
+    calls, seen = [], {}
+
+    def note(e, reads, writes, time, late, emit, behind=()):
+        me, deps = len(calls), set(behind)
+        for lst, wr in ((reads, False), (writes, True)):
+            for x in lst:
+                deps.update(i for (lo, hi, i, w) in seen.get(x[1], [])
+                            if lo < x[3] and x[2] < hi and (w or wr or (x[4] and calls[i][0] != e)))
+        for x in reads:
+            seen.setdefault(x[1], []).append((x[2], x[3], me, False))
+        for x in writes:
+            seen[x[1]] = [r for r in seen.get(x[1], []) if not (x[2] <= r[0] and r[1] <= x[3])] + [(x[2], x[3], me, True)]
+        deps.discard(me)
+        calls.append((e, time, late, sorted(deps), emit))
+        return me
+
+    def issue_all():
+        n = len(calls)
+
+        def gap(i, j):
+            return 0.0 if calls[i][0] == calls[j][0] == "P" else calls[i][2]
+        way = [c[1] + c[2] for c in calls]
+        for j in range(n - 1, -1, -1):
+            for i in calls[j][3]:
+                way[i] = max(way[i], calls[i][1] + gap(i, j) + way[j])
+        start, held = [0.0] * n, {}
+        for j in sorted(range(n), key=lambda j: (-way[j], j)):
+            t = max([start[i] + calls[i][1] + gap(i, j) for i in calls[j][3]] + [0.0])
+            slots = held.setdefault(calls[j][0], [])
+            k = 0
+            while k < len(slots) and slots[k][0] < t + calls[j][1]:
+                t = max(t, slots[k][1])
+                k += 1
+            slots.insert(k, (t, t + calls[j][1]))
+            start[j] = t
+        awaited = set()
+        for c in calls:
+            mine = [i for i in c[3] if calls[i][0] == "P"]
+            if mine and c[0] != "P":
+                awaited.add(max(mine, key=lambda i: (start[i], i)))
+        for j in sorted(range(n), key=lambda j: (start[j], j)):
+            calls[j][4](calls[j][0] != "P" or j in awaited)
+
+    def narrow(x):
+        return SCRATCH[x[1]][2] in (B, H, U)
+
+    def op(e, out, ins, call, rate=1.0, also=()):
         reads = [x for x in ins if isinstance(x, tuple)]
-        reads = reads + [x[5] for x in reads + [out] if len(x) > 5]
-        before(e, reads, [out])
-        ins_ = call()
-        if inc:
-            ins_.then_inc(T.sem[e], 1)
-            cnt[e] += 1
-            after((e, cnt[e]), reads, [out])
-        else:
-            after((e, cnt[e] + 1), reads, [out])
+        if len(out) > 6:
+            rate = SCATTER
+        elif any(len(x) > 6 for x in reads):
+            rate = GATHER
+        n = out[5][1]
+        time = FIXED[e] + CYCLE[e] * (rate * max(64, n) if e == "P" else max(64, rate * n))
+        reads = reads + [x[6] for x in reads + [out] if len(x) > 6]
+        writes = [out] + list(also)
+
+        def emit(inc):
+            before(e, reads, writes)
+            ins_ = call()
+            if inc:
+                ins_.then_inc(T.sem[e], 1)
+                cnt[e] += 1
+            after((e, cnt[e] + (0 if inc else 1)), reads, writes)
+        note(e, reads, writes, time, WAKE, emit)
 
     def v_(x):
         return x[0] if isinstance(x, tuple) else x
 
+    def half(*sides):
+        return 0.5 if all(narrow(x) for x in sides) else 1.0
+
     def ts(out, x, s1, o1, s2=None, o2=None):
         if o2 is None:
-            op("V", out, [x, s1], lambda: g.vector.tensor_scalar(out[0], x[0], v_(s1), None, o1))
+            op("V", out, [x, s1], lambda: g.vector.tensor_scalar(out[0], x[0], v_(s1), None, o1), half(out, x))
         else:
-            op("V", out, [x, s1, s2], lambda: g.vector.tensor_scalar(out[0], x[0], v_(s1), v_(s2), o1, o2))
+            op("V", out, [x, s1, s2], lambda: g.vector.tensor_scalar(out[0], x[0], v_(s1), v_(s2), o1, o2), half(out, x))
 
     def tt(out, x, y, o):
-        op("V", out, [x, y], lambda: g.vector.tensor_tensor(out[0], x[0], y[0], o))
+        op("V", out, [x, y], lambda: g.vector.tensor_tensor(out[0], x[0], y[0], o), 1.0 if x[4] or y[4] else 2.0)
 
     def cp(out, x):
-        op("V", out, [x], lambda: g.vector.tensor_copy(out[0], x[0]))
+        op("V", out, [x], lambda: g.vector.tensor_copy(out[0], x[0]), half(out, x))
 
     def ms(out, c):
-        op("V", out, [], lambda: g.vector.memset(out[0], c))
+        op("V", out, [], lambda: g.vector.memset(out[0], c), half(out))
 
     def scan(out, x, y, init, o0, o1):
-        op("V", out, [x, y, init], lambda: g.vector.tensor_tensor_scan(out[0], x[0], y[0], v_(init), o0, o1))
+        op("V", out, [x, y, init], lambda: g.vector.tensor_tensor_scan(out[0], x[0], y[0], v_(init), o0, o1), half(out, x, y))
 
-    def act(out, x, f=AF.Identity, bias=None, scale=None):
+    def act(out, x, f=AF.Identity, bias=None, scale=None, total=None):
         kw = {}
-        if bias is not None:
-            kw["bias"] = v_(bias)
-        if scale is not None:
-            kw["scale"] = v_(scale)
-        op("S", out, [x, bias, scale], lambda: g.scalar.activation(out[0], x[0], f, **kw))
+        for k, v in (("bias", bias), ("scale", scale), ("accum_out", total)):
+            if v is not None:
+                kw[k] = v_(v)
+        op("S", out, [x, bias, scale], lambda: g.scalar.activation(out[0], x[0], f, **kw), also=[total] if total else [])
 
     def iota(out, pat, base, cm, flt=True):
         if flt:
-            op("G", out, [], lambda: g.iota(out[0], pat, base, cm, allow_small_or_imprecise_dtypes=True))
+            op("G", out, [], lambda: g.iota(out[0], pat, base, cm, allow_small_or_imprecise_dtypes=True), 2.0)
         else:
-            op("G", out, [], lambda: g.iota(out[0], pat, base, cm))
+            op("G", out, [], lambda: g.iota(out[0], pat, base, cm), 2.0)
 
-    def mm(out, l, r, start, stop, inc=None):
-        op("P", out, [l, r], lambda: g.tensor.matmul(out[0], l[0], r[0], start, stop), inc=stop if inc is None else inc)
+    def mm(out, l, r, start, stop):
+        op("P", out, [l, r], lambda: g.tensor.matmul(out[0], l[0], r[0], start, stop), 1.0 if narrow(l) else 4.0)
 
     def dmas(sem, lst):
-        for (e, o, i_) in lst:
-            before(e, [i_] if isinstance(i_, tuple) else [], [o] if isinstance(o, tuple) else [])
-            Q[e].dma_start(v_(o), v_(i_)).then_inc(T.sem[sem], 16)
-        tot[sem] = tot.get(sem, 0) + 16 * len(lst)
-        for (e, o, i_) in lst:
-            after((sem, tot[sem]), [i_] if isinstance(i_, tuple) else [], [o] if isinstance(o, tuple) else [])
+        reads = [i_ for (o, i_) in lst if isinstance(i_, tuple)]
+        writes = [o for (o, i_) in lst if isinstance(o, tuple)]
+        size = 0
+        for (o, i_) in lst:
+            x = o if isinstance(o, tuple) else i_
+            size += x[5][0] * x[5][1] * (2 if narrow(x) else 4)
 
-    def send(lst, per):
-        trs = []
-        for n, (d, src, dst, sem) in enumerate(lst):
-            before("G", [src], [])
-            dc = T.cores[d]
-            en = topo.engines(core, dc)
-            m = 0
-            for k in range(per):
-                m |= 1 << en[n * per + k]
-            rid, pid, _se = topo.addr(dc)
-            trs.append(RemoteDMATransfer(dst_ids=[DstId(rid=rid, pnc=pid)], dma_engine_mask=m, remote_sem=T.sem[sem],
-                                         src=src[0], dst=dst[0]))
-        g.remote_dma_fused(trs, local_sem=T.sem.loc)
-        tot["loc"] = tot.get("loc", 0) + per * len(lst)
+        def emit(_inc):
+            before("Y", reads, writes)
+            for (o, i_) in lst:
+                g.sync.dma_start(v_(o), v_(i_)).then_inc(T.sem[sem], 16)
+            tot[sem] = tot.get(sem, 0) + 16 * len(lst)
+            after((sem, tot[sem]), reads, writes)
+        note("Y", reads, writes, 0.1 * len(lst) + size / DMA_RATE, DMA_LATE, emit)
 
-    def landed(sem, n, place):
-        tot[sem] = tot.get(sem, 0) + n
-        after((sem, tot[sem]), [], [place])
+    def send(lst, first=0.0):
+        per = 1
+        while 2 * per * len(lst) <= len(topo.engines(core, T.cores[lst[0][0]])):
+            per *= 2
+
+        def emit(_inc):
+            trs = []
+            for n, (d, src, dst, sem) in enumerate(lst):
+                before("G", [src], [])
+                dc = T.cores[d]
+                en = topo.engines(core, dc)
+                m = 0
+                for k in range(per):
+                    m |= 1 << en[n * per + k]
+                rid, pid, _se = topo.addr(dc)
+                trs.append(RemoteDMATransfer(dst_ids=[DstId(rid=rid, pnc=pid)], dma_engine_mask=m, remote_sem=T.sem[sem],
+                                             src=src[0], dst=dst[0]))
+            tot["loc"] = tot.get("loc", 0) + per * len(lst)
+            g.remote_dma_fused(trs, local_sem=T.sem.loc)
+
+        def landed(_inc):
+            for (d, src, dst, sem) in lst:
+                tot[sem] = tot.get(sem, 0) + per
+            for (d, src, dst, sem) in lst:
+                after((sem, tot[sem]), [], [dst])
+        me = note("G", [x[1] for x in lst], [], SEND + first, SEND_LATE, emit)
+        note("landing", [], [x[2] for x in lst], 0.0, 0.0, landed, [me])
 
     def sel(fam, k):
         return a(fam, 15 - k, 143 - k)
 
-    def w2l(out, fam, src, lo, hi):
+    def w2l(out, fam, src, lo, hi, start=True, stop=True):
         for k in range(16):
-            mm(out, sel(fam, k), a(src, lo + k, hi, 16), k == 0, k == 15)
+            mm(out, sel(fam, k), a(src, lo + k, hi, 16), start and k == 0, stop and k == 15)
 
     col = {}
 
@@ -203,600 +281,378 @@ def rank_program(g, core, T, topo):
     def ek(k):
         return a("ek", k, k + 1)
 
-    others = [(rank + d) % N for d in range(1, N)]
-    order = [rank] + others
+    def row(k):
+        return slice(k, 128, 16)
 
-    dmas("d0", [("Y", a("gst_r", 0, 64), T.gst[:]), ("S", a("gln_r", 0, 64), T.gln[:])])
-    dmas("d1", [("Y", a("rel_r"), T.rel[:])])
-    dmas("d2", [("S", a("sens_r"), T.sens[:])])
-    dmas("d3", [("S", a("cur_r"), T.cur[:])])
-    dmas("d4", [("Y", a("nxt_r"), T.nxt[:])])
-    dmas("d5", [("Y", a("heap_r"), T.heap[:])])
+    def fam(name, weight, at=0.0):
+        ts(a(name), a("r143"), at, OP.is_equal, weight, OP.mult)
+
+    dmas("d0", [(a("gst_r", 0, 64), T.gst[:]), (a("gln_r", 0, 64), T.gln[:])])
+    dmas("d1", [(a("sens_r"), T.sens[:])])
+    dmas("d2", [(a("rel_r"), T.rel[:])])
+    dmas("d3", [(a("cur_r", c, c + 1), T.cur[:, 16 * c:16 * c + 16]) for c in range(4)])
+    dmas("d4", [(a("nxt_r"), T.nxt[:])])
+    dmas("d5", [(a("heap_r"), T.heap[:])])
+    for k in range(4):
+        dmas("q%d" % k, [(a("pos_r", 1024 * k, 1024 * k + 1024), T.wpos[:, 1024 * k:1024 * k + 1024])])
+
     iota(a("io_p", 0, 1), [[0, 1]], 0, 1, False)
     iota(a("xf"), [[1, 256]], 0, 0)
-
-    ms(a("hw", 0, 2048), 0.0)
-    act(a("hw", 2048, 4096), a("hw", 0, 2048))
-    act(a("hw", 4096, 6144), a("hw", 0, 2048))
-    ms(a("gst_r", 64, 68), 0)
-    ms(a("gln_r", 64, 68), 0)
+    iota(a("sw"), [[1, 1024]], 0, 0, False)
     ts(a("io_p", 1, 2), a("io_p", 0, 1), 15, OP.bitwise_and)
     ts(a("io_p", 2, 3), a("io_p", 0, 1), 7, OP.bitwise_and)
     ts(a("io_p", 3, 4), a("io_p", 0, 1), 3, OP.bitwise_and)
     c_, c8, c4 = a("io_p", 1, 2), a("io_p", 2, 3), a("io_p", 3, 4)
     cp(pcol("c"), c_)
-    tt(pcol("g16"), a("io_p", 0, 1), c_, OP.subtract)
     cp(pcol("k"), c4)
-    ts(a("ek"), a("xf", 0, 16), pcol("c"), OP.is_equal)
+    cp(pcol("c8"), c8)
+    tt(pcol("g16"), a("io_p", 0, 1), c_, OP.subtract)
+    ts(a("idu"), a("xf", 0, 64), 16.0, OP.mult, pcol("c"), OP.add)
     ts(a("b1"), a("xf", 0, 128), pcol("g16"), OP.subtract)
     ts(a("r143"), a("xf", 0, 144), pcol("g16"), OP.subtract, 15.0, OP.subtract)
     ts(a("b2"), a("b1"), 15.0, OP.is_gt, 1000.0, OP.mult)
-    ts(pcol("lo8"), c_, 8, OP.is_lt)
     tt(a("rg"), a("b1"), a("b2"), OP.subtract)
+    ts(a("ek"), a("xf", 0, 16), pcol("c"), OP.is_equal)
+    ts(a("ek8"), a("xf", 0, 16), pcol("c8"), OP.is_equal)
+    ts(pcol("c3"), c_, 3.0, OP.mult)
+    ts(a("ek3"), a("xf", 0, 48), pcol("c3"), OP.is_equal)
+    ts(pcol("c4x"), c_, 4.0, OP.mult)
+    ts(pcol("w4"), c_, 2, OP.is_lt, 4.0, OP.mult)
+    ts(a("f5"), a("r143"), pcol("c4x"), OP.subtract, 0.0, OP.is_ge)
+    ts(a("f6"), a("r143"), pcol("c4x"), OP.subtract, 4.0, OP.is_lt)
+    tt(a("f5"), a("f5"), a("f6"), OP.mult)
+    ts(a("rqf"), a("f5"), pcol("w4"), OP.mult)
+    ts(pcol("h01"), c_, 2, OP.is_lt)
+    ts(pcol("lo8"), c_, 8, OP.is_lt)
+    ts(pcol("hi8"), c_, 8, OP.is_ge)
+    ts(pcol("nh8"), c_, 8, OP.is_ge, -1.0, OP.mult)
+    ts(a("ss", 0, 1), c_, 8, OP.is_lt, -768.0, OP.mult)
+    ts(pcol("hs"), ek(0), 65536.0, OP.mult, ek(1), OP.subtract)
+    ts(pcol("hb"), ek(0), ek(2), OP.subtract, CUT, OP.mult)
+    ts(pcol("wd"), pcol("hi8"), 2.0, OP.mult, -1.0, OP.add)
+    ts(pcol("u2"), ek(2), 0.25, OP.mult)
+    ts(pcol("u3"), ek(2), -(2.0 ** -14), OP.mult)
+    ts(pcol("u4"), ek(2), ek(3), OP.add)
+    ts(pcol("cm2"), c_, -2.0, OP.add)
+    ts(pcol("lo512"), pcol("lo8"), 512.0, OP.mult)
+    ts(pcol("hi512"), pcol("hi8"), 512.0, OP.mult)
+    ts(pcol("a0"), c8, 4, OP.is_lt)
+    ts(pcol("a1"), pcol("a0"), -2.0 / 512, OP.mult, 1.0 / 512, OP.add)
+    ts(pcol("u5"), pcol("hi8"), 4.0, OP.mult, pcol("k"), OP.add)
+    ts(a("idf"), a("rg"), pcol("c"), OP.is_equal)
+    ts(a("idb"), a("rg"), pcol("c"), OP.is_equal)
+    ts(a("idn"), a("rg"), pcol("c"), OP.is_equal, -1.0, OP.mult)
+    ts(a("b3"), a("rg"), 0.0, OP.is_equal, 2.0 ** -16, OP.mult)
+    ts(a("b4"), a("rg"), 1.0, OP.is_equal)
+    tt(a("f7"), a("b3"), a("b4"), OP.add)
+    ts(a("bc"), a("b4"), CUT / 16, OP.mult)
+    ts(a("bdp"), a("f7"), pcol("wd"), OP.mult)
+    ts(a("bdm"), a("f7"), pcol("wd"), OP.mult, -1.0, OP.mult)
+    ts(a("b15"), a("rg"), 0.0, OP.is_ge, ek(15), OP.mult)
+    ts(a("bon"), a("rg"), 0.0, OP.is_ge, -1.0, OP.mult)
+    ts(a("bop"), a("rg"), 0.0, OP.is_ge)
+    ts(a("boh"), a("rg"), 0.0, OP.is_ge)
+    for k in range(16):
+        ts(a("tri", 128 * k, 128 * k + 128), a("rg"), float(k), OP.is_ge)
+    for name, weight in (("sh", pcol("h01")), ("sn", ek(2)), ("sz", pcol("lo8")), ("szb", pcol("lo8")), ("sf", pcol("u2")),
+                         ("sk", pcol("u3")), ("s2", 2.0), ("s1", 1.0), ("sm", -1.0)):
+        fam(name, weight)
+    fam("lsf", pcol("u4"), pcol("cm2"))
+    fam("wsf", 1.0, pcol("u5"))
+    ts(a("ridx"), a("xf", 0, 32), 16.0, OP.mult, pcol("c"), OP.add)
+    ts(a("top"), a("ridx"), 6144.0, OP.add)
+    ts(a("top2"), a("ridx", 0, 16), 4097.0, OP.add)
+    ts(a("cd2"), a("ridx", 0, 16), -1.0, OP.mult, -2049.0, OP.add)
+    ts(a("nfr"), a("ridx", 0, 16), -1.0 / 512, OP.mult, -1.0 / 1024, OP.add)
+    ts(a("rfr"), a("xf"), 1.0 / 8192, OP.mult)
+    ms(a("relw"), 0.0)
+    ts(a("iotab"), a("relw", 0, 384), 0.0, OP.mult, pcol("c"), OP.add)
+    ts(a("iotab"), a("iotab"), 1.0, OP.add)
+    ts(a("iotab", 0, 384, 48), a("iotab", 0, 384, 48), -1.0, OP.add)
+    ms(a("ones"), 1.0)
+    ms(a("mend"), 1.0)
+    ms(a("mend", 47, 384, 48), 0.0)
+    ms(a("cc"), 0.0)
+    ms(a("cs", 0, 1), 0.0)
+    ms(a("ds", 0, 1), 16384.0)
+    ms(a("rw", 0, 8), -2048.0)
+    ms(a("gone"), -1.25)
+    ms(a("pt", 0, 1), -1.25)
+    ms(a("pt", 4097, 4368), 0.0)
+    for k in range(DEEP):
+        ms(a("y%d" % k, 7, 8), 0.25)
 
-    own = 88 * rank
+    ms(a("gst_r", 64, 68), 0)
+    ms(a("gln_r", 64, 68), 0)
     tt(a("f1", 0, 66), a("gst_r", 0, 66), a("gln_r", 0, 66), OP.add)
     ts(a("f2", 0, 66), a("gln_r", 0, 66), 0, OP.is_gt)
     ts(a("f3", 0, 22), a("gln_r", 1, 66, 3), 32.0, OP.mult)
     ts(a("f4", 0, 22), a("gln_r", 2, 66, 3), 1024.0, OP.mult)
     tt(a("f1", 0, 66), a("f1", 0, 66), a("f2", 0, 66), OP.mult)
     tt(a("f3", 0, 22), a("f3", 0, 22), a("gln_r", 0, 66, 3), OP.add)
-    ts(a("ti"), a("rel_r"), 1023, OP.bitwise_and)
     tt(a("f3", 0, 22), a("f3", 0, 22), a("f4", 0, 22), OP.add)
     for x in range(3):
-        cp(a("tl", own + x, own + 88, 4), a("f1", x, 66, 3))
-    cp(a("tl", own + 3, own + 88, 4), a("f3", 0, 22))
-    send([(d, a("tl", own, own + 88), a("tl", own, own + 88), "tarr") for d in others], 2)
-    tot["tarr"] = 2 * (N - 1)
-    for d in others:
-        after(("tarr", tot["tarr"]), [], [a("tl", 88 * d, 88 * d + 88)])
-    iota(a("w0"), [[0, 6656]], 0, 0)
-    iota(a("hw", 10240, 13312), [[0, 3072]], 0, 0)
-
-    cp(a("ht"), a("ti"))
-    tt(a("hq"), a("rel_r"), a("ti"), OP.subtract)
-    for k in range(16):
-        if k < 4:
-            ts(a("rs", 128 * k, 128 * k + 128), a("rg"), 0.0, OP.is_ge, ek(k), OP.mult)
-        py = "py%d" % (k // 4 % 2)
-        o = a(py, 256 * (k % 4), 256 * (k % 4) + 256)
-        mm(o, a("rs", 128 * k, 128 * k + 128), a("ht"), True, False)
-        mm(o, a("rs", 128 * k, 128 * k + 128), a("hq"), False, True)
-        if k % 4 == 3:
-            act(a("relw", 1024 * (k // 4), 1024 * (k // 4) + 1024), a(py))
-        if k == 3:
-            cp(a("hs"), a("sens_r"))
-            for j in range(4, 16):
-                ts(a("rs", 128 * j, 128 * j + 128), a("rg"), 0.0, OP.is_ge, ek(j), OP.mult)
-            for j in range(16):
-                mm(a(("pa", "pb", "pcc", "pd")[j // 4], 128 * (j % 4), 128 * (j % 4) + 128), a("rs", 128 * j, 128 * j + 128), a("hs"), True, True)
-    ts(pcol("hi8"), c_, 8, OP.is_ge)
-    ts(pcol("a0"), c8, 4, OP.is_lt, 4.0, OP.mult)
-    ts(pcol("a1"), c8, 4, OP.is_ge, 4.0, OP.mult)
-    ts(a("sr0"), a("r143"), 0.0, OP.is_equal, ek(0), OP.mult)
-    cp(a("hn"), a("nxt_r"))
+        cp(a("tl", x, 88, 4), a("f1", x, 66, 3))
+    cp(a("tl", 3, 88, 4), a("f3", 0, 22))
+    send([((rank - n) % N, a("tl", 0, 88), a("tl", 88 * n, 88 * n + 88), "tarr") for n in range(1, N)], FIRST)
+    for k in range(4):
+        iota(a("w", 1664 * k, 1664 * k + 1664), [[0, 1664]], 0, 0)
     cp(a("tli", 528, 704), a("tl", 3, 704, 4))
     for x in range(3):
         cp(a("tli", x, 528, 3), a("tl", x, 704, 4))
     ts(a("lnf", 0, 528, 3), a("tli", 528, 704), 31, OP.bitwise_and)
     ts(a("lnf", 1, 528, 3), a("tli", 528, 704), 5, OP.logical_shift_right, 31, OP.bitwise_and)
     ts(a("lnf", 2, 528, 3), a("tli", 528, 704), 10, OP.logical_shift_right)
-    dmas("d7", [("Y", a("tab", rows=slice(8 + q, 128, 16)), a("tli", 66 * q, 66 * q + 64)) for q in range(N)]
-         + [("Y", a("tab", rows=slice(q, 128, 16)), a("lnf", 66 * q, 66 * q + 64)) for q in range(N)])
-    for j, p in enumerate(("pa", "pb", "pcc", "pd")):
-        cp(a("sensw", 512 * j, 512 * j + 512), a(p))
+    dmas("d6", [(a("tab", rows=row(8 + q)), a("tli", 66 * q, 66 * q + 64)) for q in range(N)]
+         + [(a("tab", rows=row(q)), a("lnf", 66 * q, 66 * q + 64)) for q in range(N)])
 
-    def senses(out_pieces, n, src):
-        m = n // 16
-        ts(a("l2", 0, m), src, 2.0, OP.mult)
-        ts(a("l2", 8, 8 + m), src, 2.0, OP.mult, 1.0, OP.add)
-        ts(a("f1", 0, n), ind(a("sensw"), a("l2", 0, m)), pcol("a0"), OP.mult, pcol("k"), OP.add)
-        ts(a("f2", 0, n), ind(a("sensw"), a("l2", 8, 8 + m)), pcol("a1"), OP.mult)
-        for (o, lo, hi) in out_pieces:
-            tt(o, a("f1", lo, hi), a("f2", lo, hi), OP.add)
-
-    def blend(out, ev, od, t="w"):
-        ts(a(t + "a"), ev, pcol("lo8"), OP.mult)
-        ts(a(t + "b"), od, pcol("hi8"), OP.mult)
-        tt(out, a(t + "a"), a(t + "b"), OP.add)
-
-    def lists_a(nc):
-        if nc == 1:
-            cp(a("l2", 0, 32), a("cb", 0, 32))
-        act(a("rqw", 0, 512 * nc), ind(a("relw"), a("l2", 0, 32 * nc)))
-        w2l(a("pd", 0, 32 * nc), "sr0", "rqw", 0, 512 * nc)
-
-    def lists_b(nc):
-        n = 32 * nc
-        cp(a("n1", 0, n), a("pd", 0, n))
-        ts(a("n4", 0, n), a("n1", 0, n), 1023, OP.bitwise_and)
-        ts(a("n2", 0, n), a("n1", 0, n), 10, OP.logical_shift_right)
-        cp(a("l3", 0, n), a("n4", 0, n))
-        ts(a("pq", 0, n), a("n2", 0, n), 768.0, OP.mult, 511.0, OP.add)
-        if nc == 2:
-            tt(a("cd", 0, 32), a("pq", 32, 64), a("pq", 0, 32), OP.subtract)
-
-    senses([(a("skw", i, 64, 4), 16 * i, 16 * i + 16) for i in range(4)], 64, a("cur_r"))
-    blend(a("cb", 0, 32), a("skw", 0, 64, 2), a("skw", 1, 64, 2))
-    lists_a(1)
-    dmas("d6", [("Y", a("pos_r"), T.wpos[:])])
-    ts(pcol("qb"), c8, -1024.0, OP.mult, -511.5, OP.add)
-    act(a("a1"), a("rqw", 0, 512), AF.Abs, bias=pcol("qb"))
-    act(a("hw", 6144, 8192), a("hw", 0, 2048))
-    cp(a("skh"), a("skw"))
-    cp(a("pt", 0, 1024), a("heap_r"))
-    ts(a("idf"), a("rg"), pcol("c"), OP.is_equal)
-    ts(a("idn"), a("rg"), pcol("c"), OP.is_equal, -1.0, OP.mult)
-    act(a("hhi"), a("pt", 0, 1024))
-    for j, p in enumerate(("pa", "pb")):
-        mm(a(p), a("idf"), a("pt", 512 * j, 512 * j + 512), True, False)
+    for x in range(2):
+        cp(a("sp", 64 * x, 64 * x + 64), a("sens_r", x, 128, 2))
+    ts(a("sx", 0, 128), a("sp", 0, 128), 63, OP.bitwise_and)
+    ts(a("sx", 128, 256), a("sp", 0, 128), 6, OP.logical_shift_right)
+    ts(a("sx", 0, 128), a("sx", 0, 128), 16.0, OP.mult)
+    tt(a("sp", 128, 256), a("sx", 0, 128), a("sx", 128, 256), OP.add)
+    dmas("d7", [(a("sw", rows=row(x)), a("sp", 64 * x, 64 * x + 64)) for x in range(4)])
+    cp(a("lnx"), a("nxt_r"))
+    act(a("tsy"), ind(a("sw"), a("lnx")))
+    ts(a("ti"), a("rel_r"), float(1024 * (N - rank)), OP.add)
+    ts(a("rp", 0, 256), a("rel_r"), 992, OP.bitwise_and)
+    ts(a("rp", 256, 512), a("rel_r"), 31, OP.bitwise_and)
+    ts(a("rp", 512, 768), a("ti"), 10, OP.logical_shift_right, 7, OP.bitwise_and)
+    cp(a("rpb"), a("rp"))
+    dmas("d8", [(a("relw", rows=row(x)), a("rpb", 256 * x, 256 * x + 256)) for x in range(3)])
+    act(a("hhi"), ind(a("heap_r"), a("idu")))
+    act(a("heapf"), ind(a("heap_r"), a("idu")))
+    for j, p in enumerate(("p0", "p1")):
+        mm(a(p), a("idf"), a("heapf", 512 * j, 512 * j + 512), True, False)
         mm(a(p), a("idn"), a("hhi", 512 * j, 512 * j + 512), False, True)
-    b0 = 32768.5 / 2 ** 17
-    ts(pcol("u1"), c_, 2, OP.is_ge, 0.5, OP.mult)
-    ts(pcol("u2"), ek(1), b0, OP.mult)
-    tt(pcol("beta"), ek(0), ek(1), OP.subtract)
-    ts(pcol("h01"), c_, 2, OP.is_lt)
-    ts(pcol("nh8"), pcol("hi8"), -1.0, OP.mult)
-    ts(pcol("u3"), ek(2), -65536.0, OP.mult, ek(3), OP.subtract)
-    ts(pcol("wd"), pcol("hi8"), 2.0 ** -16, OP.mult, -(2.0 ** -17), OP.add)
-    tt(pcol("gam"), pcol("u1"), pcol("u2"), OP.add)
-    ts(pcol("bb0"), pcol("beta"), b0, OP.mult)
-    ts(pcol("nc"), c_, -1.0, OP.mult)
-    ts(pcol("wt"), pcol("h01"), float(2 ** 17), OP.mult, pcol("u3"), OP.add)
-    ts(a("bdp"), a("rg"), 0.0, OP.is_ge, pcol("wd"), OP.mult)
-    ts(a("sz"), a("r143"), 0.0, OP.is_equal, pcol("lo8"), OP.mult)
-    cp(a("ss", 0, 1), pcol("lo8"))
-    ts(a("bdm"), a("bdp"), -1.0, OP.mult)
-    ts(a("ridx"), a("xf", 0, 32), 16.0, OP.mult, pcol("c"), OP.add)
-    ts(a("idb"), a("rg"), pcol("c"), OP.is_equal)
-    ts(a("iotab"), a("hw", 0, 384), pcol("c"), OP.add, 1.0, OP.add)
-    ts(a("iotab", 0, 384, 48), a("hw", 0, 8), pcol("c"), OP.add)
-    ts(a("mq"), a("a1"), 512.0, OP.is_lt)
-    lists_b(1)
-    cp(a("sel", 64, 96), a("pq", 0, 32))
+        act(a("hlo", 512 * j, 512 * j + 512), a(p))
+    for k in range(16):
+        if k < HW_V:
+            ms(a("hw", 1024 * k, 1024 * k + 1024), 0.0)
+        else:
+            act(a("hw", 1024 * k, 1024 * k + 1024), a("hw", 0, 1024))
+    dmas("d9", [(a("hw", rows=row(0)), a("hhi")), (a("hw", rows=row(1)), a("hlo"))])
+    for k in range(4):
+        o, x = a("pt", 1 + 1024 * k, 1025 + 1024 * k), a("pos_r", 1024 * k, 1024 * k + 1024)
+        if k < POS_V:
+            ts(o, x, -1.25, OP.add)
+        else:
+            act(o, ind(x, a("idu")), bias=-1.25)
 
-    def startup_1():
+    def look_up(nc):
+        n = 32 * nc
+        for x in range(nc):
+            for b in range(2):
+                mm(a("p7", 32 * x, 32 * x + 32), sel("rqf", 8 * b), a("gc", nc * b + x, 64 * nc, 2 * nc), x + b == 0, x == nc - 1 and b == 1)
+        ts(a("l2", 0, n), a("p7", 0, n), pcol("k"), OP.add)
+        act(a("rqw", 0, 16 * n), ind(a("relw"), a("l2", 0, n)))
+        w2l(a("p7", 0, n), "sh", "rqw", 0, 16 * n, stop=False)
+        w2l(a("p7", n, 2 * n), "sn", "rqw", 0, 16 * n, start=False)
+        cp(a("l3", 0, 2 * n), a("p7", 0, 2 * n))
+        ts(a("pq", 0, n) if nc == 2 else a("sel"), a("p7", n, 2 * n), 768.0, OP.mult, 768.0, OP.add)
+        act(a("msk", 0, 16 * n), ind(a("ek8"), a("l3", n, 2 * n)))
+        if nc == 2:
+            tt(a("cd"), a("pq", 32, 64), a("pq", 0, 32), OP.subtract)
+            ts(a("cd"), a("cd"), 1.0 / 512, OP.mult)
+            for h in range(2):
+                tt(a("g2c", 512 * h, 512 * h + 512), ind(a("tab"), a("l3", 32 * h, 32 * h + 32)), a("msk", 512 * h, 512 * h + 512), OP.mult)
+
+    def next_senses(src, lo):
         for k in range(8):
-            ts(a("tri", 128 * k, 128 * k + 128), a("rg"), float(k), OP.is_ge, pcol("wt"), OP.mult)
+            mm(a("p7", 0, 8), sel("lsf", 2 * k), a(src, lo + k, lo + 64, 8), k == 0, k == 7)
+        cp(a("lsy"), a("p7", 0, 8))
+        act(a("gc"), ind(a("tsy"), a("lsy")))
 
-    def startup_2():
-        act(a("hlo", 0, 512), a("pa"))
-        act(a("hlo", 512, 1024), a("pb"))
-        for k in range(8, 16):
-            ts(a("tri", 128 * k, 128 * k + 128), a("rg"), float(k), OP.is_ge, pcol("wt"), OP.mult)
+    cp(a("lcur"), a("cur_r"))
+    act(a("gc", 0, 64), ind(a("sw"), a("lcur")))
+    cp(a("ls0"), a("gc", 0, 64))
+    look_up(1)
 
-    def startup_3():
-        ms(a("hw", 13312, 16384), 0.0)
-        dmas("d8", [("Y", a("hw", rows=slice(0, 128, 16)), a("hhi")), ("Y", a("hw", rows=slice(1, 128, 16)), a("hlo"))])
-        ts(a("b15"), a("rg"), 0.0, OP.is_ge, ek(15), OP.mult)
-        ms(a("mend"), 1.0)
-        ms(a("mend", 47, 384, 48), 0.0)
-        ms(a("cc", 0, 1), 0.0)
-        ts(a("szb"), a("r143"), 0.0, OP.is_equal, pcol("lo8"), OP.mult)
-        ts(a("b1"), a("rg"), pcol("c"), OP.is_equal, pcol("lo8"), OP.mult)
-        ts(a("b2"), a("rg"), -8.0, OP.add, pcol("c"), OP.is_equal)
-        ts(pcol("zm"), pcol("hi8"), -384.0, OP.mult, -192.5, OP.add)
-        tt(a("bq"), a("b1"), a("b2"), OP.add)
-
-    def startup_4():
-        iota(a("ones"), [[0, 768]], 1, 0)
-        iota(a("pt", 4096, 4352), [[0, 256]], 0, 0)
-        iota(a("m16"), [[0, 408]], -16, 0)
-        iota(a("cs"), [[0, 416]], 0, 0)
-        iota(a("ds"), [[0, 416]], 100, 0)
-        ts(a("sh"), a("r143"), 0.0, OP.is_equal, pcol("h01"), OP.mult)
-        ts(pcol("q0"), ek(0), 0.25, OP.mult)
-        ts(pcol("q4"), ek(4), 0.25, OP.mult)
-        ts(a("srh"), a("r143"), 0.0, OP.is_equal, ek(0), OP.mult)
-        ts(a("sq0"), a("r143"), 0.0, OP.is_equal, pcol("q0"), OP.mult)
-        ts(a("sq4"), a("r143"), 0.0, OP.is_equal, pcol("q4"), OP.mult)
-
-    def startup_5():
-        ts(pcol("w4"), ek(0), 4.0, OP.mult)
-        tt(pcol("u1"), c_, c4, OP.add)
-        ts(a("sw4"), a("r143"), 0.0, OP.is_equal, pcol("w4"), OP.mult)
-        ts(a("s2"), a("r143"), 0.0, OP.is_equal, 2.0, OP.mult)
-        ts(a("s1"), a("r143"), 0.0, OP.is_equal)
-        ts(a("sd"), a("r143"), 0.0, OP.is_equal, 1.0 / BIG, OP.mult)
-        ts(a("bon"), a("rg"), 0.0, OP.is_ge, -1.0, OP.mult)
-        ts(a("bop"), a("rg"), 0.0, OP.is_ge)
-        ts(pcol("u2"), c4, -2.0, OP.mult, pcol("u1"), OP.add)
-        ts(a("rfrac"), a("xf"), 1.0 / 512, OP.mult)
-        ts(pcol("u2"), pcol("u2"), pcol("c"), OP.add)
-        ts(a("base2"), a("xf", 0, 16), 32.0, OP.mult, pcol("u2"), OP.add)
-        ms(a("negb"), -BIG)
-        ts(pcol("lo512"), pcol("lo8"), 512.0, OP.mult)
-        ts(pcol("hi512"), pcol("hi8"), 512.0, OP.mult)
-        ms(a("x0", 7, 8), -BIG)
-        ms(a("x1", 7, 8), -BIG)
-
-
-    def positions(parts):
-        for k in parts:
-            py = a("py%d" % (k % 2))
-            for lo in (0, 512):
-                mm(a("py%d" % (k % 2), lo, lo + 512), a("idb"), a("ow", 2048 + 1024 * k + lo, 2560 + 1024 * k + lo), True, True)
-            tt(a("pt", 1024 * k, 1024 * k + 1024), a("pos_r", 1024 * k, 1024 * k + 1024), py, OP.subtract)
-
-    def absent():
-        act(a("hw", 8192, 10240), a("hw", 0, 2048))
-        ts(a("idu"), a("xf"), 16.0, OP.mult, pcol("c"), OP.add)
-        for k in range(4):
-            act(a("ow", 2048 + 1024 * k, 3072 + 1024 * k), ind(a("pos_r"), a("idu", 64 * k, 64 * k + 64)), AF.Relu, bias=BIG, scale=-BIG)
-
-    def nothing():
-        return None
-
-    def requests(r, gap1, gap1b, gap2, gap3, gap4, gap5, gap6):
-        w = "w%d" % (r % 2)
+    def requests(r):
         if r > 0:
-            cp(a("g2"), ind(a("g2c"), a("lu", 0, 32)))
-            act(a("d0"), ind(a("g2c"), a("lu", 0, 32)), AF.Relu, bias=1.0, scale=pcol("nh8"))
+            cp(a("g2"), ind(a("g2c"), a("lu")))
+            act(a("d0"), ind(a("g2c"), a("lu")), AF.Relu, bias=1.0, scale=pcol("nh8"))
         else:
-            tt(a("g2"), ind(a("tab"), a("l3", 0, 32)), a("mq"), OP.mult)
+            tt(a("g2"), ind(a("tab"), a("l3", 0, 32)), a("msk", 0, 512), OP.mult)
             act(a("d0"), a("g2"), AF.Relu, bias=1.0, scale=pcol("nh8"))
-        act(a("pcc"), a("g2"), AF.Sign)
-        gap1()
-        scan(a("ss", 1, 513), a("d0"), a("g2"), pcol("lo8"), OP.mult, OP.add)
-        hv = (a("py0", 0, 256), a("py0", 512, 768))
-        lv = (a("py1", 0, 256), a("py1", 512, 768))
-        mm(hv[0], a("bdp"), a("ss", 1, 257), True, False)
-        mm(hv[0], a("bdm"), a("ss", 0, 256), False, True)
-        tt(a("xm"), a("pcc"), a("ss", 0, 512), OP.mult)
-        w2l(a("pcc", 0, 32), "sz", "xm", 0, 512)
-        mm(hv[1], a("bdp"), a("ss", 257, 513), True, False)
-        mm(hv[1], a("bdm"), a("ss", 256, 512), False, True)
+        act(a("p6"), a("g2"), AF.Sign)
+        scan(a("ss", 1, 513), a("d0"), a("g2"), a("ss", 0, 1), OP.mult, OP.add)
+        tt(a("xm"), a("p6"), a("ss", 0, 512), OP.mult)
+        w2l(a("p7", 0, 32), "sz", "xm", 0, 512)
+        for h in range(2):
+            o, lo = a("p%d" % (4 + h), 0, 256), 256 * h
+            mm(o, a("bc"), a("ones", 0, 256), True, False)
+            mm(o, a("bdp"), a("ss", lo + 1, lo + 257), False, False)
+            mm(o, a("bdm"), a("ss", lo, lo + 256), False, True)
+            act(a("hh", lo, lo + 256), o, bias=pcol("hb"), scale=pcol("hs"))
+            tt(a("val", lo, lo + 256), o, a("hh", lo, lo + 256), OP.add)
+        ts(a("zf"), a("p7", 0, 32), 0.0, OP.is_ge, 8192.0, OP.mult)
+        tt(a("zt"), a("p7", 0, 32), a("sel"), OP.add)
+        ts(a("sh_"), a("p7", 0, 32), -384.0, OP.is_ge, 384.0, OP.mult)
+        tt(a("zu"), a("zt"), a("zf"), OP.add)
+        tt(a("zo"), a("zu"), a("top"), OP.min)
+        cp(a("offu"), a("zo"))
+        cp(ind(a("w"), a("offu")), a("val"))
+
+    def addresses(r, b):
+        lo, hi = ADDR[b]
+        n = 48 * (hi - lo)
+        o = a("p%d" % b, 0, n)
+        mm(o, a("idb"), a("iotab", 0, n), True, False)
+        for k in range(16):
+            mm(o, a("tri", 128 * k, 128 * k + 128), a("w", 768 * lo + k, 768 * hi, 16), False, k == 15)
+        scan(a("cc", 48 * lo + 1, 48 * hi + 1), o, a("mend", 0, n), 0.0, OP.add, OP.mult)
+        base, near = a("p%d" % (4 + b), 0, n), a("near", 48 * lo, 48 * hi)
+        mm(base, a("b15"), a("cc", 48 * lo, 48 * hi), True, True)
+        act(near, o)
+        tt(near, base, near, OP.add)
+        ts(a("as%d" % r, 48 * lo, 48 * hi), near, 16383.0, OP.min)
+        send([((rank + n) % N, a("as%d" % r, 48 * n, 48 * n + 48), a("al%d" % r, 48 * n, 48 * n + 48), "aa%d" % n)
+              for n in range(max(lo, 1), hi)])
+
+    def firsts(last):
+        w2l(a("p2", 0, 384), "sf", "w", 0, 6144)
+        act(a("fl"), a("p2", 0, 384))
+        for k in range(16):
+            n = 384 if k % 2 else 408
+            mm(a("p3", 0, n), sel("sk", k), a("w", 384 * k, 384 * k + n), k == 0, k == 15)
+        act(a("keep"), a("p3", 0, 408), AF.Relu, bias=1.0, scale=-1.0)
+        if not last:
+            dmas("clr", [(a("w", 0, 6144, rows=row(x)), a("hw", 0, 6144, rows=row(3 + x))) for x in range(3)])
+
+    def segments():
         act(a("g2b"), a("g2"))
-        gap1b()
-        gap2()
-        act(a("hh", 0, 256), hv[0], bias=pcol("bb0"), scale=pcol("beta"))
-        act(lv[0], hv[0], bias=pcol("gam"), scale=ek(1))
-        ts(a("zc"), a("pcc", 0, 32), 1.0, OP.max, 768.0, OP.min)
-        tt(a("zv"), a("pcc", 0, 32), a("zc"), OP.is_equal)
-        tt(a("zd"), a("zc"), a("sel", 64, 96), OP.add)
-        tt(a("val", 0, 256), lv[0], a("hh", 0, 256), OP.add)
-        tt(a("ze"), a("zd"), a("zv"), OP.mult)
-        gap3()
-        act(a("hh", 256, 512), hv[1], bias=pcol("bb0"), scale=pcol("beta"))
-        act(lv[1], hv[1], bias=pcol("gam"), scale=ek(1))
-        tt(a("ze"), a("ze"), a("ridx"), OP.max)
-        cp(a("offu"), a("ze"))
-        tt(a("val", 256, 512), lv[1], a("hh", 256, 512), OP.add)
-        gap4()
-        mm(a("pa", 0, 384), a("idb"), a("iotab"), True, False)
-        cp(ind(a(w), a("offu")), a("val"))
-        for k in range(16):
-            mm(a("pa", 0, 384), a("tri", 128 * k, 128 * k + 128), a(w, 512 + k, 6656, 16), False, k == 15)
-            if k == 3:
-                gap5()
-        scan(a("cc", 1, 385), a("pa", 0, 384), a("mend"), 0.0, OP.add, OP.mult)
-        mm(a("pcc", 0, 384), a("b15"), a("cc", 0, 384), True, True)
-        cp(a("p1s"), a("pa", 0, 384))
-        gap6()
-        tt(a("p1s"), a("pcc", 0, 384), a("p1s"), OP.add)
-        ts(a("as%d" % r), a("p1s"), 16383.0, OP.min)
-        send([(d, a("as%d" % r, 48 * d, 48 * d + 48), a("al%d" % r, 48 * rank, 48 * rank + 48), "aa%d" % rank) for d in others], 2)
-        for d in others:
-            landed("aa%d" % d, 2, a("al%d" % r, 48 * d, 48 * d + 48))
+        w2l(a("p7", 0, 32), "szb", "g2b", 0, 512)
+        tt(a("se"), a("p7", 0, 32), a("zt"), OP.add)
+        tt(a("sl"), a("sel"), a("zf"), OP.subtract)
+        tt(a("sr"), a("sel"), a("sh_"), OP.add)
+        tt(a("se"), a("se"), a("sl"), OP.min)
+        ts(a("rho"), a("sr"), -768.0, OP.add, 1.0 / 128, OP.mult)
+        tt(a("sq"), a("se"), a("sr"), OP.subtract)
+        ts(a("leu"), a("sq"), 768.0, OP.add, 0.0, OP.max)
+        act(a("mc"), ind(a("ek3"), a("rho")))
 
-    def segments_a(r):
-        w2l(a("pd", 0, 32), "szb", "g2b", 0, 512)
-        mm(a("pcc"), a("bq"), a("xm"), True, True)
+    def answer(r, b):
+        lo, hi = BACK[b]
+        for n in range(lo, hi):
+            lst = a(("al%d" if n else "as%d") % r, 48 * n, 48 * n + 48)
+            (act if OWN[n] == "S" else cp)(a("ow", 768 * n, 768 * n + 768), ind(a("hw"), lst))
+        o = a("p%d" % (4 + b % 3), 0, 48 * (hi - lo))
+        w2l(o, "sh", "ow", 768 * lo, 768 * hi)
+        ts(a(("rs%d" if lo else "rl%d") % r, 48 * lo, 48 * hi), o, 1.0, OP.add)
+        if lo:
+            send([((rank - n) % N, a("rs%d" % r, 48 * n, 48 * n + 48), a("rl%d" % r, 48 * n, 48 * n + 48), "ra%d" % n)
+                  for n in range(lo, hi)])
 
-    def segments_s(r):
-        act(a("uu"), a("pcc"), AF.Abs, bias=pcol("zm"))
-        act(a("uu"), a("uu"), AF.Relu, bias=192.5, scale=-1.0)
-        act(a("mc%d" % (r % 2)), a("uu"), AF.Sign)
+    def phrases(r, b):
+        lo, hi = BACK[b]
+        ts(a("rw", 8 + 48 * lo, 8 + 48 * hi), a("rl%d" % r, 48 * lo, 48 * hi), -2048.0, OP.add)
+        mm(a("p2", 48 * lo, 48 * hi), a("idb"), a("fl", 48 * lo, 48 * hi), True, False)
+        mm(a("p2", 48 * lo, 48 * hi), a("idf"), a("rw", 8 + 48 * lo, 8 + 48 * hi), False, True)
+        ts(a("lx", 48 * lo, 48 * hi), a("p2", 48 * lo, 48 * hi), 2048.0, OP.add, 0.0, OP.max)
+        for n in range(lo, hi):
+            s = str(n % DEEP)
+            act(a("y" + s, 8, 776), ind(a("pt"), a("rl%d" % r, 48 * n, 48 * n + 48)), AF.Abs, bias=1.0)
+            tt(a("ct" + s), ind(a("pt"), a("lx", 48 * n, 48 * n + 48)), a("y" + s, 7, 775), OP.is_equal)
+            if PRESENT[n] == "S":
+                act(a("pr" + s), a("y" + s, 8, 776), AF.Sign, bias=-0.25)
+            else:
+                ts(a("pr" + s), a("y" + s, 8, 776), 0.5, OP.is_gt)
+            scan(a("rr" + s), a("ct" + s), a("ct" + s), 0.0, OP.mult, OP.add)
+            for f_, src, p in (("s1", "ct", "p1"), ("s1", "pr", "p0"), ("s2", "rr", "p0")):
+                for h in range(2):
+                    first = n == 0 and h == 0 and src != "rr"
+                    last = n == N - 1 and h == 1 and src != "pr"
+                    mm(a(p, 0, 384 if h else 408), sel(f_, 2 * n + h), a(src + s, 384 * h, 768 if h else 408), first, last)
 
-    def segments_b(r):
-        s = str(r % 2)
-        ts(a("ua"), a("zc"), -1.0, OP.mult, 769.0, OP.add)
-        ts(a("ub"), a("zc"), 384.0, OP.is_gt, 384.0, OP.mult)
-        tt(a("ua"), a("pd", 0, 32), a("ua"), OP.min)
-        tt(a("ub"), a("zc"), a("ub"), OP.subtract)
-        tt(a("kv" + s), a("ua"), a("zv"), OP.mult)
-        tt(a("ep" + s), a("ua"), a("zd"), OP.add)
-        ts(a("lsu" + s), a("ub"), -1.0, OP.add)
-        tt(a("ua"), a("ub"), a("ua"), OP.add)
-        ts(a("leu" + s), a("ua"), -1.0, OP.add)
-
-    def own_gather(r, n, e):
-        d = order[n]
-        lst = a(("as%d" if d == rank else "al%d") % r, 48 * d, 48 * d + 48)
-        o = a("ow", 768 * n, 768 * n + 768)
-        if e == "S":
-            act(o, ind(a("hw"), lst))
-        else:
-            cp(o, ind(a("hw"), lst))
-
-    def own_extract(r, pr):
-        w2l(a("pa" if pr % 2 == 0 else "pcc", 0, 96), "sh", "ow", 1536 * pr, 1536 * pr + 1536)
-
-    def own_evac(r, pr):
-        p = "pa" if pr % 2 == 0 else "pcc"
-        if pr == 0:
-            cp(a("rl%d" % r, 48 * rank, 48 * rank + 48), a(p, 0, 48))
-            cp(a("rs%d" % r, 48, 96), a(p, 48, 96))
-        else:
-            cp(a("rs%d" % r, 96 * pr, 96 * pr + 96), a(p, 0, 96))
-
-    def own_send(r, ns):
-        send([(order[n], a("rs%d" % r, 48 * n, 48 * n + 48), a("rl%d" % r, 48 * rank, 48 * rank + 48), "ra%d" % rank) for n in ns], 4)
-
-    def candidates_a():
-        for k in range(16):
-            mm(a("py0", 0, 8), sel("sq4" if k % 2 else "sq0", k), a("skh", k // 2, 64, 8), k == 0, k == 15)
-
-    def candidates_b(last):
-        cp(a("l2", 0, 8), a("py0", 0, 8))
-        cp(a("wc"), ind(a("nxtw"), a("l2", 0, 8)))
+    def totals(r, last):
+        scan(a("cs", 1, 409), a("keep"), a("p0", 0, 408), 0.0, OP.mult, OP.add)
+        tt(a("ge"), ind(a("cs", 0, 409), a("leu")), a("mc"), OP.mult)
+        for k in range(8):
+            mm(a("p3", 0, 64), a("bop" if k >= 4 else "bon"), a("ge", k, 512, 8), k == 0, k == 7)
+        ts(a("wa"), a("p3", 0, 64, 2), 0.0, OP.is_gt, pcol("lo512"), OP.mult)
+        ts(a("wb"), a("p3", 1, 64, 2), 0.0, OP.is_gt, pcol("hi512"), OP.mult)
+        ts(a("winr"), a("p3", 0, 64), 0.0, OP.is_gt)
+        tt(a("ab"), a("wa"), a("wb"), OP.add)
         if not last:
-            w2l(a("py0", 0, 8), "srh", "wc", 0, 128)
+            tt(a("wl"), a("ab"), a("ridx"), OP.add)
+            cp(a("lu"), a("wl"))
+            tt(a("wc"), a("ab"), a("cd"), OP.mult)
+            tt(a("sel"), a("wc"), a("pq", 0, 32), OP.add)
+        for k in range(4):
+            mm(a("p0", 0, 128), a("bop"), a("ge", k, 512, 4), k == 0, k == 3)
+        act(a("ytb", 128 * r, 128 * r + 128), a("p0", 0, 128))
+        tt(a("hd"), a("gc", 1, 128, 2), a("gc", 0, 128, 2), OP.subtract)
+        tt(a("hd2"), a("hd"), a("winr"), OP.mult)
+        tt(a("ywb", 64 * r, 64 * r + 64), a("hd2"), a("gc", 0, 128, 2), OP.add)
 
-    def candidates_d():
-        senses([(a("sk"), 0, 128)], 128, a("py0", 0, 8))
-        for x in range(2):
-            blend(a("cb", 96 * x, 96 * x + 32), a("sk", x, 128, 4), a("sk", 2 + x, 128, 4), "wu"[x])
-        for x in range(2):
-            cp(a("l2", 32 * x, 32 * x + 32), a("cb", 96 * x, 96 * x + 32))
+    def barrier_places():
+        act(a("nh"), a("p1", 0, 408), AF.Relu, bias=73728.0, scale=-8192.0)
+        scan(a("ds", 1, 409), a("ones"), a("nh"), 16384.0, OP.add, OP.min)
+        tt(a("dg"), ind(a("ds", 0, 409), a("leu")), a("mc"), OP.mult)
+        w2l(a("p2", 0, 32), "s1", "dg", 0, 512)
+        tt(a("ba"), a("se"), a("p2", 0, 32), OP.subtract)
+        tt(a("bd"), a("ba"), a("zt"), OP.is_gt)
+        tt(a("ba"), a("ba"), a("bd"), OP.mult)
 
-    def wide(r, lead):
-        w = "w%d" % (r % 2)
-        qs = [(rank - n) % N for n in range(N)]
-
-        def s_part(n):
-            q, s = qs[n], str(n % 2)
-            act(a("x" + s, 8, 776), ind(a("pt"), a("rl%d" % r, 48 * q, 48 * q + 48)))
-            act(a("py" + s, 0, 768), a("x" + s, 7, 775), AF.Relu, bias=1.0)
-
-        def p_part(n):
-            for h, p in enumerate(("pcc", "pd")):
-                lo = 512 + 768 * qs[n] + 384 * h
-                mm(a(p, 0, 384), a("idb"), a(w, lo, lo + 384), True, True)
-
-        s_part(0)
-        lead()
-        p_part(0)
-        for n in range(N):
-            q, s = qs[n], str(n % 2)
-            if n + 1 < N:
-                s_part(n + 1)
-            tt(a("dd" + s), a("x" + s, 8, 776), a("py" + s, 0, 768), OP.subtract)
-            for h, p in enumerate(("pcc", "pd")):
-                tt(a("ct" + s, 384 * h, 384 * h + 384), a("dd" + s, 384 * h, 384 * h + 384), a(p, 0, 384), OP.is_equal)
-            if n + 1 < N:
-                p_part(n + 1)
-            scan(a("rr" + s), a("ct" + s), a("ones"), 0.0, OP.mult, OP.add)
-            pieces = ((0, 0, 408), (1, 384, 768))
-            for fam, src, p in (("sd", "dd", "pa"), ("s1", "ct", "pb"), ("s2", "rr", "pa")):
-                for h, lo, hi in pieces:
-                    first = n == 0 and h == 0 and fam != "s2"
-                    last = n == N - 1 and h == 1 and fam != "sd"
-                    mm(a(p, 0, hi - lo), sel(fam, q + 8 * h), a(src + s, lo, hi), first, last, inc=(h == 1 and fam != "sd"))
-
-    def hot(r):
-        s = str(r % 2)
-        scan(a("ds", 1, 409), a("ones", 0, 408), a("nh"), 100.0, OP.add, OP.min)
-        tt(a("dg"), ind(a("ds"), a("leu" + s)), a("mc" + s), OP.mult)
-        w2l(a("pd", 0, 32), "s1", "dg", 0, 512)
-
-    def winners_list(r):
-        for k in range(16):
-            mm(a("py1", 0, 16), sel("sw4", k), a("winw", 64 * r + k // 4, 64 * r + 64, 4), k == 0, k == 15)
-
-    def winners_list_b():
-        tt(a("keyl", 0, 16), a("py1", 0, 16), a("base2"), OP.add)
-        cp(a("wiu"), a("keyl", 0, 16))
-
-    def totals(r):
-        s = str(r % 2)
-        last = r + 1 == RO
-        if not last:
-            both_senses_s()
-        act(a("nh"), a("pb", 0, 408), AF.Relu, bias=900.0, scale=-100.0)
-        if not last:
-            both_senses_v()
-        else:
-            ts(a("rw"), a("rl%d" % r), 1.0, OP.add)
-            hot(r)
-        scan(a("cs", 1, 409), a("pa", 0, 408), a("m16"), 0.0, OP.add, OP.add)
+    def barrier_words(r, last):
+        ts(a("wm"), a("ab"), pcol("a1"), OP.mult, pcol("a0"), OP.add)
+        tt(a("bb"), a("ba"), a("wm"), OP.mult)
+        for p in range(2):
+            mm(a("p2", 64, 80), sel("wsf", 8 * p), a("bb", p, 32, 2), p == 0, p == 1)
+        ts(a("m1"), a("p2", 64, 80), 127.0, OP.add)
+        ts(a("m2", 0, 16), a("m1"), 4, OP.logical_shift_right)
+        ts(a("m2", 16, 32), a("m1"), 15, OP.bitwise_and)
+        cp(a("cl"), a("m2"))
+        act(a("mk"), ind(a("ek"), a("cl", 16, 32)))
+        tt(a("bw"), ind(a("rw"), a("cl", 0, 16)), a("mk"), OP.mult)
+        mm(a("p1", 0, 256), a("boh"), a("bw"), True, True)
+        act(a("ybb", 256 * r, 256 * r + 256), a("p1", 0, 256), bias=2047.0)
         if last:
-            barrier_b(r)
-            barrier_c1(r)
-        tt(a("ge"), ind(a("cs"), a("leu" + s)), a("mc" + s), OP.mult)
-        for k in range(4):
-            mm(a("pcc", 0, 128), a("bop"), a("ge", k, 512, 4), k == 0, False)
-        tt(a("uu"), ind(a("cs"), a("lsu" + s)), a("mc" + s), OP.mult)
-        for k in range(4):
-            mm(a("pcc", 0, 128), a("bon"), a("uu", k, 512, 4), False, k == 3)
-        if not last:
-            hot(r)
-        else:
-            barrier_c2(r)
-            barrier_c3(r)
-            barrier_c4(r)
-        y0 = 128 * r
-        cp(a("ytb", y0, y0 + 128), a("pcc", 0, 128))
-        tt(a("winw", 64 * r, 64 * r + 64), a("ytb", y0 + 1, y0 + 128, 2), a("ytb", y0, y0 + 128, 2), OP.is_gt)
-
-    def choose(r):
-        ts(a("wa"), a("winw", 64 * r, 64 * r + 64, 2), pcol("lo512"), OP.mult)
-        ts(a("wb"), a("winw", 64 * r + 1, 64 * r + 64, 2), pcol("hi512"), OP.mult)
-        tt(a("wa"), a("wa"), a("ridx"), OP.add)
-        tt(a("winl"), a("wa"), a("wb"), OP.add)
-        cp(a("lu", 0, 32), a("winl"))
-        winners_list(r)
-
-    def window_base(r):
-        ts(a("wa"), a("winl"), 512.0, OP.is_ge)
-        tt(a("wa"), a("wa"), a("cd", 0, 32), OP.mult)
-        tt(a("sel", 64, 96), a("wa"), a("pq", 0, 32), OP.add)
-
-    def both_senses_s():
-        act(a("rqw"), a("rqw"), AF.Abs, bias=pcol("qb"))
-        act(a("rqw"), a("rqw"), AF.Relu, bias=float(2 ** 24), scale=-32768.0)
-
-    def both_senses_v():
-        tt(a("g2c"), ind(a("tab"), a("l3")), a("rqw"), OP.min)
-
-    def heads(r):
-        win = a("winw", 64 * r, 64 * r + 64)
-        jobs = [(a("ywb", 64 * r, 64 * r + 64), "wc", "f3")] + ([(a("skh"), "sk", "f4")] if r + 1 < RO else [])
-        for o, src, t in jobs:
-            tt(a(t, 0, 64), a(src, 1, 128, 2), a(src, 0, 128, 2), OP.subtract)
-        for o, src, t in jobs:
-            tt(a(t, 0, 64), a(t, 0, 64), win, OP.mult)
-        for o, src, t in jobs:
-            tt(o, a(t, 0, 64), a(src, 0, 128, 2), OP.add)
-
-    def barrier_b(r):
-        s = str(r % 2)
-        ts(a("va"), a("pd", 0, 32), 24.0, OP.min, 513.0, OP.add)
-        tt(a("vb"), a("pd", 0, 32), a("kv" + s), OP.is_ge)
-        tt(a("va"), a("ep" + s), a("va"), OP.subtract)
-        ts(a("vb"), a("vb"), 99.0, OP.mult)
-        ts(a("m1"), a("va"), 0.0, OP.max)
-        ts(a("m2"), a("m1"), 15, OP.bitwise_and)
-        ts(a("m3"), a("m1"), 4, OP.logical_shift_right)
-        tt(a("lowh"), a("m2"), a("vb"), OP.add)
-        cp(a("colu"), a("m3"))
-
-    def barrier_c1(r):
-        for k in range(16):
-            mm(a("pb", k, 512, 16), a("rs", 128 * k, 128 * k + 128), a("lowh"), True, True, inc=(k == 15))
-
-    def barrier_c2(r):
-        if r + 1 < RO:
-            act(a("bd"), a("pb"), AF.Abs, bias=pcol("nc"))
-            act(a("bd"), a("bd"), AF.Relu, bias=1.0, scale=-1.0)
-        else:
-            ts(a("bd"), a("pb"), pcol("c"), OP.is_equal)
-
-    def barrier_c3(r):
-        tt(a("bw"), ind(a("rw"), a("colu")), a("bd"), OP.mult)
-
-    def barrier_c4(r):
-        mm(a("pb"), a("bop"), a("bw"), True, True)
-
-    def barrier_d(r):
-        act(a("bd"), a("pb"), bias=-1.0)
-        if r + 1 < RO:
-            ts(a("b16"), ind(a("bd"), a("wiu")), -2047.0, OP.add)
-            w2l(a("pb", 0, 16), "srh", "b16", 0, 256)
-            tt(a("keyw"), a("b16"), a("rfrac"), OP.add)
-            act(a("ybb", 256 * r, 256 * r + 256), ind(a("bd"), a("wiu")))
-            ts(a("va", 0, 16), a("ridx", 0, 16), -1.0 / 512, OP.mult, -1.0 / 1024, OP.add)
-            ts(a("vb", 0, 16), a("ridx", 0, 16), 4096.0, OP.add)
-        else:
-            cp(a("ybb", 256 * r, 256 * r + 256), ind(a("bd"), a("wiu")))
-
-    def barrier_e(r, lo, hi):
-        if lo == 0:
-            tt(a("keyl", 0, 16), a("va", 0, 16), a("pb", 0, 16), OP.subtract)
-            ts(a("vb", 16, 32), a("pb", 0, 16), 2047.0, OP.add)
-            ts(a("keyl", 16, 32), a("pb", 0, 16), -1.0, OP.mult, -255.5 / 512, OP.add)
-            at = [768]
-            for i in range(16):
-                for x in range(2):
-                    o, k_, b_ = a("mn", 16 * x + i, 16 * x + i + 1), a("keyw", 16 * i, 256), a("keyl", 16 * x + i, 16 * x + i + 1)
-                    z = a("ow", at[0], at[0] + 256 - 16 * i)
-                    at[0] += 256 - 16 * i
-                    before("S", [], [z])
-                    op("S", o, [k_, b_], lambda: g.scalar.activation(z[0], k_[0], AF.Sign, bias=b_[0], accum_out=o[0]))
-                    after(("S", cnt["S"]), [], [z])
-        if hi == 16:
-            ts(a("va", 16, 32), a("vb", 16, 32), 0.0, OP.is_ge)
-            tt(a("vb", 16, 32), a("vb", 16, 32), a("vb", 0, 16), OP.subtract)
-            tt(a("va", 16, 32), a("va", 16, 32), a("vb", 16, 32), OP.mult)
-            tt(a("mn", 0, 16), a("mn", 0, 16), a("mn", 16, 32), OP.is_equal)
-            tt(a("va", 0, 16), a("va", 16, 32), a("mn", 0, 16), OP.mult)
-            tt(a("va", 0, 16), a("va", 0, 16), a("vb", 0, 16), OP.add)
-            cp(a("bu"), a("va", 0, 16))
-            cp(ind(a("pt"), a("bu")), a("negb"))
-
-    def next_table():
-        for k in range(16):
-            mm(a("py0", 64 * k, 64 * k + 64), a("rs", 128 * k, 128 * k + 128), a("hn"), True, True)
-        act(a("nxtw"), a("py0"))
-
-    OWN = ("SSSSVSVS", "SSVSVVVS", "SSVSVSVS")
-
-    def seq(*fs):
-        def run():
-            for f in fs:
-                f()
-        return run
+            return
+        mm(a("p3", 0, 256), a("boh"), a("rfr"), True, False)
+        mm(a("p3", 0, 256), a("boh"), a("bw"), False, True)
+        act(a("keyw"), a("p3", 0, 256))
+        w2l(a("p2", 0, 16), "sm", "bw", 0, 256)
+        tt(a("keyl", 0, 16), a("p2", 0, 16), a("nfr"), OP.add)
+        ts(a("keyl", 16, 32), a("p2", 0, 16), -255.5 / 512, OP.add)
+        tt(a("bu_"), a("cd2"), a("p2", 0, 16), OP.subtract)
+        for i in range(16):
+            for x in range(2):
+                at = 512 * i - 16 * i * (i - 1) + x * (256 - 16 * i)
+                act(a("junk", at, at + 256 - 16 * i), a("keyw", 16 * i, 256), AF.Sign,
+                    bias=a("keyl", 16 * x + i, 16 * x + i + 1), total=a("mn", 16 * x + i, 16 * x + i + 1))
+        tt(a("bv"), a("mn", 0, 16), a("mn", 16, 32), OP.is_equal)
+        tt(a("bv"), a("bv"), a("bu_"), OP.mult)
+        tt(a("bv"), a("bv"), a("top2"), OP.add)
+        cp(a("bu"), a("bv"))
+        cp(ind(a("pt"), a("bu")), a("gone"))
 
     for r in range(RO):
-        p = r - 1
         last = r + 1 == RO
-        if r == 0:
-            requests(r, startup_1, nothing, startup_2, nothing, absent, seq(next_table, startup_3), nothing)
-        else:
-            requests(r, seq(lambda: barrier_b(p), lambda: barrier_c1(p)),
-                     seq(lambda: window_base(r), winners_list_b, lambda: barrier_c2(p)),
-                     lambda: ts(a("rw"), a("rl%d" % p), 1.0, OP.add),
-                     seq(lambda: barrier_c3(p), lambda: barrier_c4(p), lambda: segments_a(r)),
-                     nothing,
-                     seq(lambda: barrier_d(p), lambda: segments_s(r), lambda: barrier_e(p, 0, 0), lambda: heads(p), lambda: segments_b(r)),
-                     nothing)
-        eng = OWN[r]
-        own_gather(r, 0, eng[0])
-        if r == 0:
-            startup_4()
-            segments_a(r)
-            segments_s(r)
-            own_gather(r, 1, eng[1])
-            positions([0, 1, 2, 3])
-            own_gather(r, 2, eng[2])
-            own_gather(r, 3, eng[3])
-        candidates_a()
-        candidates_b(last)
-        if r > 0:
-            own_gather(r, 1, eng[1])
-        own_extract(r, 0)
+        requests(r)
+        for b in range(len(ADDR)):
+            addresses(r, b)
+        segments()
+        next_senses("ls0" if r == 0 else "ywb", 0 if r == 0 else 64 * (r - 1))
+        firsts(last)
+        for b in range(len(BACK)):
+            answer(r, b)
         if not last:
-            candidates_d()
-        if r > 0:
-            own_gather(r, 2, eng[2])
-            own_gather(r, 3, eng[3])
-        own_extract(r, 1)
-        own_evac(r, 0)
-        if r > 0:
-            barrier_e(p, 16, 16)
-        own_evac(r, 1)
-        own_send(r, [1, 2, 3])
-        if r == 0:
-            segments_b(r)
-            startup_5()
-        own_gather(r, 4, eng[4])
-        own_gather(r, 5, eng[5])
-        if not last:
-            lists_a(2)
-        own_extract(r, 2)
-        own_gather(r, 6, eng[6])
-        own_gather(r, 7, eng[7])
-        own_extract(r, 3)
-        own_evac(r, 2)
-        own_evac(r, 3)
-        own_send(r, [4, 5, 6, 7])
-        for d in others:
-            landed("ra%d" % d, 4, a("rl%d" % r, 48 * d, 48 * d + 48))
-        if not last:
-            iota(a("w%d" % ((r + 1) % 2), 0 if r == 0 else 512, 6656), [[0, 6656 if r == 0 else 6144]], 0, 0)
-        wide(r, nothing if last else (lambda: lists_b(2)))
-        totals(r)
-        if not last:
-            choose(r)
-    r = RO - 1
-    rows = slice(0, 128, 16)
-    winners_list(r)
-    heads(r)
-    dmas("dout", [("Y", T.yt[:], a("ytb", rows=rows)), ("Y", T.yw[:], a("ywb", rows=rows))])
-    winners_list_b()
-    barrier_d(r)
-    dmas("d9", [("Y", T.yb[:], a("ybb", rows=rows))])
+            look_up(2)
+        for b in range(len(BACK)):
+            phrases(r, b)
+        barrier_places()
+        totals(r, last)
+        barrier_words(r, last)
+    dmas("d10", [(T.yt[:], a("ytb", rows=row(0))), (T.yw[:], a("ywb", rows=row(4)))])
+    dmas("d11", [(T.yb[:], a("ybb", rows=row(0)))])
+    issue_all()
     for e in cnt:
         need("G", (e, cnt[e]))
     for s in sorted(tot):
         need("G", (s, tot[s]))
+
+
+HW_V, POS_V = 10, 0

@@ -4,15 +4,19 @@ from concourse.mybir import AluOpType as OP, AxisListType, ActivationFunctionTyp
 F, B, H, I, U = "float32", "bfloat16", "float16", "int32", "uint16"
 RO = 3
 CUT = 49152.0
-ADDR = ((0, 3), (3, 8))
+ADDR = ((0, 4), (4, 8))
 BACK = ((0, 1), (1, 3), (3, 5), (5, 8))
-OWN = "VVSVSSVS"
-PRESENT = "VSVSSVSS"
+EARLY = 1
 DEEP = 2
 CYCLE = {"V": 0.00083, "S": 0.00083, "G": 0.00083, "P": 0.00042}
 FIXED = {"V": 0.05, "S": 0.065, "G": 0.13, "P": 0.0}
 GATHER, SCATTER = 1.56, 3.8
-WAKE, DMA_LATE, DMA_RATE, SEND, SEND_LATE, FIRST = 0.09, 1.5, 250e3, 0.6, 1.8, 3.0
+WAKE, DMA_LATE, DMA_RATE, SEND, SEND_LATE, FIRST = 0.16, 1.5, 250e3, 0.6, 1.8, 3.0
+SHY = {"own": 0.0, "present": 0.0, "fill": 0.0, "positions": 0.0, "constant": 1.0, "heap": 1.0, "small": 1.0, "round": 1.0,
+       "out": 1.0, "look": 1.0}
+URGE = {"barred": 3.0, "mask": 8.0, "word": 3.0}
+TRIES = [(look, urge) for look in (0.5, 1.0, 2.0, 4.0) for urge in (0.5, 1.0, 1.5)]
+ORDER = []
 
 
 def _scratch():
@@ -24,24 +28,25 @@ def _scratch():
     sb(I, io_p=4, gst_r=68, gln_r=68, cur_r=4, rel_r=256, sens_r=128, nxt_r=64, heap_r=1024, pos_r=4096,
        tli=704, lnf=528, tab=1024, sw=1024, rp=768, ti=256, sp=256, sx=256, m1=16, m2=32)
     sb(F, pc=40, ek=16, ek8=16, ek3=48, xf=256, bon=128, bop=128, bdp=128, bdm=128, b15=128, idf=128, lsf=144, wsf=144, rqf=144,
-       f1=144, f2=144, f3=144, f4=144, f5=144, f6=144, f7=128, mend=384, ridx=32, top=32, top2=16, cd2=16, nfr=16, gone=256, heapf=1024,
-       pt=4368, tsy=1024, gc=128, msk=1024, g2c=1024, pq=64, cd=32, sel=32,
-       wa=32, wb=32, wc=32, ab=32, wl=32, wm=32, winr=64, hd=64, hd2=64, ls0=64,
+       f1=144, f2=144, f3=144, f4=144, f5=144, f6=144, f7=128, mend=384, ridx=32, top=32, top2=16, gone=256, heapf=1024,
+       pt=4368, tsy=1024, gc=128, msk=1024, g2c=1024, pq=32, pqs=64, cd=32, sel=32,
+       wc=32, wm=32, mid=68,
        g2=512, d0=512, ss=516, zf=32, zt=32, zu=32, zo=32, cc=392, near=384,
        sh_=32, se=32, sl=32, sr=32, sq=32, ba=32, bb=32, bd=32,
-       cs=416, ds=416, keep=408, nh=408, ge=512, mc=512, mk=256,
-       rw=392, keyw=256, keyl=32, mn=32, bu_=16, bv=16, ytb=384, ybb=768, ywb=192)
-    sb(B, iotab=384, idb=128, idn=128, r143=144, rg=128, b1=128, b2=128, b3=128, b4=128, bc=128, s2=144, s1=144, sh=144, szb=144, sf=144,
-       sk=144, sn=144, tri=2048, hhi=1024, hlo=1024, hw=16384, w=6656, relw=4096, rpb=768, rqw=1024,
-       hh=512, val=512, g2b=512, ow=6144, junk=4352, ones=408, fl=384, dg=512)
-    sb(H, sz=144, sm=144, boh=128, rfr=256, xm=512, bw=256)
-    sb(U, tl=704, idu=64, lu=32, l2=64, l3=128, lcur=4, lnx=64, lsy=8, offu=32, leu=32, rho=32, cl=32, bu=16, lx=384)
+       cs=416, ds=416, keep=408, nh=408, ge=512, mc=512, mk=256, rw=392, bv=16, keyw=256, keyl=32, mn=32, bu_=16, cd2=16, nfr=16,
+       ytb=384, ybb=768, ywb=192)
+    sb(B, iotab=384, idb=128, idn=128, r143=144, rg=128, b1=128, b2=128, b3=128, b4=128, bc=128, s2=144, s1=144, sh=144, s34=144,
+       szb=144, sn=144, tri=2048, hhi=1024, hlo=1024, hw=16384, w=6656, rpb=768, rqw=1024,
+       hh=512, val=512, g2b=512, ow=6144, wk=2304 * DEEP, eq=4352, ones=408, dg=512, sg=64, lob=128, hib=128, s32=144, sm=144)
+    sb(H, sz=144, smh=144, boh=128, rfr=256, xm=512, bw=256)
+    sb(U, tl=704, idu=64, lu=32, l2=64, l3=128, lcur=4, lnx=64, lsy=8, hl=4, offu=32, leu=32, rho=32, cl=32, bu=16, lx=384)
     for r in range(RO):
         sb(U, **{"as%d" % r: 384, "al%d" % r: 384, "rs%d" % r: 384, "rl%d" % r: 384})
+    share = {"hhi": ("ow", 0), "hlo": ("ow", 1024), "rpb": ("ow", 2048), "heapf": ("g2c", 0), "eq": ("wk", 0)}
     for k in range(DEEP):
         sb(F, **{"y%d" % k: 776})
         sb(B, **{"ct%d" % k: 768, "rr%d" % k: 768, "pr%d" % k: 768})
-    share = {"hhi": ("junk", 0), "hlo": ("junk", 1024), "rpb": ("junk", 2048), "heapf": ("g2c", 0)}
+        share.update({"ct%d" % k: ("wk", 2304 * k), "rr%d" % k: ("wk", 2304 * k + 768), "pr%d" % k: ("wk", 2304 * k + 1536)})
     place, top, out = {}, {}, {}
     for k, (_w, sh, dt) in s.items():
         if k in share:
@@ -61,8 +66,78 @@ def _scratch():
 
 
 SCRATCH, PLACE = _scratch()
-SEMAPHORES = (["V", "S", "P", "G", "loc", "tarr", "clr"] + ["d%d" % k for k in range(12)] + ["q%d" % k for k in range(4)]
+SEMAPHORES = (["V", "S", "P", "G", "loc", "tarr", "clr"] + ["d%d" % k for k in range(13)] + ["q%d" % k for k in range(4)]
               + ["aa%d" % k for k in range(1, 8)] + ["ra%d" % k for k in range(1, 8)])
+
+
+def order_of_issue(calls):
+    n = len(calls)
+    first, behind = [c[2] for c in calls], [[] for c in calls]
+    for j in range(n):
+        for i in first[j]:
+            behind[i].append(j)
+
+    def gap(i, j):
+        return 0.0 if list(calls[i][0]) == list(calls[j][0]) in (["P"], ["Y"]) else calls[min(i, j)][1]
+
+    def forwards(look, urge):
+        way = [min(c[0].values()) + c[1] for c in calls]
+        for j in range(n - 1, -1, -1):
+            way[j] += urge * calls[j][4]
+            for i in first[j]:
+                way[i] = max(way[i], min(calls[i][0].values()) + gap(i, j) + way[j])
+        left, ready, start, engine = [len(x) for x in first], [0.0] * n, [0.0] * n, [None] * n
+        free, open_ = {}, {e: [] for c in calls for e in c[0]}
+        new = [j for j in range(n) if not left[j]]
+        for _ in range(n):
+            for i in new:
+                for e in calls[i][0]:
+                    open_[e].append(i)
+            mine = dict(open_, V=[i for i in open_["V"] if len(calls[i][0]) == 1
+                                  or free.get("S", 0.0) > max(free.get("V", 0.0), ready[i]) + calls[i][3]])
+            t, e = min((max(free.get(e, 0.0), min(ready[i] for i in l)), e) for e, l in mine.items() if l)
+            now = [i for i in mine[e] if ready[i] <= t]
+            j = max(now, key=lambda i: (way[i], -i))
+            soon = [i for i in mine[e] if t < ready[i] < t + calls[j][0][e] and way[i] > way[j] + look]
+            if soon:
+                j = max(soon, key=lambda i: way[i])
+                j = max([i for i in now if t + calls[i][0][e] <= ready[j]] or [j], key=lambda i: way[i])
+            start[j], engine[j] = max(t, ready[j]), e
+            free[e] = start[j] + calls[j][0][e]
+            for x in calls[j][0]:
+                open_[x].remove(j)
+            new = []
+            for i in behind[j]:
+                ready[i] = max(ready[i], free[e] + gap(j, i))
+                left[i] -= 1
+                if not left[i]:
+                    new.append(i)
+        return start, engine
+
+    def place(order, waits_for, engine, time):
+        start, held = [0.0] * n, {}
+        for j in order:
+            t = max([start[i] + time[i] + gap(i, j) for i in waits_for[j]] + [0.0])
+            slots = held.setdefault(engine[j], [])
+            k = len(slots)
+            while k and slots[k - 1][1] > t:
+                k -= 1
+            while k < len(slots) and slots[k][0] < t + time[j]:
+                t = max(t, slots[k][1])
+                k += 1
+            slots.insert(k, (t, t + time[j]))
+            start[j] = t
+        return start
+    best = None
+    for look, urge in TRIES:
+        start, engine = forwards(look, urge)
+        time = [calls[j][0][engine[j]] for j in range(n)]
+        back = place(sorted(range(n), key=lambda j: (-start[j] - time[j], -j)), behind, engine, time)
+        start = place(sorted(range(n), key=lambda j: (-back[j] - time[j], j)), first, engine, time)
+        end = max(start[j] + time[j] for j in range(n))
+        if best is None or end < best[0]:
+            best = (end, engine, start)
+    return best[1:]
 
 
 def rank_program(g, core, T, topo):
@@ -114,53 +189,48 @@ def rank_program(g, core, T, topo):
             l = [r for r in rec.get(x[1], []) if not (x[2] <= r[0] and r[1] <= x[3])]
             rec[x[1]] = l + [(x[2], x[3], tok, True)]
 
-    calls, seen = [], {}
+    calls, emits, seen, choice, loaded = [], [], {}, [], []
 
-    def note(e, reads, writes, time, late, emit, behind=()):
-        me, deps = len(calls), set(behind)
+    def note(ways, late, behind=(), shy=0.0):
+        me, deps, time = len(calls), set(behind), {x[0]: x[3] for x in ways}
+        reads, writes = [x for w in ways for x in w[1]], [x for w in ways for x in w[2]]
         for lst, wr in ((reads, False), (writes, True)):
             for x in lst:
-                deps.update(i for (lo, hi, i, w) in seen.get(x[1], [])
-                            if lo < x[3] and x[2] < hi and (w or wr or (x[4] and calls[i][0] != e)))
+                deps.update(i for (lo, hi, i, w) in seen.get(x[1], []) if lo < x[3] and x[2] < hi
+                            and (w or wr or (x[4] and (len(time) > 1 or list(calls[i][0]) != list(time)))))
         for x in reads:
             seen.setdefault(x[1], []).append((x[2], x[3], me, False))
         for x in writes:
             seen[x[1]] = [r for r in seen.get(x[1], []) if not (x[2] <= r[0] and r[1] <= x[3])] + [(x[2], x[3], me, True)]
-        deps.discard(me)
-        calls.append((e, time, late, sorted(deps), emit))
+        calls.append([time, late, sorted(deps), shy, 0.0])
+        emits.append({x[0]: x[4] for x in ways})
         return me
 
-    def issue_all():
-        n = len(calls)
+    def either(kind, *ways):
+        choice.append([])
+        for f in ways:
+            f()
+        note(choice.pop(), WAKE, shy=SHY[kind])
 
-        def gap(i, j):
-            return 0.0 if calls[i][0] == calls[j][0] == "P" else calls[i][2]
-        way = [c[1] + c[2] for c in calls]
-        for j in range(n - 1, -1, -1):
-            for i in calls[j][3]:
-                way[i] = max(way[i], calls[i][1] + gap(i, j) + way[j])
-        start, held = [0.0] * n, {}
-        for j in sorted(range(n), key=lambda j: (-way[j], j)):
-            t = max([start[i] + calls[i][1] + gap(i, j) for i in calls[j][3]] + [0.0])
-            slots = held.setdefault(calls[j][0], [])
-            k = 0
-            while k < len(slots) and slots[k][0] < t + calls[j][1]:
-                t = max(t, slots[k][1])
-                k += 1
-            slots.insert(k, (t, t + calls[j][1]))
-            start[j] = t
+    def urge(name):
+        calls[-1][4] = URGE[name]
+
+    def issue_all():
+        if not ORDER:
+            ORDER.extend(order_of_issue(calls))
+        engine, start = ORDER
         awaited = set()
-        for c in calls:
-            mine = [i for i in c[3] if calls[i][0] == "P"]
-            if mine and c[0] != "P":
+        for j, c in enumerate(calls):
+            mine = [i for i in c[2] if engine[i] == "P"]
+            if mine and engine[j] != "P":
                 awaited.add(max(mine, key=lambda i: (start[i], i)))
-        for j in sorted(range(n), key=lambda j: (start[j], j)):
-            calls[j][4](calls[j][0] != "P" or j in awaited)
+        for j in sorted(range(len(calls)), key=lambda j: (start[j], j)):
+            emits[j][engine[j]](engine[j] != "P" or j in awaited)
 
     def narrow(x):
         return SCRATCH[x[1]][2] in (B, H, U)
 
-    def op(e, out, ins, call, rate=1.0, also=()):
+    def op(e, out, ins, call, rate=1.0, also=(), behind=()):
         reads = [x for x in ins if isinstance(x, tuple)]
         if len(out) > 6:
             rate = SCATTER
@@ -178,7 +248,10 @@ def rank_program(g, core, T, topo):
                 ins_.then_inc(T.sem[e], 1)
                 cnt[e] += 1
             after((e, cnt[e] + (0 if inc else 1)), reads, writes)
-        note(e, reads, writes, time, WAKE, emit)
+        if choice:
+            choice[-1].append((e, reads, writes, time, emit))
+        else:
+            note([(e, reads, writes, time, emit)], WAKE, behind)
 
     def v_(x):
         return x[0] if isinstance(x, tuple) else x
@@ -204,12 +277,15 @@ def rank_program(g, core, T, topo):
     def scan(out, x, y, init, o0, o1):
         op("V", out, [x, y, init], lambda: g.vector.tensor_tensor_scan(out[0], x[0], y[0], v_(init), o0, o1), half(out, x, y))
 
-    def act(out, x, f=AF.Identity, bias=None, scale=None, total=None):
+    def act(out, x, f=AF.Identity, bias=None, scale=None, total=None, behind=()):
         kw = {}
         for k, v in (("bias", bias), ("scale", scale), ("accum_out", total)):
             if v is not None:
                 kw[k] = v_(v)
-        op("S", out, [x, bias, scale], lambda: g.scalar.activation(out[0], x[0], f, **kw), also=[total] if total else [])
+        op("S", out, [x, bias, scale], lambda: g.scalar.activation(out[0], x[0], f, **kw), also=[total] if total else [], behind=behind)
+
+    def lin(kind, out, x, scale=1.0, bias=0.0):
+        either(kind, lambda: act(out, x, bias=bias, scale=scale), lambda: ts(out, x, scale, OP.mult, bias, OP.add))
 
     def iota(out, pat, base, cm, flt=True):
         if flt:
@@ -220,7 +296,7 @@ def rank_program(g, core, T, topo):
     def mm(out, l, r, start, stop):
         op("P", out, [l, r], lambda: g.tensor.matmul(out[0], l[0], r[0], start, stop), 1.0 if narrow(l) else 4.0)
 
-    def dmas(sem, lst):
+    def dmas(sem, lst, behind=()):
         reads = [i_ for (o, i_) in lst if isinstance(i_, tuple)]
         writes = [o for (o, i_) in lst if isinstance(o, tuple)]
         size = 0
@@ -234,7 +310,10 @@ def rank_program(g, core, T, topo):
                 g.sync.dma_start(v_(o), v_(i_)).then_inc(T.sem[sem], 16)
             tot[sem] = tot.get(sem, 0) + 16 * len(lst)
             after((sem, tot[sem]), reads, writes)
-        note("Y", reads, writes, 0.1 * len(lst) + size / DMA_RATE, DMA_LATE, emit)
+        if reads or behind:
+            return note([("Y", reads, writes, 0.1 * len(lst) + size / DMA_RATE, emit)], DMA_LATE, behind)
+        loaded.append(size / DMA_RATE)
+        return note([("Y", reads, writes, 0.01, emit)], DMA_LATE + sum(loaded), range(len(loaded) - 1))
 
     def send(lst, first=0.0):
         per = 1
@@ -261,8 +340,8 @@ def rank_program(g, core, T, topo):
                 tot[sem] = tot.get(sem, 0) + per
             for (d, src, dst, sem) in lst:
                 after((sem, tot[sem]), [], [dst])
-        me = note("G", [x[1] for x in lst], [], SEND + first, SEND_LATE, emit)
-        note("landing", [], [x[2] for x in lst], 0.0, 0.0, landed, [me])
+        me = note([("G", [x[1] for x in lst], [], SEND + first, emit)], SEND_LATE)
+        note([("landing", [], [x[2] for x in lst], 0.0, landed)], 0.0, [me])
 
     def sel(fam, k):
         return a(fam, 15 - k, 143 - k)
@@ -287,14 +366,17 @@ def rank_program(g, core, T, topo):
     def fam(name, weight, at=0.0):
         ts(a(name), a("r143"), at, OP.is_equal, weight, OP.mult)
 
+    def load_positions(k, behind=()):
+        dmas("q%d" % k, [(a("pos_r", 1024 * k, 1024 * k + 1024), T.wpos[:, 1024 * k:1024 * k + 1024])], behind)
+
     dmas("d0", [(a("gst_r", 0, 64), T.gst[:]), (a("gln_r", 0, 64), T.gln[:])])
     dmas("d1", [(a("sens_r"), T.sens[:])])
     dmas("d2", [(a("rel_r"), T.rel[:])])
-    dmas("d3", [(a("cur_r", c, c + 1), T.cur[:, 16 * c:16 * c + 16]) for c in range(4)])
+    dmas("d3", [(a("cur_r"), T.cur[:])])
     dmas("d4", [(a("nxt_r"), T.nxt[:])])
     dmas("d5", [(a("heap_r"), T.heap[:])])
-    for k in range(4):
-        dmas("q%d" % k, [(a("pos_r", 1024 * k, 1024 * k + 1024), T.wpos[:, 1024 * k:1024 * k + 1024])])
+    for k in range(EARLY):
+        load_positions(k)
 
     iota(a("io_p", 0, 1), [[0, 1]], 0, 1, False)
     iota(a("xf"), [[1, 256]], 0, 0)
@@ -302,85 +384,70 @@ def rank_program(g, core, T, topo):
     ts(a("io_p", 1, 2), a("io_p", 0, 1), 15, OP.bitwise_and)
     ts(a("io_p", 2, 3), a("io_p", 0, 1), 7, OP.bitwise_and)
     ts(a("io_p", 3, 4), a("io_p", 0, 1), 3, OP.bitwise_and)
-    c_, c8, c4 = a("io_p", 1, 2), a("io_p", 2, 3), a("io_p", 3, 4)
-    cp(pcol("c"), c_)
-    cp(pcol("k"), c4)
-    cp(pcol("c8"), c8)
+    c_, c8 = a("io_p", 1, 2), a("io_p", 2, 3)
+    cp(a("pc", 0, 3), a("io_p", 1, 4))
+    c, _c8, _k = pcol("c"), pcol("c8"), pcol("k")
     tt(pcol("g16"), a("io_p", 0, 1), c_, OP.subtract)
-    ts(a("idu"), a("xf", 0, 64), 16.0, OP.mult, pcol("c"), OP.add)
+    ts(a("idu"), a("xf", 0, 64), 16.0, OP.mult, c, OP.add)
     ts(a("b1"), a("xf", 0, 128), pcol("g16"), OP.subtract)
     ts(a("r143"), a("xf", 0, 144), pcol("g16"), OP.subtract, 15.0, OP.subtract)
     ts(a("b2"), a("b1"), 15.0, OP.is_gt, 1000.0, OP.mult)
     tt(a("rg"), a("b1"), a("b2"), OP.subtract)
-    ts(a("ek"), a("xf", 0, 16), pcol("c"), OP.is_equal)
+    for k in range(16):
+        ts(a("tri", 128 * k, 128 * k + 128), a("rg"), float(k), OP.is_ge)
+    group, upper = a("tri", 0, 128), a("tri", 1024, 1152)
+    ts(a("ek"), a("xf", 0, 16), c, OP.is_equal)
     ts(a("ek8"), a("xf", 0, 16), pcol("c8"), OP.is_equal)
-    ts(pcol("c3"), c_, 3.0, OP.mult)
+    ts(pcol("h01"), c_, 2, OP.is_lt)
+    ts(pcol("lo8"), c_, 8, OP.is_lt)
+    ts(pcol("a0"), c8, 4, OP.is_lt)
+    ts(pcol("hs"), ek(0), 65536.0, OP.mult, ek(1), OP.subtract)
+    ts(pcol("hb"), ek(0), ek(2), OP.subtract, CUT, OP.mult)
+    lo8 = pcol("lo8")
+    for name, x, scale, bias in (("c3", c, 3.0, 0.0), ("c4x", c, 4.0, 0.0), ("cm2", c, 1.0, -2.0), ("w4", pcol("h01"), 4.0, 0.0),
+                                 ("hi8", lo8, -1.0, 1.0), ("nh8", lo8, 1.0, -1.0), ("wd", lo8, -2.0, 1.0),
+                                 ("u4", ek(2), 1.0, ek(3)), ("u6", ek(3), 1.0, ek(4)),
+                                 ("a1", pcol("a0"), -2.0 / 512, 1.0 / 512), ("u5", pcol("hi8"), 4.0, pcol("k"))):
+        lin("constant", pcol(name), x, scale, bias)
+    lin("constant", a("ss", 0, 1), lo8, -768.0)
     ts(a("ek3"), a("xf", 0, 48), pcol("c3"), OP.is_equal)
-    ts(pcol("c4x"), c_, 4.0, OP.mult)
-    ts(pcol("w4"), c_, 2, OP.is_lt, 4.0, OP.mult)
     ts(a("f5"), a("r143"), pcol("c4x"), OP.subtract, 0.0, OP.is_ge)
     ts(a("f6"), a("r143"), pcol("c4x"), OP.subtract, 4.0, OP.is_lt)
     tt(a("f5"), a("f5"), a("f6"), OP.mult)
-    ts(a("rqf"), a("f5"), pcol("w4"), OP.mult)
-    ts(pcol("h01"), c_, 2, OP.is_lt)
-    ts(pcol("lo8"), c_, 8, OP.is_lt)
-    ts(pcol("hi8"), c_, 8, OP.is_ge)
-    ts(pcol("nh8"), c_, 8, OP.is_ge, -1.0, OP.mult)
-    ts(a("ss", 0, 1), c_, 8, OP.is_lt, -768.0, OP.mult)
-    ts(pcol("hs"), ek(0), 65536.0, OP.mult, ek(1), OP.subtract)
-    ts(pcol("hb"), ek(0), ek(2), OP.subtract, CUT, OP.mult)
-    ts(pcol("wd"), pcol("hi8"), 2.0, OP.mult, -1.0, OP.add)
-    ts(pcol("u2"), ek(2), 0.25, OP.mult)
-    ts(pcol("u3"), ek(2), -(2.0 ** -14), OP.mult)
-    ts(pcol("u4"), ek(2), ek(3), OP.add)
-    ts(pcol("cm2"), c_, -2.0, OP.add)
-    ts(pcol("lo512"), pcol("lo8"), 512.0, OP.mult)
-    ts(pcol("hi512"), pcol("hi8"), 512.0, OP.mult)
-    ts(pcol("a0"), c8, 4, OP.is_lt)
-    ts(pcol("a1"), pcol("a0"), -2.0 / 512, OP.mult, 1.0 / 512, OP.add)
-    ts(pcol("u5"), pcol("hi8"), 4.0, OP.mult, pcol("k"), OP.add)
-    ts(a("idf"), a("rg"), pcol("c"), OP.is_equal)
-    ts(a("idb"), a("rg"), pcol("c"), OP.is_equal)
-    ts(a("idn"), a("rg"), pcol("c"), OP.is_equal, -1.0, OP.mult)
+    lin("constant", a("rqf"), a("f5"), pcol("w4"))
+    ts(a("idf"), a("rg"), c, OP.is_equal)
     ts(a("b3"), a("rg"), 0.0, OP.is_equal, 2.0 ** -16, OP.mult)
     ts(a("b4"), a("rg"), 1.0, OP.is_equal)
     tt(a("f7"), a("b3"), a("b4"), OP.add)
-    ts(a("bc"), a("b4"), CUT / 16, OP.mult)
-    ts(a("bdp"), a("f7"), pcol("wd"), OP.mult)
-    ts(a("bdm"), a("f7"), pcol("wd"), OP.mult, -1.0, OP.mult)
-    ts(a("b15"), a("rg"), 0.0, OP.is_ge, ek(15), OP.mult)
-    ts(a("bon"), a("rg"), 0.0, OP.is_ge, -1.0, OP.mult)
-    ts(a("bop"), a("rg"), 0.0, OP.is_ge)
-    ts(a("boh"), a("rg"), 0.0, OP.is_ge)
-    for k in range(16):
-        ts(a("tri", 128 * k, 128 * k + 128), a("rg"), float(k), OP.is_ge)
-    for name, weight in (("sh", pcol("h01")), ("sn", ek(2)), ("sz", pcol("lo8")), ("szb", pcol("lo8")), ("sf", pcol("u2")),
-                         ("sk", pcol("u3")), ("s2", 2.0), ("s1", 1.0), ("sm", -1.0)):
+    cp(a("boh"), group)
+    tt(a("b2"), group, upper, OP.subtract)
+    for name, weight in (("s1", 1.0), ("sz", lo8), ("smh", -1.0)):
         fam(name, weight)
     fam("lsf", pcol("u4"), pcol("cm2"))
     fam("wsf", 1.0, pcol("u5"))
-    ts(a("ridx"), a("xf", 0, 32), 16.0, OP.mult, pcol("c"), OP.add)
-    ts(a("top"), a("ridx"), 6144.0, OP.add)
-    ts(a("top2"), a("ridx", 0, 16), 4097.0, OP.add)
-    ts(a("cd2"), a("ridx", 0, 16), -1.0, OP.mult, -2049.0, OP.add)
-    ts(a("nfr"), a("ridx", 0, 16), -1.0 / 512, OP.mult, -1.0 / 1024, OP.add)
+    for name, x, scale in (("idb", a("idf"), 1.0), ("idn", a("idf"), -1.0), ("bc", a("b4"), CUT / 16), ("bdp", a("f7"), pcol("wd")),
+                           ("bdm", a("bdp"), -1.0), ("bop", group, 1.0), ("b15", group, ek(15)), ("bon", group, -1.0),
+                           ("sh", a("s1"), pcol("h01")), ("sn", a("s1"), ek(2)), ("s34", a("s1"), pcol("u6")), ("szb", a("s1"), lo8),
+                           ("s2", a("s1"), 2.0), ("s32", a("s1"), 1.0 / 32), ("sm", a("s1"), -1.0),
+                           ("hib", upper, 16.0), ("lob", a("b2"), 16.0)):
+        lin("constant", a(name), x, scale)
+    lin("constant", a("ridx"), a("xf", 0, 32), 16.0, c)
+    for o, scale, bias in ((a("top"), 1.0, 6144.0), (a("mid", 0, 32), 1.0, 256.0), (a("mid", 32, 64), 0.0, 256.0), (a("mid", 64, 68), 2.0, 0.5),
+                           (a("top2"), 1.0, 4097.0), (a("cd2"), -1.0, -2049.0), (a("nfr"), -1.0 / 512, -1.0 / 1024)):
+        lin("constant", o, a("ridx", 0, o[5][1]), scale, bias)
     ts(a("rfr"), a("xf"), 1.0 / 8192, OP.mult)
-    ms(a("relw"), 0.0)
-    ts(a("iotab"), a("relw", 0, 384), 0.0, OP.mult, pcol("c"), OP.add)
-    ts(a("iotab"), a("iotab"), 1.0, OP.add)
-    ts(a("iotab", 0, 384, 48), a("iotab", 0, 384, 48), -1.0, OP.add)
     ms(a("ones"), 1.0)
-    ms(a("mend"), 1.0)
-    ms(a("mend", 47, 384, 48), 0.0)
-    ms(a("cc"), 0.0)
-    ms(a("cs", 0, 1), 0.0)
-    ms(a("ds", 0, 1), 16384.0)
-    ms(a("rw", 0, 8), -2048.0)
-    ms(a("gone"), -1.25)
-    ms(a("pt", 0, 1), -1.25)
-    ms(a("pt", 4097, 4368), 0.0)
-    for k in range(DEEP):
-        ms(a("y%d" % k, 7, 8), 0.25)
+    lin("constant", a("iotab"), a("ones", 0, 384), 1.0, c)
+    lin("constant", a("iotab", 0, 384, 48), a("ones", 0, 8), 0.0, c)
+    for o, value in ([(a("mend"), 1.0), (a("mend", 47, 384, 48), 0.0), (a("cc"), 0.0), (a("cs", 0, 1), 0.0), (a("ds", 0, 1), 16384.0),
+                      (a("rw", 0, 8), -2048.0), (a("gone"), -1.25), (a("pt", 0, 1), -1.25), (a("pt", 4097, 4368), 0.0)]
+                     + [(a("y%d" % k, 7, 8), 0.25) for k in range(DEEP)]):
+        lin("constant", o, a("ones", 0, o[5][1]), 0.0, value)
+    zero = a("hw", 15360, 16384)
+    ms(zero, 0.0)
+    for k in range(15):
+        o = a("hw", 1024 * k, 1024 * k + 1024)
+        either("fill", lambda: ms(o, 0.0), lambda: act(o, zero))
 
     ms(a("gst_r", 64, 68), 0)
     ms(a("gln_r", 64, 68), 0)
@@ -397,14 +464,16 @@ def rank_program(g, core, T, topo):
     send([((rank - n) % N, a("tl", 0, 88), a("tl", 88 * n, 88 * n + 88), "tarr") for n in range(1, N)], FIRST)
     for k in range(4):
         iota(a("w", 1664 * k, 1664 * k + 1664), [[0, 1664]], 0, 0)
-    cp(a("tli", 528, 704), a("tl", 3, 704, 4))
     for x in range(3):
         cp(a("tli", x, 528, 3), a("tl", x, 704, 4))
+    dmas("d12", [(a("tab", rows=row(8 + q)), a("tli", 66 * q, 66 * q + 64)) for q in range(N)])
+    cp(a("tli", 528, 704), a("tl", 3, 704, 4))
     ts(a("lnf", 0, 528, 3), a("tli", 528, 704), 31, OP.bitwise_and)
     ts(a("lnf", 1, 528, 3), a("tli", 528, 704), 5, OP.logical_shift_right, 31, OP.bitwise_and)
     ts(a("lnf", 2, 528, 3), a("tli", 528, 704), 10, OP.logical_shift_right)
-    dmas("d6", [(a("tab", rows=row(8 + q)), a("tli", 66 * q, 66 * q + 64)) for q in range(N)]
-         + [(a("tab", rows=row(q)), a("lnf", 66 * q, 66 * q + 64)) for q in range(N)])
+    tables = dmas("d6", [(a("tab", rows=row(q)), a("lnf", 66 * q, 66 * q + 64)) for q in range(N)])
+    for k in range(EARLY, 4):
+        load_positions(k, [tables])
 
     for x in range(2):
         cp(a("sp", 64 * x, 64 * x + 64), a("sens_r", x, 128, 2))
@@ -414,59 +483,56 @@ def rank_program(g, core, T, topo):
     tt(a("sp", 128, 256), a("sx", 0, 128), a("sx", 128, 256), OP.add)
     dmas("d7", [(a("sw", rows=row(x)), a("sp", 64 * x, 64 * x + 64)) for x in range(4)])
     cp(a("lnx"), a("nxt_r"))
-    act(a("tsy"), ind(a("sw"), a("lnx")))
+    lin("look", a("tsy"), ind(a("sw"), a("lnx")))
     ts(a("ti"), a("rel_r"), float(1024 * (N - rank)), OP.add)
     ts(a("rp", 0, 256), a("rel_r"), 992, OP.bitwise_and)
     ts(a("rp", 256, 512), a("rel_r"), 31, OP.bitwise_and)
     ts(a("rp", 512, 768), a("ti"), 10, OP.logical_shift_right, 7, OP.bitwise_and)
     cp(a("rpb"), a("rp"))
-    dmas("d8", [(a("relw", rows=row(x)), a("rpb", 256 * x, 256 * x + 256)) for x in range(3)])
-    act(a("hhi"), ind(a("heap_r"), a("idu")))
-    act(a("heapf"), ind(a("heap_r"), a("idu")))
+    dmas("d8", [(a("hw", 0, 4096, rows=row(x)), a("rpb", 256 * i, 256 * i + 256)) for i, x in enumerate((3, 4, 2))])
+    either("heap", lambda: act(a("hhi"), ind(a("heap_r"), a("idu"))), lambda: cp(a("hhi"), a("heap_r")))
+    either("heap", lambda: act(a("heapf"), ind(a("heap_r"), a("idu"))), lambda: cp(a("heapf"), a("heap_r")))
     for j, p in enumerate(("p0", "p1")):
         mm(a(p), a("idf"), a("heapf", 512 * j, 512 * j + 512), True, False)
         mm(a(p), a("idn"), a("hhi", 512 * j, 512 * j + 512), False, True)
-        act(a("hlo", 512 * j, 512 * j + 512), a(p))
-    for k in range(16):
-        if k < HW_V:
-            ms(a("hw", 1024 * k, 1024 * k + 1024), 0.0)
-        else:
-            act(a("hw", 1024 * k, 1024 * k + 1024), a("hw", 0, 1024))
+        lin("out", a("hlo", 512 * j, 512 * j + 512), a(p))
     dmas("d9", [(a("hw", rows=row(0)), a("hhi")), (a("hw", rows=row(1)), a("hlo"))])
     for k in range(4):
         o, x = a("pt", 1 + 1024 * k, 1025 + 1024 * k), a("pos_r", 1024 * k, 1024 * k + 1024)
-        if k < POS_V:
-            ts(o, x, -1.25, OP.add)
-        else:
-            act(o, ind(x, a("idu")), bias=-1.25)
+        either("positions", lambda: act(o, ind(x, a("idu")), bias=-1.25), lambda: ts(o, x, -1.25, OP.add))
 
     def look_up(nc):
         n = 32 * nc
-        for x in range(nc):
+        for x in range(2):
             for b in range(2):
-                mm(a("p7", 32 * x, 32 * x + 32), sel("rqf", 8 * b), a("gc", nc * b + x, 64 * nc, 2 * nc), x + b == 0, x == nc - 1 and b == 1)
-        ts(a("l2", 0, n), a("p7", 0, n), pcol("k"), OP.add)
-        act(a("rqw", 0, 16 * n), ind(a("relw"), a("l2", 0, n)))
-        w2l(a("p7", 0, n), "sh", "rqw", 0, 16 * n, stop=False)
-        w2l(a("p7", n, 2 * n), "sn", "rqw", 0, 16 * n, start=False)
-        cp(a("l3", 0, 2 * n), a("p7", 0, 2 * n))
-        ts(a("pq", 0, n) if nc == 2 else a("sel"), a("p7", n, 2 * n), 768.0, OP.mult, 768.0, OP.add)
-        act(a("msk", 0, 16 * n), ind(a("ek8"), a("l3", n, 2 * n)))
+                if nc == 2:
+                    o, i_ = a("p6", 32 * x, 32 * x + 32), a("gc", 2 * b + x, 128, 4)
+                else:
+                    o, i_ = a("p6", x, 32, 2), a("gc", 32 * x + 16 * b, 32 * x + 16 * b + 16)
+                mm(o, sel("rqf", 8 * b), i_, x + b == 0, x + b == 2)
+        ts(a("l2", 0, n), a("p6", 0, n), pcol("k"), OP.add)
+        lin("look", a("rqw", 0, 16 * n), ind(a("hw", 0, 4096), a("l2", 0, n)))
+        w2l(a("p6", 0, n), "s34", "rqw", 0, 16 * n, stop=False)
+        w2l(a("p6", n, 2 * n), "sn", "rqw", 0, 16 * n, start=False)
+        cp(a("l3", 0, 2 * n), a("p6", 0, 2 * n))
+        lin("small", a("pq") if nc == 2 else a("sel"), a("p6", n, n + 32), 768.0, 768.0)
+        lin("look", a("msk", 0, 16 * n), ind(a("ek8"), a("l3", n, 2 * n)))
         if nc == 2:
-            tt(a("cd"), a("pq", 32, 64), a("pq", 0, 32), OP.subtract)
-            ts(a("cd"), a("cd"), 1.0 / 512, OP.mult)
+            urge("mask")
+            lin("small", a("pqs"), a("p6", n, 2 * n), 1.5)
+            tt(a("cd"), a("pqs", 32, 64), a("pqs", 0, 32), OP.subtract)
             for h in range(2):
                 tt(a("g2c", 512 * h, 512 * h + 512), ind(a("tab"), a("l3", 32 * h, 32 * h + 32)), a("msk", 512 * h, 512 * h + 512), OP.mult)
 
-    def next_senses(src, lo):
+    def next_senses(r):
         for k in range(8):
-            mm(a("p7", 0, 8), sel("lsf", 2 * k), a(src, lo + k, lo + 64, 8), k == 0, k == 7)
-        cp(a("lsy"), a("p7", 0, 8))
-        act(a("gc"), ind(a("tsy"), a("lsy")))
+            lo = 64 * (r - 1) + k if r else 16 * (k % 4) + k // 4
+            mm(a("p6", 0, 8), sel("lsf", 2 * k), a("ywb", lo, 64 * r, 8) if r else a("gc", lo, lo + 15, 2), k == 0, k == 7)
+        cp(a("lsy"), a("p6", 0, 8))
+        lin("look", a("gc"), ind(a("tsy"), a("lsy")))
 
     cp(a("lcur"), a("cur_r"))
-    act(a("gc", 0, 64), ind(a("sw"), a("lcur")))
-    cp(a("ls0"), a("gc", 0, 64))
+    lin("look", a("gc", 0, 64), ind(a("sw"), a("lcur")))
     look_up(1)
 
     def requests(r):
@@ -476,20 +542,20 @@ def rank_program(g, core, T, topo):
         else:
             tt(a("g2"), ind(a("tab"), a("l3", 0, 32)), a("msk", 0, 512), OP.mult)
             act(a("d0"), a("g2"), AF.Relu, bias=1.0, scale=pcol("nh8"))
-        act(a("p6"), a("g2"), AF.Sign)
+        act(a("p4"), a("g2"), AF.Sign)
         scan(a("ss", 1, 513), a("d0"), a("g2"), a("ss", 0, 1), OP.mult, OP.add)
-        tt(a("xm"), a("p6"), a("ss", 0, 512), OP.mult)
-        w2l(a("p7", 0, 32), "sz", "xm", 0, 512)
+        tt(a("xm"), a("p4"), a("ss", 0, 512), OP.mult)
+        w2l(a("p5", 0, 32), "sz", "xm", 0, 512)
         for h in range(2):
-            o, lo = a("p%d" % (4 + h), 0, 256), 256 * h
+            o, lo = a("p%d" % h, 0, 256), 256 * h
             mm(o, a("bc"), a("ones", 0, 256), True, False)
             mm(o, a("bdp"), a("ss", lo + 1, lo + 257), False, False)
             mm(o, a("bdm"), a("ss", lo, lo + 256), False, True)
-            act(a("hh", lo, lo + 256), o, bias=pcol("hb"), scale=pcol("hs"))
+            lin("round", a("hh", lo, lo + 256), o, pcol("hs"), pcol("hb"))
             tt(a("val", lo, lo + 256), o, a("hh", lo, lo + 256), OP.add)
-        ts(a("zf"), a("p7", 0, 32), 0.0, OP.is_ge, 8192.0, OP.mult)
-        tt(a("zt"), a("p7", 0, 32), a("sel"), OP.add)
-        ts(a("sh_"), a("p7", 0, 32), -384.0, OP.is_ge, 384.0, OP.mult)
+        ts(a("zf"), a("p5", 0, 32), 0.0, OP.is_ge, 8192.0, OP.mult)
+        tt(a("zt"), a("p5", 0, 32), a("sel"), OP.add)
+        ts(a("sh_"), a("p5", 0, 32), -384.0, OP.is_ge, 384.0, OP.mult)
         tt(a("zu"), a("zt"), a("zf"), OP.add)
         tt(a("zo"), a("zu"), a("top"), OP.min)
         cp(a("offu"), a("zo"))
@@ -503,42 +569,38 @@ def rank_program(g, core, T, topo):
         for k in range(16):
             mm(o, a("tri", 128 * k, 128 * k + 128), a("w", 768 * lo + k, 768 * hi, 16), False, k == 15)
         scan(a("cc", 48 * lo + 1, 48 * hi + 1), o, a("mend", 0, n), 0.0, OP.add, OP.mult)
-        base, near = a("p%d" % (4 + b), 0, n), a("near", 48 * lo, 48 * hi)
+        base, near = a("p%d" % (3 + b), 0, n), a("near", 48 * lo, 48 * hi)
         mm(base, a("b15"), a("cc", 48 * lo, 48 * hi), True, True)
-        act(near, o)
+        lin("out", near, o)
         tt(near, base, near, OP.add)
         ts(a("as%d" % r, 48 * lo, 48 * hi), near, 16383.0, OP.min)
         send([((rank + n) % N, a("as%d" % r, 48 * n, 48 * n + 48), a("al%d" % r, 48 * n, 48 * n + 48), "aa%d" % n)
               for n in range(max(lo, 1), hi)])
 
-    def firsts(last):
-        w2l(a("p2", 0, 384), "sf", "w", 0, 6144)
-        act(a("fl"), a("p2", 0, 384))
+    def firsts():
         for k in range(16):
             n = 384 if k % 2 else 408
-            mm(a("p3", 0, n), sel("sk", k), a("w", 384 * k, 384 * k + n), k == 0, k == 15)
-        act(a("keep"), a("p3", 0, 408), AF.Relu, bias=1.0, scale=-1.0)
-        if not last:
-            dmas("clr", [(a("w", 0, 6144, rows=row(x)), a("hw", 0, 6144, rows=row(3 + x))) for x in range(3)])
+            mm(a("p3", 0, n), sel("sn", k), a("w", 384 * k, 384 * k + n), k == 0, k == 15)
+        either("out", lambda: act(a("keep"), a("p3", 0, 408), AF.Relu, bias=1.0), lambda: ts(a("keep"), a("p3", 0, 408), 0.0, OP.is_equal))
 
     def segments():
-        act(a("g2b"), a("g2"))
-        w2l(a("p7", 0, 32), "szb", "g2b", 0, 512)
-        tt(a("se"), a("p7", 0, 32), a("zt"), OP.add)
+        lin("look", a("g2b"), a("g2"))
+        mm(a("p5", 0, 32), a("idf"), a("zt"), True, False)
+        w2l(a("p5", 0, 32), "szb", "g2b", 0, 512, start=False)
         tt(a("sl"), a("sel"), a("zf"), OP.subtract)
         tt(a("sr"), a("sel"), a("sh_"), OP.add)
-        tt(a("se"), a("se"), a("sl"), OP.min)
+        tt(a("se"), a("p5", 0, 32), a("sl"), OP.min)
         ts(a("rho"), a("sr"), -768.0, OP.add, 1.0 / 128, OP.mult)
         tt(a("sq"), a("se"), a("sr"), OP.subtract)
         ts(a("leu"), a("sq"), 768.0, OP.add, 0.0, OP.max)
-        act(a("mc"), ind(a("ek3"), a("rho")))
+        lin("look", a("mc"), ind(a("ek3"), a("rho")))
 
     def answer(r, b):
         lo, hi = BACK[b]
         for n in range(lo, hi):
-            lst = a(("al%d" if n else "as%d") % r, 48 * n, 48 * n + 48)
-            (act if OWN[n] == "S" else cp)(a("ow", 768 * n, 768 * n + 768), ind(a("hw"), lst))
-        o = a("p%d" % (4 + b % 3), 0, 48 * (hi - lo))
+            o, x = a("ow", 768 * n, 768 * n + 768), ind(a("hw"), a(("al%d" if n else "as%d") % r, 48 * n, 48 * n + 48))
+            either("own", lambda: act(o, x), lambda: cp(o, x))
+        o = a(("p7", "p5", "p4", "p5")[b], 0, 48 * (hi - lo))
         w2l(o, "sh", "ow", 768 * lo, 768 * hi)
         ts(a(("rs%d" if lo else "rl%d") % r, 48 * lo, 48 * hi), o, 1.0, OP.add)
         if lo:
@@ -548,17 +610,16 @@ def rank_program(g, core, T, topo):
     def phrases(r, b):
         lo, hi = BACK[b]
         ts(a("rw", 8 + 48 * lo, 8 + 48 * hi), a("rl%d" % r, 48 * lo, 48 * hi), -2048.0, OP.add)
-        mm(a("p2", 48 * lo, 48 * hi), a("idb"), a("fl", 48 * lo, 48 * hi), True, False)
-        mm(a("p2", 48 * lo, 48 * hi), a("idf"), a("rw", 8 + 48 * lo, 8 + 48 * hi), False, True)
-        ts(a("lx", 48 * lo, 48 * hi), a("p2", 48 * lo, 48 * hi), 2048.0, OP.add, 0.0, OP.max)
+        o = a("p7" if b % 2 else "p2", 0, 48 * (hi - lo))
+        w2l(o, "sn", "w", 768 * lo, 768 * hi, stop=False)
+        mm(o, a("idf"), a("rw", 8 + 48 * lo, 8 + 48 * hi), False, True)
+        ts(a("lx", 48 * lo, 48 * hi), o, 2048.0, OP.add, 0.0, OP.max)
         for n in range(lo, hi):
             s = str(n % DEEP)
-            act(a("y" + s, 8, 776), ind(a("pt"), a("rl%d" % r, 48 * n, 48 * n + 48)), AF.Abs, bias=1.0)
+            y, pr = a("y" + s, 8, 776), a("pr" + s)
+            act(y, ind(a("pt"), a("rl%d" % r, 48 * n, 48 * n + 48)), AF.Abs, bias=1.0)
             tt(a("ct" + s), ind(a("pt"), a("lx", 48 * n, 48 * n + 48)), a("y" + s, 7, 775), OP.is_equal)
-            if PRESENT[n] == "S":
-                act(a("pr" + s), a("y" + s, 8, 776), AF.Sign, bias=-0.25)
-            else:
-                ts(a("pr" + s), a("y" + s, 8, 776), 0.5, OP.is_gt)
+            either("present", lambda: act(pr, y, AF.Sign, bias=-0.25), lambda: ts(pr, y, 0.5, OP.is_gt))
             scan(a("rr" + s), a("ct" + s), a("ct" + s), 0.0, OP.mult, OP.add)
             for f_, src, p in (("s1", "ct", "p1"), ("s1", "pr", "p0"), ("s2", "rr", "p0")):
                 for h in range(2):
@@ -570,34 +631,36 @@ def rank_program(g, core, T, topo):
         scan(a("cs", 1, 409), a("keep"), a("p0", 0, 408), 0.0, OP.mult, OP.add)
         tt(a("ge"), ind(a("cs", 0, 409), a("leu")), a("mc"), OP.mult)
         for k in range(8):
-            mm(a("p3", 0, 64), a("bop" if k >= 4 else "bon"), a("ge", k, 512, 8), k == 0, k == 7)
-        ts(a("wa"), a("p3", 0, 64, 2), 0.0, OP.is_gt, pcol("lo512"), OP.mult)
-        ts(a("wb"), a("p3", 1, 64, 2), 0.0, OP.is_gt, pcol("hi512"), OP.mult)
-        ts(a("winr"), a("p3", 0, 64), 0.0, OP.is_gt)
-        tt(a("ab"), a("wa"), a("wb"), OP.add)
+            mm(a("p0", 0, 64), a("bop" if k >= 4 else "bon"), a("ge", k, 512, 8), k == 0, k == 7)
+        act(a("sg"), a("p0", 0, 64), AF.Sign, bias=-0.5)
+        mm(a("p4", 0, 64), a("idf"), a("mid", 0, 64), True, False)
+        for x in range(1 if last else 0, 2):
+            for b in range(2):
+                mm(a("p4", 32 * x, 32 * x + 32), a("hib" if b else "lob"), a("sg", b, 64, 2), False, x + b == 2)
         if not last:
-            tt(a("wl"), a("ab"), a("ridx"), OP.add)
-            cp(a("lu"), a("wl"))
-            tt(a("wc"), a("ab"), a("cd"), OP.mult)
-            tt(a("sel"), a("wc"), a("pq", 0, 32), OP.add)
+            cp(a("lu"), a("p4", 0, 32))
+            tt(a("wc"), a("p4", 32, 64), a("cd"), OP.mult)
+            tt(a("sel"), a("wc"), a("pq"), OP.add)
+        lin("small", a("wm"), a("p4", 32, 64), pcol("a1"), pcol("a0"))
         for k in range(4):
-            mm(a("p0", 0, 128), a("bop"), a("ge", k, 512, 4), k == 0, k == 3)
-        act(a("ytb", 128 * r, 128 * r + 128), a("p0", 0, 128))
-        tt(a("hd"), a("gc", 1, 128, 2), a("gc", 0, 128, 2), OP.subtract)
-        tt(a("hd2"), a("hd"), a("winr"), OP.mult)
-        tt(a("ywb", 64 * r, 64 * r + 64), a("hd2"), a("gc", 0, 128, 2), OP.add)
+            mm(a("p6", 0, 128), a("bop"), a("ge", k, 512, 4), k == 0, k == 3)
+        lin("out", a("ytb", 128 * r, 128 * r + 128), a("p6", 0, 128))
+        mm(a("p6", 0, 4), a("idf"), a("mid", 64, 68), True, False)
+        w2l(a("p6", 0, 4), "s32", "sg", 0, 64, start=False)
+        cp(a("hl"), a("p6", 0, 4))
+        lin("look", a("ywb", 64 * r, 64 * r + 64), ind(a("gc"), a("hl")))
 
     def barrier_places():
-        act(a("nh"), a("p1", 0, 408), AF.Relu, bias=73728.0, scale=-8192.0)
+        either("out", lambda: act(a("nh"), a("p1", 0, 408), AF.Relu, bias=73728.0, scale=-8192.0),
+               lambda: ts(a("nh"), a("p1", 0, 408), 9.0, OP.is_lt, 8192.0, OP.mult))
         scan(a("ds", 1, 409), a("ones"), a("nh"), 16384.0, OP.add, OP.min)
         tt(a("dg"), ind(a("ds", 0, 409), a("leu")), a("mc"), OP.mult)
-        w2l(a("p2", 0, 32), "s1", "dg", 0, 512)
-        tt(a("ba"), a("se"), a("p2", 0, 32), OP.subtract)
-        tt(a("bd"), a("ba"), a("zt"), OP.is_gt)
-        tt(a("ba"), a("ba"), a("bd"), OP.mult)
+        mm(a("p2", 0, 32), a("idf"), a("se"), True, False)
+        w2l(a("p2", 0, 32), "sm", "dg", 0, 512, start=False)
+        tt(a("bd"), a("p2", 0, 32), a("zt"), OP.is_gt)
+        tt(a("ba"), a("p2", 0, 32), a("bd"), OP.mult)
 
     def barrier_words(r, last):
-        ts(a("wm"), a("ab"), pcol("a1"), OP.mult, pcol("a0"), OP.add)
         tt(a("bb"), a("ba"), a("wm"), OP.mult)
         for p in range(2):
             mm(a("p2", 64, 80), sel("wsf", 8 * p), a("bb", p, 32, 2), p == 0, p == 1)
@@ -605,44 +668,50 @@ def rank_program(g, core, T, topo):
         ts(a("m2", 0, 16), a("m1"), 4, OP.logical_shift_right)
         ts(a("m2", 16, 32), a("m1"), 15, OP.bitwise_and)
         cp(a("cl"), a("m2"))
-        act(a("mk"), ind(a("ek"), a("cl", 16, 32)))
+        lin("look", a("mk"), ind(a("ek"), a("cl", 16, 32)))
         tt(a("bw"), ind(a("rw"), a("cl", 0, 16)), a("mk"), OP.mult)
-        mm(a("p1", 0, 256), a("boh"), a("bw"), True, True)
-        act(a("ybb", 256 * r, 256 * r + 256), a("p1", 0, 256), bias=2047.0)
+        urge("word")
+        mm(a("p3", 0, 256), a("boh"), a("bw"), True, True)
+        lin("out", a("ybb", 256 * r, 256 * r + 256), a("p3", 0, 256), 1.0, 2047.0)
         if last:
             return
-        mm(a("p3", 0, 256), a("boh"), a("rfr"), True, False)
-        mm(a("p3", 0, 256), a("boh"), a("bw"), False, True)
-        act(a("keyw"), a("p3", 0, 256))
-        w2l(a("p2", 0, 16), "sm", "bw", 0, 256)
+        mm(a("p7", 0, 256), a("boh"), a("rfr"), True, False)
+        mm(a("p7", 0, 256), a("boh"), a("bw"), False, True)
+        lin("out", a("keyw"), a("p7", 0, 256))
+        w2l(a("p2", 0, 16), "smh", "bw", 0, 256)
         tt(a("keyl", 0, 16), a("p2", 0, 16), a("nfr"), OP.add)
-        ts(a("keyl", 16, 32), a("p2", 0, 16), -255.5 / 512, OP.add)
+        lin("out", a("keyl", 16, 32), a("p2", 0, 16), 1.0, -255.5 / 512)
         tt(a("bu_"), a("cd2"), a("p2", 0, 16), OP.subtract)
         for i in range(16):
             for x in range(2):
                 at = 512 * i - 16 * i * (i - 1) + x * (256 - 16 * i)
-                act(a("junk", at, at + 256 - 16 * i), a("keyw", 16 * i, 256), AF.Sign,
-                    bias=a("keyl", 16 * x + i, 16 * x + i + 1), total=a("mn", 16 * x + i, 16 * x + i + 1))
+                act(a("eq", at, at + 256 - 16 * i), a("keyw", 16 * i, 256), AF.Sign, bias=a("keyl", 16 * x + i, 16 * x + i + 1),
+                    total=a("mn", 16 * x + i, 16 * x + i + 1), behind=[len(calls) - 1] if i + x else [])
+                calls[-1][0]["S"] += 0.02
+                calls[-1][1] = WAKE if i + x in (0, 16) else 0.0
         tt(a("bv"), a("mn", 0, 16), a("mn", 16, 32), OP.is_equal)
         tt(a("bv"), a("bv"), a("bu_"), OP.mult)
         tt(a("bv"), a("bv"), a("top2"), OP.add)
         cp(a("bu"), a("bv"))
         cp(ind(a("pt"), a("bu")), a("gone"))
+        urge("barred")
 
     for r in range(RO):
         last = r + 1 == RO
         requests(r)
         for b in range(len(ADDR)):
             addresses(r, b)
-        segments()
-        next_senses("ls0" if r == 0 else "ywb", 0 if r == 0 else 64 * (r - 1))
-        firsts(last)
-        for b in range(len(BACK)):
-            answer(r, b)
+        next_senses(r)
         if not last:
             look_up(2)
+        segments()
+        firsts()
+        for b in range(len(BACK)):
+            answer(r, b)
         for b in range(len(BACK)):
             phrases(r, b)
+        if not last:
+            dmas("clr", [(a("w", 0, 6144, rows=row(x)), a("hw", 0, 6144, rows=row(5 + x))) for x in range(3)])
         barrier_places()
         totals(r, last)
         barrier_words(r, last)
@@ -653,6 +722,3 @@ def rank_program(g, core, T, topo):
         need("G", (e, cnt[e]))
     for s in sorted(tot):
         need("G", (s, tot[s]))
-
-
-HW_V, POS_V = 10, 0

from concourse.bass import DstId, RemoteDMATransfer
from concourse.mybir import AluOpType as OP, AxisListType, ActivationFunctionType as AF

F, B, H, I, U = "float32", "bfloat16", "float16", "int32", "uint16"
RO = 3
CUT = 49152.0
ADDR = ((0, 4), (4, 8))
BACK = ((0, 1), (1, 3), (3, 5), (5, 8))
EARLY = 1
DEEP = 2
CYCLE = {"V": 0.00083, "S": 0.00083, "G": 0.00083, "P": 0.00042}
FIXED = {"V": 0.05, "S": 0.065, "G": 0.13, "P": 0.0}
GATHER, SCATTER = 1.56, 3.8
WAKE, DMA_LATE, DMA_RATE, SEND, SEND_LATE, FIRST = 0.16, 1.5, 250e3, 0.6, 1.8, 3.0
SHY = {"own": 0.0, "present": 0.0, "fill": 0.0, "positions": 0.0, "constant": 1.0, "heap": 1.0, "small": 1.0, "round": 1.0,
       "out": 1.0, "look": 1.0}
URGE = {"barred": 3.0, "mask": 8.0, "word": 3.0}
TRIES = [(look, urge) for look in (0.5, 1.0, 2.0, 4.0) for urge in (0.5, 1.0, 1.5)]
ORDER = []


def _scratch():
    s = {}

    def sb(dt, **kw):
        for k, w in kw.items():
            s[k] = ("sbuf", [128, w], dt)
    sb(I, io_p=4, gst_r=68, gln_r=68, cur_r=4, rel_r=256, sens_r=128, nxt_r=64, heap_r=1024, pos_r=4096,
       tli=704, lnf=528, tab=1024, sw=1024, rp=768, ti=256, sp=256, sx=256, m1=16, m2=32)
    sb(F, pc=40, ek=16, ek8=16, ek3=48, xf=256, bon=128, bop=128, bdp=128, bdm=128, b15=128, idf=128, lsf=144, wsf=144, rqf=144,
       f1=144, f2=144, f3=144, f4=144, f5=144, f6=144, f7=128, mend=384, ridx=32, top=32, top2=16, gone=256, heapf=1024,
       pt=4368, tsy=1024, gc=128, msk=1024, g2c=1024, pq=32, pqs=64, cd=32, sel=32,
       wc=32, wm=32, mid=68,
       g2=512, d0=512, ss=516, zf=32, zt=32, zu=32, zo=32, cc=392, near=384,
       sh_=32, se=32, sl=32, sr=32, sq=32, ba=32, bb=32, bd=32,
       cs=416, ds=416, keep=408, nh=408, ge=512, mc=512, mk=256, rw=392, bv=16, keyw=256, keyl=32, mn=32, bu_=16, cd2=16, nfr=16,
       ytb=384, ybb=768, ywb=192)
    sb(B, iotab=384, idb=128, idn=128, r143=144, rg=128, b1=128, b2=128, b3=128, b4=128, bc=128, s2=144, s1=144, sh=144, s34=144,
       szb=144, sn=144, tri=2048, hhi=1024, hlo=1024, hw=16384, w=6656, rpb=768, rqw=1024,
       hh=512, val=512, g2b=512, ow=6144, wk=2304 * DEEP, eq=4352, ones=408, dg=512, sg=64, lob=128, hib=128, s32=144, sm=144)
    sb(H, sz=144, smh=144, boh=128, rfr=256, xm=512, bw=256)
    sb(U, tl=704, idu=64, lu=32, l2=64, l3=128, lcur=4, lnx=64, lsy=8, hl=4, offu=32, leu=32, rho=32, cl=32, bu=16, lx=384)
    for r in range(RO):
        sb(U, **{"as%d" % r: 384, "al%d" % r: 384, "rs%d" % r: 384, "rl%d" % r: 384})
    share = {"hhi": ("ow", 0), "hlo": ("ow", 1024), "rpb": ("ow", 2048), "heapf": ("g2c", 0), "eq": ("wk", 0)}
    for k in range(DEEP):
        sb(F, **{"y%d" % k: 776})
        sb(B, **{"ct%d" % k: 768, "rr%d" % k: 768, "pr%d" % k: 768})
        share.update({"ct%d" % k: ("wk", 2304 * k), "rr%d" % k: ("wk", 2304 * k + 768), "pr%d" % k: ("wk", 2304 * k + 1536)})
    place, top, out = {}, {}, {}
    for k, (_w, sh, dt) in s.items():
        if k in share:
            place[k] = (share[k][0], share[k][1], sh[1])
        elif sh[1] >= 1024:
            out[k] = s[k]
            place[k] = (k, 0, sh[1])
        else:
            pool = "pool_" + dt
            place[k] = (pool, top.get(pool, 0), sh[1])
            top[pool] = top.get(pool, 0) + (sh[1] + 15) // 16 * 16
            out[pool] = ("sbuf", [128, top[pool]], dt)
    for k in range(8):
        out["p%d" % k] = ("psum", [128, 512], F)
        place["p%d" % k] = ("p%d" % k, 0, 512)
    return out, place


SCRATCH, PLACE = _scratch()
SEMAPHORES = (["V", "S", "P", "G", "loc", "tarr", "clr"] + ["d%d" % k for k in range(13)] + ["q%d" % k for k in range(4)]
              + ["aa%d" % k for k in range(1, 8)] + ["ra%d" % k for k in range(1, 8)])


def order_of_issue(calls):
    n = len(calls)
    first, behind = [c[2] for c in calls], [[] for c in calls]
    for j in range(n):
        for i in first[j]:
            behind[i].append(j)

    def gap(i, j):
        return 0.0 if list(calls[i][0]) == list(calls[j][0]) in (["P"], ["Y"]) else calls[min(i, j)][1]

    def forwards(look, urge):
        way = [min(c[0].values()) + c[1] for c in calls]
        for j in range(n - 1, -1, -1):
            way[j] += urge * calls[j][4]
            for i in first[j]:
                way[i] = max(way[i], min(calls[i][0].values()) + gap(i, j) + way[j])
        left, ready, start, engine = [len(x) for x in first], [0.0] * n, [0.0] * n, [None] * n
        free, open_ = {}, {e: [] for c in calls for e in c[0]}
        new = [j for j in range(n) if not left[j]]
        for _ in range(n):
            for i in new:
                for e in calls[i][0]:
                    open_[e].append(i)
            mine = dict(open_, V=[i for i in open_["V"] if len(calls[i][0]) == 1
                                  or free.get("S", 0.0) > max(free.get("V", 0.0), ready[i]) + calls[i][3]])
            t, e = min((max(free.get(e, 0.0), min(ready[i] for i in l)), e) for e, l in mine.items() if l)
            now = [i for i in mine[e] if ready[i] <= t]
            j = max(now, key=lambda i: (way[i], -i))
            soon = [i for i in mine[e] if t < ready[i] < t + calls[j][0][e] and way[i] > way[j] + look]
            if soon:
                j = max(soon, key=lambda i: way[i])
                j = max([i for i in now if t + calls[i][0][e] <= ready[j]] or [j], key=lambda i: way[i])
            start[j], engine[j] = max(t, ready[j]), e
            free[e] = start[j] + calls[j][0][e]
            for x in calls[j][0]:
                open_[x].remove(j)
            new = []
            for i in behind[j]:
                ready[i] = max(ready[i], free[e] + gap(j, i))
                left[i] -= 1
                if not left[i]:
                    new.append(i)
        return start, engine

    def place(order, waits_for, engine, time):
        start, held = [0.0] * n, {}
        for j in order:
            t = max([start[i] + time[i] + gap(i, j) for i in waits_for[j]] + [0.0])
            slots = held.setdefault(engine[j], [])
            k = len(slots)
            while k and slots[k - 1][1] > t:
                k -= 1
            while k < len(slots) and slots[k][0] < t + time[j]:
                t = max(t, slots[k][1])
                k += 1
            slots.insert(k, (t, t + time[j]))
            start[j] = t
        return start
    best = None
    for look, urge in TRIES:
        start, engine = forwards(look, urge)
        time = [calls[j][0][engine[j]] for j in range(n)]
        back = place(sorted(range(n), key=lambda j: (-start[j] - time[j], -j)), behind, engine, time)
        start = place(sorted(range(n), key=lambda j: (-back[j] - time[j], j)), first, engine, time)
        end = max(start[j] + time[j] for j in range(n))
        if best is None or end < best[0]:
            best = (end, engine, start)
    return best[1:]


def rank_program(g, core, T, topo):
    rank = T.rank_of(core)
    if rank is None:
        return
    N = len(T.cores)
    Q = {"V": g.vector, "S": g.scalar, "P": g.tensor, "G": g, "Y": g.sync}
    cnt = {"V": 0, "S": 0, "P": 0, "G": 0}
    known = {e: {} for e in Q}
    rec = {}
    tot = {}

    def a(name, lo=0, hi=None, st=1, rows=None):
        name, off, w = PLACE[name]
        lo, hi = off + lo, off + (w if hi is None else hi)
        cs_ = slice(lo, hi, st) if st != 1 else slice(lo, hi)
        ap = T[name][(slice(None) if rows is None else rows), cs_]
        size = (128 if rows is None else 8, (hi - lo + st - 1) // st)
        if SCRATCH[name][0] == "psum":
            return (ap, name, 0, 512, True, size)
        return (ap, name, lo, hi, False, size)

    def ind(win, off):
        return (win[0].indirect(off[0]), win[1], win[2], win[3], False, (128, 16 * off[5][1]), off)

    def need(e, tok):
        if known[e].get(tok[0], 0) < tok[1]:
            Q[e].wait_ge(T.sem[tok[0]], tok[1])
            known[e][tok[0]] = tok[1]

    def before(e, reads, writes):
        toks = {}
        for lst, wr in ((reads, False), (writes, True)):
            for x in lst:
                for (lo, hi, tok, w) in rec.get(x[1], []):
                    if lo < x[3] and x[2] < hi and (w or wr or (x[4] and tok[0] != e)):
                        if tok[0] == e and e == "P":
                            continue
                        toks[tok[0]] = max(toks.get(tok[0], 0), tok[1])
        for k in sorted(toks):
            need(e, (k, toks[k]))

    def after(tok, reads, writes):
        for x in reads:
            l = [r for r in rec.get(x[1], []) if not (r[2][0] == tok[0] and not r[3] and x[2] <= r[0] and r[1] <= x[3])]
            rec[x[1]] = l + [(x[2], x[3], tok, False)]
        for x in writes:
            l = [r for r in rec.get(x[1], []) if not (x[2] <= r[0] and r[1] <= x[3])]
            rec[x[1]] = l + [(x[2], x[3], tok, True)]

    calls, emits, seen, choice, loaded = [], [], {}, [], []

    def note(ways, late, behind=(), shy=0.0):
        me, deps, time = len(calls), set(behind), {x[0]: x[3] for x in ways}
        reads, writes = [x for w in ways for x in w[1]], [x for w in ways for x in w[2]]
        for lst, wr in ((reads, False), (writes, True)):
            for x in lst:
                deps.update(i for (lo, hi, i, w) in seen.get(x[1], []) if lo < x[3] and x[2] < hi
                            and (w or wr or (x[4] and (len(time) > 1 or list(calls[i][0]) != list(time)))))
        for x in reads:
            seen.setdefault(x[1], []).append((x[2], x[3], me, False))
        for x in writes:
            seen[x[1]] = [r for r in seen.get(x[1], []) if not (x[2] <= r[0] and r[1] <= x[3])] + [(x[2], x[3], me, True)]
        calls.append([time, late, sorted(deps), shy, 0.0])
        emits.append({x[0]: x[4] for x in ways})
        return me

    def either(kind, *ways):
        choice.append([])
        for f in ways:
            f()
        note(choice.pop(), WAKE, shy=SHY[kind])

    def urge(name):
        calls[-1][4] = URGE[name]

    def issue_all():
        if not ORDER:
            ORDER.extend(order_of_issue(calls))
        engine, start = ORDER
        awaited = set()
        for j, c in enumerate(calls):
            mine = [i for i in c[2] if engine[i] == "P"]
            if mine and engine[j] != "P":
                awaited.add(max(mine, key=lambda i: (start[i], i)))
        for j in sorted(range(len(calls)), key=lambda j: (start[j], j)):
            emits[j][engine[j]](engine[j] != "P" or j in awaited)

    def narrow(x):
        return SCRATCH[x[1]][2] in (B, H, U)

    def op(e, out, ins, call, rate=1.0, also=(), behind=()):
        reads = [x for x in ins if isinstance(x, tuple)]
        if len(out) > 6:
            rate = SCATTER
        elif any(len(x) > 6 for x in reads):
            rate = GATHER
        n = out[5][1]
        time = FIXED[e] + CYCLE[e] * (rate * max(64, n) if e == "P" else max(64, rate * n))
        reads = reads + [x[6] for x in reads + [out] if len(x) > 6]
        writes = [out] + list(also)

        def emit(inc):
            before(e, reads, writes)
            ins_ = call()
            if inc:
                ins_.then_inc(T.sem[e], 1)
                cnt[e] += 1
            after((e, cnt[e] + (0 if inc else 1)), reads, writes)
        if choice:
            choice[-1].append((e, reads, writes, time, emit))
        else:
            note([(e, reads, writes, time, emit)], WAKE, behind)

    def v_(x):
        return x[0] if isinstance(x, tuple) else x

    def half(*sides):
        return 0.5 if all(narrow(x) for x in sides) else 1.0

    def ts(out, x, s1, o1, s2=None, o2=None):
        if o2 is None:
            op("V", out, [x, s1], lambda: g.vector.tensor_scalar(out[0], x[0], v_(s1), None, o1), half(out, x))
        else:
            op("V", out, [x, s1, s2], lambda: g.vector.tensor_scalar(out[0], x[0], v_(s1), v_(s2), o1, o2), half(out, x))

    def tt(out, x, y, o):
        op("V", out, [x, y], lambda: g.vector.tensor_tensor(out[0], x[0], y[0], o), 1.0 if x[4] or y[4] else 2.0)

    def cp(out, x):
        op("V", out, [x], lambda: g.vector.tensor_copy(out[0], x[0]), half(out, x))

    def ms(out, c):
        op("V", out, [], lambda: g.vector.memset(out[0], c), half(out))

    def scan(out, x, y, init, o0, o1):
        op("V", out, [x, y, init], lambda: g.vector.tensor_tensor_scan(out[0], x[0], y[0], v_(init), o0, o1), half(out, x, y))

    def act(out, x, f=AF.Identity, bias=None, scale=None, total=None, behind=()):
        kw = {}
        for k, v in (("bias", bias), ("scale", scale), ("accum_out", total)):
            if v is not None:
                kw[k] = v_(v)
        op("S", out, [x, bias, scale], lambda: g.scalar.activation(out[0], x[0], f, **kw), also=[total] if total else [], behind=behind)

    def lin(kind, out, x, scale=1.0, bias=0.0):
        either(kind, lambda: act(out, x, bias=bias, scale=scale), lambda: ts(out, x, scale, OP.mult, bias, OP.add))

    def iota(out, pat, base, cm, flt=True):
        if flt:
            op("G", out, [], lambda: g.iota(out[0], pat, base, cm, allow_small_or_imprecise_dtypes=True), 2.0)
        else:
            op("G", out, [], lambda: g.iota(out[0], pat, base, cm), 2.0)

    def mm(out, l, r, start, stop):
        op("P", out, [l, r], lambda: g.tensor.matmul(out[0], l[0], r[0], start, stop), 1.0 if narrow(l) else 4.0)

    def dmas(sem, lst, behind=()):
        reads = [i_ for (o, i_) in lst if isinstance(i_, tuple)]
        writes = [o for (o, i_) in lst if isinstance(o, tuple)]
        size = 0
        for (o, i_) in lst:
            x = o if isinstance(o, tuple) else i_
            size += x[5][0] * x[5][1] * (2 if narrow(x) else 4)

        def emit(_inc):
            before("Y", reads, writes)
            for (o, i_) in lst:
                g.sync.dma_start(v_(o), v_(i_)).then_inc(T.sem[sem], 16)
            tot[sem] = tot.get(sem, 0) + 16 * len(lst)
            after((sem, tot[sem]), reads, writes)
        if reads or behind:
            return note([("Y", reads, writes, 0.1 * len(lst) + size / DMA_RATE, emit)], DMA_LATE, behind)
        loaded.append(size / DMA_RATE)
        return note([("Y", reads, writes, 0.01, emit)], DMA_LATE + sum(loaded), range(len(loaded) - 1))

    def send(lst, first=0.0):
        per = 1
        while 2 * per * len(lst) <= len(topo.engines(core, T.cores[lst[0][0]])):
            per *= 2

        def emit(_inc):
            trs = []
            for n, (d, src, dst, sem) in enumerate(lst):
                before("G", [src], [])
                dc = T.cores[d]
                en = topo.engines(core, dc)
                m = 0
                for k in range(per):
                    m |= 1 << en[n * per + k]
                rid, pid, _se = topo.addr(dc)
                trs.append(RemoteDMATransfer(dst_ids=[DstId(rid=rid, pnc=pid)], dma_engine_mask=m, remote_sem=T.sem[sem],
                                             src=src[0], dst=dst[0]))
            tot["loc"] = tot.get("loc", 0) + per * len(lst)
            g.remote_dma_fused(trs, local_sem=T.sem.loc)

        def landed(_inc):
            for (d, src, dst, sem) in lst:
                tot[sem] = tot.get(sem, 0) + per
            for (d, src, dst, sem) in lst:
                after((sem, tot[sem]), [], [dst])
        me = note([("G", [x[1] for x in lst], [], SEND + first, emit)], SEND_LATE)
        note([("landing", [], [x[2] for x in lst], 0.0, landed)], 0.0, [me])

    def sel(fam, k):
        return a(fam, 15 - k, 143 - k)

    def w2l(out, fam, src, lo, hi, start=True, stop=True):
        for k in range(16):
            mm(out, sel(fam, k), a(src, lo + k, hi, 16), start and k == 0, stop and k == 15)

    col = {}

    def pcol(name):
        if name not in col:
            col[name] = len(col)
        return a("pc", col[name], col[name] + 1)

    def ek(k):
        return a("ek", k, k + 1)

    def row(k):
        return slice(k, 128, 16)

    def fam(name, weight, at=0.0):
        ts(a(name), a("r143"), at, OP.is_equal, weight, OP.mult)

    def load_positions(k, behind=()):
        dmas("q%d" % k, [(a("pos_r", 1024 * k, 1024 * k + 1024), T.wpos[:, 1024 * k:1024 * k + 1024])], behind)

    dmas("d0", [(a("gst_r", 0, 64), T.gst[:]), (a("gln_r", 0, 64), T.gln[:])])
    dmas("d1", [(a("sens_r"), T.sens[:])])
    dmas("d2", [(a("rel_r"), T.rel[:])])
    dmas("d3", [(a("cur_r"), T.cur[:])])
    dmas("d4", [(a("nxt_r"), T.nxt[:])])
    dmas("d5", [(a("heap_r"), T.heap[:])])
    for k in range(EARLY):
        load_positions(k)

    iota(a("io_p", 0, 1), [[0, 1]], 0, 1, False)
    iota(a("xf"), [[1, 256]], 0, 0)
    iota(a("sw"), [[1, 1024]], 0, 0, False)
    ts(a("io_p", 1, 2), a("io_p", 0, 1), 15, OP.bitwise_and)
    ts(a("io_p", 2, 3), a("io_p", 0, 1), 7, OP.bitwise_and)
    ts(a("io_p", 3, 4), a("io_p", 0, 1), 3, OP.bitwise_and)
    c_, c8 = a("io_p", 1, 2), a("io_p", 2, 3)
    cp(a("pc", 0, 3), a("io_p", 1, 4))
    c, _c8, _k = pcol("c"), pcol("c8"), pcol("k")
    tt(pcol("g16"), a("io_p", 0, 1), c_, OP.subtract)
    ts(a("idu"), a("xf", 0, 64), 16.0, OP.mult, c, OP.add)
    ts(a("b1"), a("xf", 0, 128), pcol("g16"), OP.subtract)
    ts(a("r143"), a("xf", 0, 144), pcol("g16"), OP.subtract, 15.0, OP.subtract)
    ts(a("b2"), a("b1"), 15.0, OP.is_gt, 1000.0, OP.mult)
    tt(a("rg"), a("b1"), a("b2"), OP.subtract)
    for k in range(16):
        ts(a("tri", 128 * k, 128 * k + 128), a("rg"), float(k), OP.is_ge)
    group, upper = a("tri", 0, 128), a("tri", 1024, 1152)
    ts(a("ek"), a("xf", 0, 16), c, OP.is_equal)
    ts(a("ek8"), a("xf", 0, 16), pcol("c8"), OP.is_equal)
    ts(pcol("h01"), c_, 2, OP.is_lt)
    ts(pcol("lo8"), c_, 8, OP.is_lt)
    ts(pcol("a0"), c8, 4, OP.is_lt)
    ts(pcol("hs"), ek(0), 65536.0, OP.mult, ek(1), OP.subtract)
    ts(pcol("hb"), ek(0), ek(2), OP.subtract, CUT, OP.mult)
    lo8 = pcol("lo8")
    for name, x, scale, bias in (("c3", c, 3.0, 0.0), ("c4x", c, 4.0, 0.0), ("cm2", c, 1.0, -2.0), ("w4", pcol("h01"), 4.0, 0.0),
                                 ("hi8", lo8, -1.0, 1.0), ("nh8", lo8, 1.0, -1.0), ("wd", lo8, -2.0, 1.0),
                                 ("u4", ek(2), 1.0, ek(3)), ("u6", ek(3), 1.0, ek(4)),
                                 ("a1", pcol("a0"), -2.0 / 512, 1.0 / 512), ("u5", pcol("hi8"), 4.0, pcol("k"))):
        lin("constant", pcol(name), x, scale, bias)
    lin("constant", a("ss", 0, 1), lo8, -768.0)
    ts(a("ek3"), a("xf", 0, 48), pcol("c3"), OP.is_equal)
    ts(a("f5"), a("r143"), pcol("c4x"), OP.subtract, 0.0, OP.is_ge)
    ts(a("f6"), a("r143"), pcol("c4x"), OP.subtract, 4.0, OP.is_lt)
    tt(a("f5"), a("f5"), a("f6"), OP.mult)
    lin("constant", a("rqf"), a("f5"), pcol("w4"))
    ts(a("idf"), a("rg"), c, OP.is_equal)
    ts(a("b3"), a("rg"), 0.0, OP.is_equal, 2.0 ** -16, OP.mult)
    ts(a("b4"), a("rg"), 1.0, OP.is_equal)
    tt(a("f7"), a("b3"), a("b4"), OP.add)
    cp(a("boh"), group)
    tt(a("b2"), group, upper, OP.subtract)
    for name, weight in (("s1", 1.0), ("sz", lo8), ("smh", -1.0)):
        fam(name, weight)
    fam("lsf", pcol("u4"), pcol("cm2"))
    fam("wsf", 1.0, pcol("u5"))
    for name, x, scale in (("idb", a("idf"), 1.0), ("idn", a("idf"), -1.0), ("bc", a("b4"), CUT / 16), ("bdp", a("f7"), pcol("wd")),
                           ("bdm", a("bdp"), -1.0), ("bop", group, 1.0), ("b15", group, ek(15)), ("bon", group, -1.0),
                           ("sh", a("s1"), pcol("h01")), ("sn", a("s1"), ek(2)), ("s34", a("s1"), pcol("u6")), ("szb", a("s1"), lo8),
                           ("s2", a("s1"), 2.0), ("s32", a("s1"), 1.0 / 32), ("sm", a("s1"), -1.0),
                           ("hib", upper, 16.0), ("lob", a("b2"), 16.0)):
        lin("constant", a(name), x, scale)
    lin("constant", a("ridx"), a("xf", 0, 32), 16.0, c)
    for o, scale, bias in ((a("top"), 1.0, 6144.0), (a("mid", 0, 32), 1.0, 256.0), (a("mid", 32, 64), 0.0, 256.0), (a("mid", 64, 68), 2.0, 0.5),
                           (a("top2"), 1.0, 4097.0), (a("cd2"), -1.0, -2049.0), (a("nfr"), -1.0 / 512, -1.0 / 1024)):
        lin("constant", o, a("ridx", 0, o[5][1]), scale, bias)
    ts(a("rfr"), a("xf"), 1.0 / 8192, OP.mult)
    ms(a("ones"), 1.0)
    lin("constant", a("iotab"), a("ones", 0, 384), 1.0, c)
    lin("constant", a("iotab", 0, 384, 48), a("ones", 0, 8), 0.0, c)
    for o, value in ([(a("mend"), 1.0), (a("mend", 47, 384, 48), 0.0), (a("cc"), 0.0), (a("cs", 0, 1), 0.0), (a("ds", 0, 1), 16384.0),
                      (a("rw", 0, 8), -2048.0), (a("gone"), -1.25), (a("pt", 0, 1), -1.25), (a("pt", 4097, 4368), 0.0)]
                     + [(a("y%d" % k, 7, 8), 0.25) for k in range(DEEP)]):
        lin("constant", o, a("ones", 0, o[5][1]), 0.0, value)
    zero = a("hw", 15360, 16384)
    ms(zero, 0.0)
    for k in range(15):
        o = a("hw", 1024 * k, 1024 * k + 1024)
        either("fill", lambda: ms(o, 0.0), lambda: act(o, zero))

    ms(a("gst_r", 64, 68), 0)
    ms(a("gln_r", 64, 68), 0)
    tt(a("f1", 0, 66), a("gst_r", 0, 66), a("gln_r", 0, 66), OP.add)
    ts(a("f2", 0, 66), a("gln_r", 0, 66), 0, OP.is_gt)
    ts(a("f3", 0, 22), a("gln_r", 1, 66, 3), 32.0, OP.mult)
    ts(a("f4", 0, 22), a("gln_r", 2, 66, 3), 1024.0, OP.mult)
    tt(a("f1", 0, 66), a("f1", 0, 66), a("f2", 0, 66), OP.mult)
    tt(a("f3", 0, 22), a("f3", 0, 22), a("gln_r", 0, 66, 3), OP.add)
    tt(a("f3", 0, 22), a("f3", 0, 22), a("f4", 0, 22), OP.add)
    for x in range(3):
        cp(a("tl", x, 88, 4), a("f1", x, 66, 3))
    cp(a("tl", 3, 88, 4), a("f3", 0, 22))
    send([((rank - n) % N, a("tl", 0, 88), a("tl", 88 * n, 88 * n + 88), "tarr") for n in range(1, N)], FIRST)
    for k in range(4):
        iota(a("w", 1664 * k, 1664 * k + 1664), [[0, 1664]], 0, 0)
    for x in range(3):
        cp(a("tli", x, 528, 3), a("tl", x, 704, 4))
    dmas("d12", [(a("tab", rows=row(8 + q)), a("tli", 66 * q, 66 * q + 64)) for q in range(N)])
    cp(a("tli", 528, 704), a("tl", 3, 704, 4))
    ts(a("lnf", 0, 528, 3), a("tli", 528, 704), 31, OP.bitwise_and)
    ts(a("lnf", 1, 528, 3), a("tli", 528, 704), 5, OP.logical_shift_right, 31, OP.bitwise_and)
    ts(a("lnf", 2, 528, 3), a("tli", 528, 704), 10, OP.logical_shift_right)
    tables = dmas("d6", [(a("tab", rows=row(q)), a("lnf", 66 * q, 66 * q + 64)) for q in range(N)])
    for k in range(EARLY, 4):
        load_positions(k, [tables])

    for x in range(2):
        cp(a("sp", 64 * x, 64 * x + 64), a("sens_r", x, 128, 2))
    ts(a("sx", 0, 128), a("sp", 0, 128), 63, OP.bitwise_and)
    ts(a("sx", 128, 256), a("sp", 0, 128), 6, OP.logical_shift_right)
    ts(a("sx", 0, 128), a("sx", 0, 128), 16.0, OP.mult)
    tt(a("sp", 128, 256), a("sx", 0, 128), a("sx", 128, 256), OP.add)
    dmas("d7", [(a("sw", rows=row(x)), a("sp", 64 * x, 64 * x + 64)) for x in range(4)])
    cp(a("lnx"), a("nxt_r"))
    lin("look", a("tsy"), ind(a("sw"), a("lnx")))
    ts(a("ti"), a("rel_r"), float(1024 * (N - rank)), OP.add)
    ts(a("rp", 0, 256), a("rel_r"), 992, OP.bitwise_and)
    ts(a("rp", 256, 512), a("rel_r"), 31, OP.bitwise_and)
    ts(a("rp", 512, 768), a("ti"), 10, OP.logical_shift_right, 7, OP.bitwise_and)
    cp(a("rpb"), a("rp"))
    dmas("d8", [(a("hw", 0, 4096, rows=row(x)), a("rpb", 256 * i, 256 * i + 256)) for i, x in enumerate((3, 4, 2))])
    either("heap", lambda: act(a("hhi"), ind(a("heap_r"), a("idu"))), lambda: cp(a("hhi"), a("heap_r")))
    either("heap", lambda: act(a("heapf"), ind(a("heap_r"), a("idu"))), lambda: cp(a("heapf"), a("heap_r")))
    for j, p in enumerate(("p0", "p1")):
        mm(a(p), a("idf"), a("heapf", 512 * j, 512 * j + 512), True, False)
        mm(a(p), a("idn"), a("hhi", 512 * j, 512 * j + 512), False, True)
        lin("out", a("hlo", 512 * j, 512 * j + 512), a(p))
    dmas("d9", [(a("hw", rows=row(0)), a("hhi")), (a("hw", rows=row(1)), a("hlo"))])
    for k in range(4):
        o, x = a("pt", 1 + 1024 * k, 1025 + 1024 * k), a("pos_r", 1024 * k, 1024 * k + 1024)
        either("positions", lambda: act(o, ind(x, a("idu")), bias=-1.25), lambda: ts(o, x, -1.25, OP.add))

    def look_up(nc):
        n = 32 * nc
        for x in range(2):
            for b in range(2):
                if nc == 2:
                    o, i_ = a("p6", 32 * x, 32 * x + 32), a("gc", 2 * b + x, 128, 4)
                else:
                    o, i_ = a("p6", x, 32, 2), a("gc", 32 * x + 16 * b, 32 * x + 16 * b + 16)
                mm(o, sel("rqf", 8 * b), i_, x + b == 0, x + b == 2)
        ts(a("l2", 0, n), a("p6", 0, n), pcol("k"), OP.add)
        lin("look", a("rqw", 0, 16 * n), ind(a("hw", 0, 4096), a("l2", 0, n)))
        w2l(a("p6", 0, n), "s34", "rqw", 0, 16 * n, stop=False)
        w2l(a("p6", n, 2 * n), "sn", "rqw", 0, 16 * n, start=False)
        cp(a("l3", 0, 2 * n), a("p6", 0, 2 * n))
        lin("small", a("pq") if nc == 2 else a("sel"), a("p6", n, n + 32), 768.0, 768.0)
        lin("look", a("msk", 0, 16 * n), ind(a("ek8"), a("l3", n, 2 * n)))
        if nc == 2:
            urge("mask")
            lin("small", a("pqs"), a("p6", n, 2 * n), 1.5)
            tt(a("cd"), a("pqs", 32, 64), a("pqs", 0, 32), OP.subtract)
            for h in range(2):
                tt(a("g2c", 512 * h, 512 * h + 512), ind(a("tab"), a("l3", 32 * h, 32 * h + 32)), a("msk", 512 * h, 512 * h + 512), OP.mult)

    def next_senses(r):
        for k in range(8):
            lo = 64 * (r - 1) + k if r else 16 * (k % 4) + k // 4
            mm(a("p6", 0, 8), sel("lsf", 2 * k), a("ywb", lo, 64 * r, 8) if r else a("gc", lo, lo + 15, 2), k == 0, k == 7)
        cp(a("lsy"), a("p6", 0, 8))
        lin("look", a("gc"), ind(a("tsy"), a("lsy")))

    cp(a("lcur"), a("cur_r"))
    lin("look", a("gc", 0, 64), ind(a("sw"), a("lcur")))
    look_up(1)

    def requests(r):
        if r > 0:
            cp(a("g2"), ind(a("g2c"), a("lu")))
            act(a("d0"), ind(a("g2c"), a("lu")), AF.Relu, bias=1.0, scale=pcol("nh8"))
        else:
            tt(a("g2"), ind(a("tab"), a("l3", 0, 32)), a("msk", 0, 512), OP.mult)
            act(a("d0"), a("g2"), AF.Relu, bias=1.0, scale=pcol("nh8"))
        act(a("p4"), a("g2"), AF.Sign)
        scan(a("ss", 1, 513), a("d0"), a("g2"), a("ss", 0, 1), OP.mult, OP.add)
        tt(a("xm"), a("p4"), a("ss", 0, 512), OP.mult)
        w2l(a("p5", 0, 32), "sz", "xm", 0, 512)
        for h in range(2):
            o, lo = a("p%d" % h, 0, 256), 256 * h
            mm(o, a("bc"), a("ones", 0, 256), True, False)
            mm(o, a("bdp"), a("ss", lo + 1, lo + 257), False, False)
            mm(o, a("bdm"), a("ss", lo, lo + 256), False, True)
            lin("round", a("hh", lo, lo + 256), o, pcol("hs"), pcol("hb"))
            tt(a("val", lo, lo + 256), o, a("hh", lo, lo + 256), OP.add)
        ts(a("zf"), a("p5", 0, 32), 0.0, OP.is_ge, 8192.0, OP.mult)
        tt(a("zt"), a("p5", 0, 32), a("sel"), OP.add)
        ts(a("sh_"), a("p5", 0, 32), -384.0, OP.is_ge, 384.0, OP.mult)
        tt(a("zu"), a("zt"), a("zf"), OP.add)
        tt(a("zo"), a("zu"), a("top"), OP.min)
        cp(a("offu"), a("zo"))
        cp(ind(a("w"), a("offu")), a("val"))

    def addresses(r, b):
        lo, hi = ADDR[b]
        n = 48 * (hi - lo)
        o = a("p%d" % b, 0, n)
        mm(o, a("idb"), a("iotab", 0, n), True, False)
        for k in range(16):
            mm(o, a("tri", 128 * k, 128 * k + 128), a("w", 768 * lo + k, 768 * hi, 16), False, k == 15)
        scan(a("cc", 48 * lo + 1, 48 * hi + 1), o, a("mend", 0, n), 0.0, OP.add, OP.mult)
        base, near = a("p%d" % (3 + b), 0, n), a("near", 48 * lo, 48 * hi)
        mm(base, a("b15"), a("cc", 48 * lo, 48 * hi), True, True)
        lin("out", near, o)
        tt(near, base, near, OP.add)
        ts(a("as%d" % r, 48 * lo, 48 * hi), near, 16383.0, OP.min)
        send([((rank + n) % N, a("as%d" % r, 48 * n, 48 * n + 48), a("al%d" % r, 48 * n, 48 * n + 48), "aa%d" % n)
              for n in range(max(lo, 1), hi)])

    def firsts():
        for k in range(16):
            n = 384 if k % 2 else 408
            mm(a("p3", 0, n), sel("sn", k), a("w", 384 * k, 384 * k + n), k == 0, k == 15)
        either("out", lambda: act(a("keep"), a("p3", 0, 408), AF.Relu, bias=1.0), lambda: ts(a("keep"), a("p3", 0, 408), 0.0, OP.is_equal))

    def segments():
        lin("look", a("g2b"), a("g2"))
        mm(a("p5", 0, 32), a("idf"), a("zt"), True, False)
        w2l(a("p5", 0, 32), "szb", "g2b", 0, 512, start=False)
        tt(a("sl"), a("sel"), a("zf"), OP.subtract)
        tt(a("sr"), a("sel"), a("sh_"), OP.add)
        tt(a("se"), a("p5", 0, 32), a("sl"), OP.min)
        ts(a("rho"), a("sr"), -768.0, OP.add, 1.0 / 128, OP.mult)
        tt(a("sq"), a("se"), a("sr"), OP.subtract)
        ts(a("leu"), a("sq"), 768.0, OP.add, 0.0, OP.max)
        lin("look", a("mc"), ind(a("ek3"), a("rho")))

    def answer(r, b):
        lo, hi = BACK[b]
        for n in range(lo, hi):
            o, x = a("ow", 768 * n, 768 * n + 768), ind(a("hw"), a(("al%d" if n else "as%d") % r, 48 * n, 48 * n + 48))
            either("own", lambda: act(o, x), lambda: cp(o, x))
        o = a(("p7", "p5", "p4", "p5")[b], 0, 48 * (hi - lo))
        w2l(o, "sh", "ow", 768 * lo, 768 * hi)
        ts(a(("rs%d" if lo else "rl%d") % r, 48 * lo, 48 * hi), o, 1.0, OP.add)
        if lo:
            send([((rank - n) % N, a("rs%d" % r, 48 * n, 48 * n + 48), a("rl%d" % r, 48 * n, 48 * n + 48), "ra%d" % n)
                  for n in range(lo, hi)])

    def phrases(r, b):
        lo, hi = BACK[b]
        ts(a("rw", 8 + 48 * lo, 8 + 48 * hi), a("rl%d" % r, 48 * lo, 48 * hi), -2048.0, OP.add)
        o = a("p7" if b % 2 else "p2", 0, 48 * (hi - lo))
        w2l(o, "sn", "w", 768 * lo, 768 * hi, stop=False)
        mm(o, a("idf"), a("rw", 8 + 48 * lo, 8 + 48 * hi), False, True)
        ts(a("lx", 48 * lo, 48 * hi), o, 2048.0, OP.add, 0.0, OP.max)
        for n in range(lo, hi):
            s = str(n % DEEP)
            y, pr = a("y" + s, 8, 776), a("pr" + s)
            act(y, ind(a("pt"), a("rl%d" % r, 48 * n, 48 * n + 48)), AF.Abs, bias=1.0)
            tt(a("ct" + s), ind(a("pt"), a("lx", 48 * n, 48 * n + 48)), a("y" + s, 7, 775), OP.is_equal)
            either("present", lambda: act(pr, y, AF.Sign, bias=-0.25), lambda: ts(pr, y, 0.5, OP.is_gt))
            scan(a("rr" + s), a("ct" + s), a("ct" + s), 0.0, OP.mult, OP.add)
            for f_, src, p in (("s1", "ct", "p1"), ("s1", "pr", "p0"), ("s2", "rr", "p0")):
                for h in range(2):
                    first = n == 0 and h == 0 and src != "rr"
                    last = n == N - 1 and h == 1 and src != "pr"
                    mm(a(p, 0, 384 if h else 408), sel(f_, 2 * n + h), a(src + s, 384 * h, 768 if h else 408), first, last)

    def totals(r, last):
        scan(a("cs", 1, 409), a("keep"), a("p0", 0, 408), 0.0, OP.mult, OP.add)
        tt(a("ge"), ind(a("cs", 0, 409), a("leu")), a("mc"), OP.mult)
        for k in range(8):
            mm(a("p0", 0, 64), a("bop" if k >= 4 else "bon"), a("ge", k, 512, 8), k == 0, k == 7)
        act(a("sg"), a("p0", 0, 64), AF.Sign, bias=-0.5)
        mm(a("p4", 0, 64), a("idf"), a("mid", 0, 64), True, False)
        for x in range(1 if last else 0, 2):
            for b in range(2):
                mm(a("p4", 32 * x, 32 * x + 32), a("hib" if b else "lob"), a("sg", b, 64, 2), False, x + b == 2)
        if not last:
            cp(a("lu"), a("p4", 0, 32))
            tt(a("wc"), a("p4", 32, 64), a("cd"), OP.mult)
            tt(a("sel"), a("wc"), a("pq"), OP.add)
        lin("small", a("wm"), a("p4", 32, 64), pcol("a1"), pcol("a0"))
        for k in range(4):
            mm(a("p6", 0, 128), a("bop"), a("ge", k, 512, 4), k == 0, k == 3)
        lin("out", a("ytb", 128 * r, 128 * r + 128), a("p6", 0, 128))
        mm(a("p6", 0, 4), a("idf"), a("mid", 64, 68), True, False)
        w2l(a("p6", 0, 4), "s32", "sg", 0, 64, start=False)
        cp(a("hl"), a("p6", 0, 4))
        lin("look", a("ywb", 64 * r, 64 * r + 64), ind(a("gc"), a("hl")))

    def barrier_places():
        either("out", lambda: act(a("nh"), a("p1", 0, 408), AF.Relu, bias=73728.0, scale=-8192.0),
               lambda: ts(a("nh"), a("p1", 0, 408), 9.0, OP.is_lt, 8192.0, OP.mult))
        scan(a("ds", 1, 409), a("ones"), a("nh"), 16384.0, OP.add, OP.min)
        tt(a("dg"), ind(a("ds", 0, 409), a("leu")), a("mc"), OP.mult)
        mm(a("p2", 0, 32), a("idf"), a("se"), True, False)
        w2l(a("p2", 0, 32), "sm", "dg", 0, 512, start=False)
        tt(a("bd"), a("p2", 0, 32), a("zt"), OP.is_gt)
        tt(a("ba"), a("p2", 0, 32), a("bd"), OP.mult)

    def barrier_words(r, last):
        tt(a("bb"), a("ba"), a("wm"), OP.mult)
        for p in range(2):
            mm(a("p2", 64, 80), sel("wsf", 8 * p), a("bb", p, 32, 2), p == 0, p == 1)
        ts(a("m1"), a("p2", 64, 80), 127.0, OP.add)
        ts(a("m2", 0, 16), a("m1"), 4, OP.logical_shift_right)
        ts(a("m2", 16, 32), a("m1"), 15, OP.bitwise_and)
        cp(a("cl"), a("m2"))
        lin("look", a("mk"), ind(a("ek"), a("cl", 16, 32)))
        tt(a("bw"), ind(a("rw"), a("cl", 0, 16)), a("mk"), OP.mult)
        urge("word")
        mm(a("p3", 0, 256), a("boh"), a("bw"), True, True)
        lin("out", a("ybb", 256 * r, 256 * r + 256), a("p3", 0, 256), 1.0, 2047.0)
        if last:
            return
        mm(a("p7", 0, 256), a("boh"), a("rfr"), True, False)
        mm(a("p7", 0, 256), a("boh"), a("bw"), False, True)
        lin("out", a("keyw"), a("p7", 0, 256))
        w2l(a("p2", 0, 16), "smh", "bw", 0, 256)
        tt(a("keyl", 0, 16), a("p2", 0, 16), a("nfr"), OP.add)
        lin("out", a("keyl", 16, 32), a("p2", 0, 16), 1.0, -255.5 / 512)
        tt(a("bu_"), a("cd2"), a("p2", 0, 16), OP.subtract)
        for i in range(16):
            for x in range(2):
                at = 512 * i - 16 * i * (i - 1) + x * (256 - 16 * i)
                act(a("eq", at, at + 256 - 16 * i), a("keyw", 16 * i, 256), AF.Sign, bias=a("keyl", 16 * x + i, 16 * x + i + 1),
                    total=a("mn", 16 * x + i, 16 * x + i + 1), behind=[len(calls) - 1] if i + x else [])
                calls[-1][0]["S"] += 0.02
                calls[-1][1] = WAKE if i + x in (0, 16) else 0.0
        tt(a("bv"), a("mn", 0, 16), a("mn", 16, 32), OP.is_equal)
        tt(a("bv"), a("bv"), a("bu_"), OP.mult)
        tt(a("bv"), a("bv"), a("top2"), OP.add)
        cp(a("bu"), a("bv"))
        cp(ind(a("pt"), a("bu")), a("gone"))
        urge("barred")

    for r in range(RO):
        last = r + 1 == RO
        requests(r)
        for b in range(len(ADDR)):
            addresses(r, b)
        next_senses(r)
        if not last:
            look_up(2)
        segments()
        firsts()
        for b in range(len(BACK)):
            answer(r, b)
        for b in range(len(BACK)):
            phrases(r, b)
        if not last:
            dmas("clr", [(a("w", 0, 6144, rows=row(x)), a("hw", 0, 6144, rows=row(5 + x))) for x in range(3)])
        barrier_places()
        totals(r, last)
        barrier_words(r, last)
    dmas("d10", [(T.yt[:], a("ytb", rows=row(0))), (T.yw[:], a("ywb", rows=row(4)))])
    dmas("d11", [(T.yb[:], a("ybb", rows=row(0)))])
    issue_all()
    for e in cnt:
        need("G", (e, cnt[e]))
    for s in sorted(tot):
        need("G", (s, tot[s]))
